import numpy as np, ml_dtypes
CORES = [3,11,19,27,35,43,51,59]
N = 8
import mx_ref
BF = ml_dtypes.bfloat16
def gentries(a):
    return np.ascontiguousarray(a.reshape(8, 16, -1).transpose(0, 2, 1)).reshape(8, -1)
def gtable(e):
    e = np.asarray(e); return np.ascontiguousarray(e.reshape(8, -1, 16).transpose(0, 2, 1)).reshape(128, -1).astype(np.int32)
def gcols(t, e):
    v = np.concatenate([t.reshape(8, 16, -1, 4), np.zeros((8, 16, 1, 4), BF)], axis=2)
    return np.ascontiguousarray(np.stack([v[g][:, e[g]] for g in range(8)])).reshape(128, -1)
def tile(rs):
    return np.stack(rs, axis=2).reshape(128, -1).astype(BF)
def pick(q, e):
    c = np.concatenate([q[0].reshape(128, -1, 4), np.zeros((128, 1, 4), np.uint8)], axis=1); s = np.concatenate([q[1], np.ones((16, 1), np.uint8)], axis=1)
    return (np.ascontiguousarray(c[:, e].reshape(128, -1)), np.ascontiguousarray(s[:, e]))
def join(*qs):
    return (np.concatenate([q[0] for q in qs], axis=1), np.concatenate([q[1] for q in qs], axis=1))
def put(q, e, v):
    c, s = q[0].reshape(128, -1, 4).copy(), q[1].copy(); c[:, e] = v[0].reshape(128, -1, 4); s[:, e] = v[1]
    return (c.reshape(128, -1), s)
def pk(c, s):
    return (np.ascontiguousarray(c), mx_ref.live(s))
def emit(q):
    return q[0], q[1]
def packed(v, rng):
    q = [mx_ref.quantize(np.ascontiguousarray(v[r])) for r in range(N)]
    return np.stack([a for a, b in q]), np.stack([mx_ref.plane(b, rng) for a, b in q])
def values_of_codes():
    e, c = np.zeros((128, 128, 4), np.float32), np.zeros((128, 2, 4), np.uint8)
    e[np.arange(128), np.arange(128), 0] = 1
    c[:127, :, 0] = np.arange(256).reshape(2, 128).T[:127]
    return mx_ref.matmul(mx_ref.quantize(e.reshape(128, 512).astype(BF)), (c.reshape(128, 8), np.full((16, 2), 127, np.uint8))).T.reshape(-1).astype(np.float64)
CODE_VALUE, SCALE_VALUE = values_of_codes(), 2.0 ** (np.arange(256) - 127.0)
def decode(q):
    return (CODE_VALUE[q[0]].reshape(16, 8, -1, 4) * SCALE_VALUE[q[1]][:, None, :, None] + 0.0).reshape(128, -1).astype(np.float32)
def f(rng, *shape):
    return mx_ref.flush((rng.standard_normal(shape, dtype=np.float32) * np.exp2(rng.integers(-2, 3, shape[:-1] + (1,)))).astype(BF))
def wide(rng, *shape, cols=0):
    v = rng.standard_normal(shape, dtype=np.float32) * np.exp2(rng.integers(-12, 13, shape)).astype(np.float32)
    if cols: v *= np.repeat(np.exp2(rng.integers(-cols, cols + 1, shape[:-2] + (1, shape[-1] // 4))) * (rng.random(shape[:-2] + (1, shape[-1] // 4)) > 0.0625), 4, axis=-1).astype(np.float32)
    return mx_ref.flush(v.astype(BF))
C, G, E, K, S = 256, 8, 8, 32, 256
STRIDE = [4, 2, 1]
DIR = [(-1, 0), (-1, 1), (0, 1), (1, 1), (1, 0), (1, -1), (0, -1), (-1, -1)]
def around(e, h):
    return np.stack([np.roll(e[:, g].reshape(N * G, 32), (-h * DIR[g][0], -h * DIR[g][1]), axis=(0, 1)).reshape(N, C) for g in range(8)], axis=1)
def numbers_of(rng):
    return {"x": np.array(f(rng, N, 128, 4 * C)), "u": np.array(f(rng, N, 128, 512)), "v": np.array(f(rng, N, 128, 512))}
def pointers(rng):
    return np.stack([gtable(rng.integers(0, S, (8, C))) for r in range(N)])
def same(rng, w):
    c, s = packed(np.stack([w] * N), rng)
    return {"wc": c, "ws": np.stack([s[0]] * N)}
def weights(rng, still=[]):
    w = np.array(f(rng, 128, 2048)).reshape(8, 16, 4, 8, 16, 4)
    for i in still:
        w[:, i] = 0
        w[:, :, :, :, i] = 0
    return same(rng, w.reshape(128, 2048))
def setup_inputs(rng):
    return {**numbers_of(rng), "p": pointers(rng), **weights(rng)}
def setup_inputs_ties(rng):
    d = numbers_of(rng)
    x = d["x"].reshape(N, 8, 16, C, 4)
    k = np.where(rng.random((N, 1, C)) < 0.5, 4, rng.integers(0, 3, (N, 1, C))) * np.ones((1, 8, 1))
    k[:, :, ::E] = rng.integers(0, 3, (N, 8, K))
    x[:, :, 0] = 0
    x[:, :, 0, :, 0] = k.astype(np.float32).astype(BF)
    u = d["u"].reshape(N, 128, 128, 4)
    u[:, :, ::16] = 0
    o = rng.permutation(N)
    for r in range(N):
        for h in range(0, 128, 16): u[r, h, h, 0] = 0.0 if r == o[0] else -1.0 if r == o[1] else 1.0
    return {"x": x.reshape(N, 128, 4 * C), "u": u.reshape(N, 128, 512), "v": d["v"], "p": pointers(rng), **weights(rng, [0])}
def setup_inputs_near(rng):
    d = numbers_of(rng)
    x = d["x"].astype(np.float32).reshape(N, 8, 16, C, 4)
    x[:, :, 0] = 0
    x[:, :, 8:] = 0
    x[:, :, 0, :, 0] = rng.integers(0, 2, (N, 1, C)) * 2.0 - 1.0
    x[:, :, 0, ::E] = 0
    s = rng.integers(0, 16, (N, 8, K))
    x[:, :, 8, ::E] = ((s[:, :, :, None] >> np.arange(4)) & 1) * np.exp2(np.arange(4) - 23.0)
    x[:, :, 10, :, 0] = (np.where(np.arange(8) < 4, -1.0, -1.125) * 2.0 ** -30)[:, None]
    x[:, :, 10, ::E, 0] = rng.integers(0, 2, (N, 8, K)) * 2.0 ** -30
    u = d["u"].reshape(N, 128, 128, 4)
    u[:, :, ::16] = 0
    o = rng.permutation(N) % 4
    for r in range(N):
        k = 1.0 if o[r] == 0 else 2.0 ** -30
        far = rng.permutation(8)
        if o[r] < 2:
            x[r, :, 11, :, 0] = -2.0 ** -10
            x[r, :, 11, ::E, 0] = 0
        for h in range(0, 128, 16):
            if o[r] < 2:
                u[r, h, h, 0] = k
                u[r, h + 11, h, 0] = k
            if o[r] == 2 and 16 * far[0] == h: u[r, h, h, 0] = 1.0
            if o[r] == 2 and 16 * far[1] == h: u[r, h, h, 0] = -1.0
            if o[r] < 3: u[r, h + 8, h] = k
            else: u[r, h + 10, h, 0] = k * 1.125 if h >= 64 else k * 1.25
    return {"x": x.reshape(N, 128, 4 * C).astype(BF), "u": u.reshape(N, 128, 512), "v": d["v"], "p": pointers(rng), **weights(rng, [0, 8, 9, 10, 11, 12, 13, 14, 15])}
def setup_inputs_huge(rng):
    d = numbers_of(rng)
    o = rng.permutation(N)
    c = rng.integers(0, 2, (N, 1, 1, C, 1)) * 2.0 - 1.0
    x = (0.6 + 0.09 * rng.random((N, 8, 16, C, 4))) * 2.0 ** 30 * c
    x[o == 0] = 0.875 * 2.0 ** 30 * c[o == 0]
    x[:, :, :, ::E] = (rng.random((N, 8, 1, K, 1)) * 2.0 - 1.0) * (0.8 + 0.2 * rng.random((N, 8, 16, K, 4))) * 2.0 ** 26
    a = 2.0 ** 29 * (1.0 - 0.1 * rng.random((N, 8, 16, 8, 4)))
    for g in range(8): a[:, g, :, g] *= 2.0
    for r in range(N):
        if o[r] == 0:
            a[r] = 2.0 ** 30
            for g in range(8): a[r, 0, :7 - g, g] *= 0.5
        if o[r] < N // 2: a[r] *= (rng.permutation(8) % 2 * 2.0 - 1.0)[None, None, :, None]
    u = d["u"].reshape(N, 128, 128, 4)
    u[:, :, ::16] = a.reshape(N, 128, 8, 4).astype(np.float32).astype(BF)
    w = np.zeros((128, 4, 128, 4), np.float32)
    i = np.arange(128)
    for b in range(4): w[i, b, i, b] = 4
    return {"x": x.astype(np.float32).reshape(N, 128, 4 * C).astype(BF), "u": u.reshape(N, 128, 512), "v": d["v"], "p": pointers(rng), **same(rng, w.reshape(128, 2048).astype(BF))}
def setup_inputs_few(rng):
    d = numbers_of(rng)
    e = rng.permutation(N)
    t = K * e[0] + rng.integers(0, K, (N, 8, C))
    t[e[0]] = S - 1
    t[e[1]] = 0
    t[e[2]] = K * e[2] + rng.integers(0, K, (8, C))
    t[e[3]] = rng.integers(0, S, (8, 1))
    return {**d, "p": np.stack([gtable(t[r]) for r in range(N)]), **weights(rng)}
def setup_inputs_spread(rng):
    d = setup_inputs(rng)
    d["x"] = wide(rng, N, 128, 4 * C, cols=6)
    return d
def check_inputs(d):
    b = []
    for k in ("x", "u", "v"):
        a = np.abs(d[k].astype(np.float32))
        if not (np.isfinite(a).all() and ((a == 0) | (a >= 2.0 ** -30) & (a <= 2.0 ** 30)).all()): b.append("a value of " + k)
    if not ((d["p"] >= 0) & (d["p"] < S)).all(): b.append("an entry of p")
    if ((d["wc"] & 0x7F) == 0x7F).any(): b.append("a code of wc that is no number")
    for k in ("wc", "ws"):
        if (d[k] != d[k][:1]).any(): b.append(k + " isn't the same on all ranks")
    z = np.zeros((128, 4, 4), np.float32)
    z[:, 1] = 2.0 ** -30
    z[:, 2] = 2.0 ** 30
    c, s = emit(mx_ref.quantize(z.reshape(128, 16).astype(BF)))
    for r in range(N):
        a = mx_ref.live(d["ws"][r])
        if not ((a == s[0, 0]) | (a >= s[0, 1]) & (a <= s[0, 2])).all(): b.append("a scale of ws")
    return b
def reference(x, u, v, p, wc, ws):
    qu = [mx_ref.quantize(u[r]) for r in range(N)]
    lay = [pk(wc[r], ws[r]) for r in range(N)]
    now = [x[r] for r in range(N)]
    ptr = np.stack([gentries(p[r]) for r in range(N)])
    for h in STRIDE:
        own = [decode(mx_ref.quantize(now[r])) for r in range(N)]
        seeds = np.concatenate([own[r].reshape(128, C, 4)[:, ::E] for r in range(N)], axis=1).reshape(128, 4 * S).astype(BF)
        came, new = around(ptr, h), []
        for r in range(N):
            z = (gcols(seeds, came[r]).astype(np.float32) - own[r]).astype(BF)
            s = mx_ref.matmul(qu[r], mx_ref.quantize(z))[::16] + np.float32(0.0)
            new.append(np.take_along_axis(came[r], np.argsort(-s, axis=0, kind="stable"), axis=0))
        ptr = np.stack(new)
        again = around(ptr, h)
        for r in range(N):
            q = mx_ref.quantize(gcols(seeds, again[r]))
            now[r] = tile([np.maximum(mx_ref.matmul(pick(lay[r], np.arange(128 * b, 128 * b + 128)), q), np.float32(0.0)) * np.float32(0.015625) + own[r][:, b::4] for b in range(4)])
    y, op = np.zeros((N, 128, C), np.float32), np.zeros((N, 8, C), np.float32)
    oc, osc = np.zeros((N, 128, 4 * C), np.uint8), np.zeros((N, 16, C), np.uint8)
    for r in range(N):
        q = mx_ref.quantize(now[r])
        y[r] = mx_ref.matmul(mx_ref.quantize(v[r]), q)
        op[r] = ptr[r]
        oc[r], osc[r] = emit(q)
    return {"y": y, "op": op, "oc": oc, "osc": osc}

@@ -1,0 +1,533 @@
+from concourse.bass import DstId, RemoteDMATransfer
+from concourse.mybir import dt, AluOpType, ActivationFunctionType
+
+F32, BF, I32, U16, U8, CODE = "float32", "bfloat16", "int32", "uint16", "uint8", "float8_e4m3fn_x4"
+N = 8
+STRIDE = [4, 2, 1]
+
+SCRATCH = {}
+for _n, _w, _d in [
+    ("xin", 1024, BF), ("uin", 512, BF), ("vin", 512, BF), ("landp", 48, I32),
+    ("land1", 128, BF), ("land2", 128, BF), ("land3", 48, BF),
+    ("eb", 2048, BF), ("idn", 128, BF), ("vv", 128, BF), ("va", 128, BF), ("vb", 128, BF), ("cb", 512, BF),
+    ("pi", 2, I32), ("fi", 16, I32), ("ff", 16, F32), ("kk", 192, F32), ("cc", 64, F32),
+    ("gi", 32, I32), ("g1", 32, F32), ("g2", 32, F32), ("dd", 32, F32),
+    ("w1", 64, F32), ("w2", 64, F32), ("w3", 64, F32), ("i1", 64, I32), ("i2", 64, I32), ("i3", 64, I32), ("i4", 64, I32),
+    ("of", 128, U16), ("keep", 128, F32),
+    ("zt", 1024, BF), ("yt", 2048, BF), ("xt", 2048, BF), ("bt", 1024, BF), ("tmp", 1024, F32),
+    ("sy", 256, F32), ("fl", 512, BF), ("rk", 64, F32), ("key", 64, F32), ("cl", 128, F32), ("sc", 128, F32),
+    ("lq", 64, F32), ("a1", 64, BF), ("gg", 64, BF), ("a2", 32, F32), ("uu", 32, F32), ("a3", 128, F32),
+    ("s1", 128, F32), ("s2", 128, F32), ("rot0", 320, F32), ("rot1", 320, F32), ("rot2", 320, F32),
+    ("om", 16, U16), ("oi", 16, U16), ("osd", 16, U16), ("ol", 32, U16),
+    ("p1", 64, I32), ("p2", 64, I32), ("p3", 64, I32), ("p4", 64, F32), ("p5", 64, F32), ("po", 32, F32), ("pt", 32, F32),
+    ("ysb", 256, F32),
+]:
+    SCRATCH[_n] = ("sbuf", [128, _w], _d)
+for _n, _w in [("qa", 256), ("snd", 32), ("ls", 256), ("qx1", 512), ("qx2", 512), ("qx3", 512), ("qx4", 256),
+               ("pa1", 512), ("pa2", 512), ("pa3", 512), ("qe", 1536), ("qc", 128), ("qu", 128), ("qup", 256),
+               ("qv", 128), ("qw", 512), ("qz", 256), ("qf", 128), ("qy", 512)]:
+    SCRATCH[_n + "c"] = ("sbuf", [128, _w], CODE)
+    SCRATCH[_n + "s"] = ("sbuf", [128, _w], U8)
+for _b in range(8):
+    SCRATCH["ps%d" % _b] = ("psum", [128, 512], F32)
+
+SEMAPHORES = (["eV", "eA", "eP", "eG"] + ["d%d" % _i for _i in range(24)] + ["l%d" % _i for _i in range(8)]
+              + ["ap", "ac", "asc", "an1", "an2", "an3", "af1", "af2"])
+
+A = AluOpType
+FN = ActivationFunctionType
+CY, WAKE, ROW, START = 0.001, 0.08, 0.025, 2.0
+
+
+def rank_program(g, core, T, topo):
+    me = T.rank_of(core)
+    if me is None:
+        return
+    Q = {"V": g.vector, "A": g.scalar, "P": g.tensor, "G": g, "S": g.sync}
+    ops, lastw, readers, totals, used = [], {}, {}, {}, {"d": 0, "l": 0}
+
+    def rec(q, fn, r, w, c, tok=None, lat=0.0):
+        op = {"q": q, "fn": fn, "deps": [], "need": False, "tok": tok, "c": c, "lat": lat, "n": len(ops)}
+        for k in r:
+            op["deps"].append(lastw[k])
+            if k.startswith("ps"):
+                op["deps"].extend(o for o in readers.get(k, []) if o["q"] != q)
+        for k in w:
+            if k in lastw:
+                op["deps"].append(lastw[k])
+            op["deps"].extend(readers.get(k, []))
+        for k in r:
+            readers.setdefault(k, []).append(op)
+        for k in w:
+            lastw[k] = op
+            readers[k] = []
+        ops.append(op)
+        return op
+
+    def newsem(kind):
+        used[kind] += 1
+        return "%s%d" % (kind, used[kind] - 1)
+
+    def dma(q, out, in_, r, w, sem=None, lat=START):
+        sem = sem or newsem("d")
+        totals[sem] = totals.get(sem, 0) + 16
+        return rec(q, lambda: Q[q].dma_start(out, in_).then_inc(T.sem[sem], 16), r, w, 0.1, tok=sem, lat=lat)
+
+    def group(k):
+        prv_, nxt_ = (k - 1) % N, (k + 1) % N
+        return [prv_, nxt_], [o for o in range(N) if o not in (k, prv_, nxt_)], [o for o in range(N) if o != k]
+
+    def engines(k, which):
+        m = -1
+        for o in group(k)[which]:
+            m &= topo.mask(T.cores[k], T.cores[o])
+        return m
+
+    def send(src, place, which, rsem, r, key, before=0):
+        to, m = group(me)[which], engines(me, which)
+        ids = [DstId(rid=topo.addr(T.cores[o])[0], pnc=topo.addr(T.cores[o])[1]) for o in to]
+        sem = newsem("l")
+        totals[sem] = bin(m).count("1")
+        tr = RemoteDMATransfer(dst_ids=ids, dma_engine_mask=m, remote_sem=T.sem[rsem], srcs=[src], dsts=[place(o) for o in to])
+        op = rec("G", lambda: g.remote_dma_fused([tr], local_sem=T.sem[sem]), r + ["gq"], ["gq"], 0.4, tok=sem,
+                 lat=START + ROW * 128 * (len(to) + before) / totals[sem])
+        op["deps"], op["after"] = op["deps"][:len(r)], op["deps"][len(r):]
+        totals[rsem] = sum(bin(engines(s, which)).count("1") for s in to)
+        lastw[key] = {"q": "R", "tok": rsem, "like": op}
+        return op
+
+    def size(n):
+        return max(64, n) * CY
+
+    def ts(out, in0, s1, s2, o0, o1, r, w, n=64):
+        if o1 is None:
+            return rec("V", lambda: g.vector.tensor_scalar(out, in0, s1, None, o0), r, w, size(n))
+        return rec("V", lambda: g.vector.tensor_scalar(out, in0, s1, s2, o0, o1), r, w, size(n))
+
+    def af(out, in0, scale, bias, r, w):
+        return rec("A", lambda: g.scalar.activation(out, in0, FN.Identity, bias=bias, scale=scale), r, w, size(64))
+
+    def tt(out, a, b, o, r, w, n=64):
+        return rec("V", lambda: g.vector.tensor_tensor(out, a, b, o), r, w, size(n))
+
+    def cp(out, in_, r, w, n=64):
+        return rec("V", lambda: g.vector.tensor_copy(out, in_), r, w, size(n))
+
+    def ms(out, c, w, n=64):
+        return rec("V", lambda: g.vector.memset(out, c), [], w, size(n))
+
+    def tp(out, in_, r, w, n=64):
+        return rec("V", lambda: g.vector.transpose(out, in_), r, w, size(n))
+
+    def act(out, in_, fn, r, w, n=64, **kw):
+        return rec("A", lambda: g.scalar.activation(out, in_, fn, **kw), r, w, size(n))
+
+    def iota(out, pat, base, cm, w, n=8):
+        return rec("G", lambda: g.iota(out, pat, base, cm, allow_small_or_imprecise_dtypes=True), [], w, 0.13 + 2 * n * CY)
+
+    def qz(name, a, n, tile, r, w):
+        return rec("V", lambda: g.vector.quantize_mx(T[name + "c"][:, a:a + n], T[name + "s"][:, a:a + n], tile), r, w, 1.1 * n * CY)
+
+    def mm(bank, n, sn, sa, mn, ma, start, stop, r):
+        return rec("P", lambda: g.tensor.matmul_mx(T["ps%d" % bank][:, 0:n], T[sn + "c"][:, sa:sa + 128], T[sn + "s"][:, sa:sa + 128],
+                                                   T[mn + "c"][:, ma:ma + n], T[mn + "s"][:, ma:ma + n], start, stop),
+                   r, ["ps%d" % bank], 0.6 * (n + 16) * CY)
+
+    def gat(n):
+        return int(55 + 1.5 * n)
+
+    def pick(dn, da, sn, sa, sw, off, k, r, w):
+        n = 16 * k
+        cp(T[dn + "c"][:, da:da + n].bitcast(dt.uint32), T[sn + "c"][:, sa:sa + sw].bitcast(dt.uint32).indirect(off), r, [w + "c"], gat(n))
+        act(T[dn + "s"][:, da:da + n], T[sn + "s"][:, sa:sa + sw].indirect(off), FN.Copy, r, [w + "s"], gat(n))
+
+    prv, nxt = group(me)[0]
+    ff, kk, cc, of, dd = T.ff, T.kk, T.cc, T.of, T.dd
+
+    dma("A", T.landp[:, 16:32], T.p[:], [], ["lpo"])
+    dma("S", T.xin[:], T.x[:], [], ["xin"], lat=START + 1.0)
+    dma("S", T.uin[:], T.u[:], [], ["uin"], lat=START + 1.5)
+
+    lastw["gq"] = rec("G", lambda: g.iota(T.pi[:, 0:1], [[0, 1]], 0, 1), [], ["pi"], 0.13)
+    EC, X4, E8, B16, K64, E16, UX, SG, LQ = 0, 10, 14, 22, 32, 96, 112, 120, 136
+    iota(T.idn[:], [[-1, 128]], 0, 1, ["idn"], 128)
+    iota(kk[:, EC:EC + 2], [[1, 2]], 0, 0, ["k0"])
+    iota(kk[:, EC + 2:EC + 10], [[0, 2], [1, 2], [0, 2]], 0, 0, ["k1"])
+    iota(kk[:, X4:X4 + 4], [[0, 2], [16, 2]], 0, 0, ["k2"])
+    iota(T.vv[:], [[1, 32], [-8, 4]], 0, 0, ["vv"], 128)
+    iota(kk[:, UX:UX + 8], [[0, 2], [32, 4]], 0, 0, ["k7"])
+    iota(kk[:, LQ:LQ + 4], [[1, 2], [4, 2]], 0, 0, ["k9"])
+    iota(kk[:, K64:K64 + 64], [[0, 8], [-256, 8]], 1792, 0, ["k5"], 64)
+    iota(kk[:, E16:E16 + 16], [[1, 2], [0, 8]], 0, 0, ["k6"])
+    iota(kk[:, SG:SG + 16], [[64, 4], [1, 4]], 0, 0, ["k8"])
+    iota(kk[:, E8:E8 + 8], [[0, 4], [1, 2]], 0, 0, ["k3"])
+    iota(kk[:, B16:B16 + 8], [[16, 4], [0, 2]], 0, 0, ["k4"])
+    send(T.landp[:, 16:32], lambda o: T.landp[:, 32:48] if o == prv else T.landp[:, 0:16], 0, "ap", ["lpo"], "lpa", before=6)
+
+    fields = {"q": (0, 15), "r": (0, 7), "w": (3, 1), "ch": (4, 1), "a": (5, 3), "g": (4, 7), "lo": (3, 7), "top": (6, 1),
+              "b0": (0, 1), "r1": (1, 3), "q1": (1, 7), "q2": (2, 3), "cs": (0, 3)}
+    col = {}
+    for i, (nm, (sh, an)) in enumerate(fields.items()):
+        ts(T.fi[:, i:i + 1], T.pi[:, 0:1], sh, an, A.logical_shift_right, A.bitwise_and, ["pi"], ["fi%d" % i])
+        col[nm] = ff[:, i:i + 1]
+    cp(ff[:, 0:13], T.fi[:, 0:13], ["fi%d" % i for i in range(13)], ["ff"])
+    O_SP, O_R0, O_C, O_FM, O_FL, O_LQ, O_U, O_SG, O_R, O_SF, O_OP, O_FB, O_RI = 0, 2, 6, 36, 38, 40, 44, 60, 76, 104, 108, 110, 112
+    ts(of[:, O_SP:O_SP + 1], col["q"], 8.0, 0.0, A.mult, A.add, ["ff"], ["osp0"])
+    ts(of[:, O_SP + 1:O_SP + 2], col["q"], 8.0, 128.0, A.mult, A.add, ["ff"], ["osp1"])
+    taken = [0]
+
+    def cnew(n=1):
+        taken[0] += n
+        return cc[:, taken[0] - n:taken[0]]
+
+    qz("qa", 0, 256, T.xin[:], ["xin"], ["qa"])
+    osp = of[:, O_SP:O_SP + 2]
+    pick("snd", 0, "qa", 0, 256, osp, 2, ["qa", "osp0", "osp1"], "snd")
+    send(T.sndc[:].bitcast(dt.uint8), lambda o: T.lsc[:, 32 * me:32 * me + 32].bitcast(dt.uint8), 2, "ac", ["sndc"], "lsac", before=4)
+    lastw["sent"] = send(T.snds[:], lambda o: T.lss[:, 32 * me:32 * me + 32], 2, "asc", ["snds"], "lsas", before=10)
+    pick("ls", 32 * me, "qa", 0, 256, osp, 2, ["qa", "osp0", "osp1"], "lso")
+    qz("qx1", 0, 256, T.xin[:], ["xin"], ["qx1o"])
+
+    ms(T.eb[:, 0:512], 0.0, ["eb0"], 256)
+    for b in range(1, 4):
+        act(T.eb[:, 512 * b:512 * b + 512], T.eb[:, 0:512], FN.Copy, ["eb0"], ["eb%d" % b], 512)
+    ts(T.idn[:], T.idn[:], 0.0, None, A.is_equal, None, ["idn"], ["idn"])
+    nev, nod = cnew(), cnew()
+    af(nev, col["ch"], 1.0, -1.0, ["ff"], ["nev"])
+    af(nod, col["ch"], -1.0, 0.0, ["ff"], ["nod"])
+    for v, (scale, keys) in enumerate([(1.0, []), (nev, ["nev"]), (nod, ["nod"])]):
+        for b in range(4):
+            act(T.eb[:, 512 * b + b:512 * (b + 1):4], T.idn[:], FN.Identity, ["idn"] + keys, ["eb%d" % b], 128, scale=scale)
+        qz("qe", 512 * v, 512, T.eb[:], ["eb%d" % b for b in range(4)], ["qe%d" % v])
+
+    a2 = cnew()
+    ts(a2, col["a"], 2.0, None, A.mult, None, ["ff"], ["a2"])
+    ts(T.gi[:, 0:10], kk[:, EC:EC + 10], a2, 2.0, A.add, A.add, ["k0", "k1", "a2"], ["gia"])
+    ts(T.gi[:, 10:14], kk[:, EC + 2:EC + 6], a2, None, A.add, None, ["k1", "a2"], ["gib"])
+    ts(T.gi[:, 14:15], col["g"], 0.0, None, A.add, None, ["ff"], ["gic"])
+    ts(T.gi[:, 15:16], col["g"], 2.0, None, A.add, None, ["ff"], ["gid"])
+    ts(T.gi[:, 16:24], kk[:, E8:E8 + 8], a2, None, A.add, None, ["k3", "a2"], ["gie"])
+    s = slice(0, 24)
+    ts(T.gi[:, s], T.gi[:, s], 7, None, A.bitwise_and, None, ["gia", "gib", "gic", "gid", "gie"], ["gi"])
+    ts(T.g1[:, s], T.gi[:, s], -2.0, 1.0, A.add, A.min, ["gi"], ["g1"])
+    ts(T.g2[:, s], T.gi[:, s], -1.0, 6.0, A.mult, A.add, ["gi"], ["g2"])
+    tt(T.g1[:, s], T.g1[:, s], T.g2[:, s], A.min, ["g1", "g2"], ["g1"])
+    ts(dd[:, s], T.g1[:, s], -1.0, None, A.max, None, ["g1"], ["dd"])
+
+    c16, r2, fm, r0c = cnew(), cnew(), cnew(), cnew()
+    xa = taken[0]
+    x10 = cnew(10)
+    af(c16, col["ch"], 16.0, col["q"], ["ff"], ["c16"])
+    af(r2, col["r"], 2.0, 16.0, ["ff"], ["r2"])
+    af(fm, col["b0"], 16.0, col["q1"], ["ff"], ["fm"])
+    af(cc[:, xa:xa + 6], kk[:, EC:EC + 6], 0.0, c16, ["k0", "k1", "c16"], ["x10a"])
+    af(cc[:, xa + 6:xa + 10], kk[:, X4:X4 + 4], 1.0, col["q"], ["k2", "ff"], ["x10b"])
+    ts(of[:, O_FM:O_FM + 1], fm, 0.0, None, A.add, None, ["fm"], ["ofm"])
+    ts(of[:, O_FL:O_FL + 1], fm, 8.0, None, A.add, None, ["fm"], ["ofl0"])
+    ts(of[:, O_FL + 1:O_FL + 2], fm, 40.0, None, A.add, None, ["fm"], ["ofl1"])
+    ts(r0c, dd[:, 14:15], 8.0, r2, A.mult, A.add, ["dd", "r2"], ["r0c"])
+    ts(of[:, O_R0:O_R0 + 4], kk[:, EC + 2:EC + 6], r0c, None, A.add, None, ["k1", "r0c"], ["or0"])
+    for i, h in enumerate(STRIDE):
+        s = slice(10 * i, 10 * i + 10)
+        ts(T.w1[:, s], dd[:, 0:10], float(h), 32.0, A.mult, A.add, ["dd"], ["w1%d" % i])
+        af(T.w3[:, s], kk[:, EC:EC + 10], 32.0, 0.0, ["k0", "k1"], ["w3%d" % i])
+        tt(T.i1[:, s], T.w1[:, s], x10, A.add, ["w1%d" % i, "x10a", "x10b"], ["i1%d" % i])
+    ts(T.i1[:, 0:30], T.i1[:, 0:30], 31, None, A.bitwise_and, None, ["i10", "i11", "i12"], ["i1"])
+    ts(T.i2[:, 2:10], T.i1[:, 2:10], 16, None, A.bitwise_and, None, ["i1"], ["i2"])
+    af(T.w2[:, 2:10], kk[:, EC + 2:EC + 10], 16.0, 0.0, ["k1"], ["w2"])
+    tt(T.w3[:, 2:10], T.w2[:, 2:10], T.i2[:, 2:10], A.add, ["w2", "i2", "w30"], ["w30"])
+    tt(T.w1[:, 0:30], T.w3[:, 0:30], T.i1[:, 0:30], A.add, ["w30", "w31", "w32", "i1"], ["w10", "w11", "w12"])
+    cp(of[:, O_C:O_C + 30], T.w1[:, 0:30], ["w10"], ["oc"])
+
+    def cand_lists(x):
+        rot, rn = T["rot%d" % x], "rot%d" % x
+        cp(T.a3[:], T.gg[:].indirect(of[:, O_C + 10 * x + 2:O_C + 10 * x + 10]), ["gg", "oc"], ["a3"], gat(128))
+        tp(rot[:, 0:128], T.a3[:], ["a3"], [rn, rn + "l"], 128)
+        cp(T.ol[:], rot[:, 0:64].indirect(of[:, O_FL:O_FL + 2]), [rn + "l", "ofl0", "ofl1"], ["ol"], gat(32))
+
+    def relabel(n, out, wkey, back):
+        s = slice(0, n)
+        ts(T.p2[:, s], T.p1[:, s], 4 if back else 0, 3, A.logical_shift_right, A.bitwise_and, ["p1"], ["p2"])
+        ts(T.p3[:, s], T.p1[:, s], 0 if back else 2, 15, A.logical_shift_right, A.bitwise_and, ["p1"], ["p3"])
+        sg = -1.0 if back else 1.0
+        ts(T.p4[:, s], T.p2[:, s], 15.0 * sg, None, A.mult, None, ["p2"], ["p4"])
+        ts(T.p5[:, s], T.p3[:, s], -3.0 * sg, None, A.mult, None, ["p3"], ["p5"])
+        tt(T.p4[:, s], T.p4[:, s], T.p1[:, s], A.add, ["p4", "p1"], ["p4"], 2 * n)
+        tt(out, T.p4[:, s], T.p5[:, s], A.add, ["p4", "p5"], [wkey], 2 * n)
+
+    def spread(x):
+        rot, rn, sem = T["rot%d" % x], "rot%d" % x, newsem("d")
+        for j in range(1, 4):
+            c0 = 64 + 64 * j
+            dma("S", rot[0:128 - 32 * j, c0:c0 + 64], rot[32 * j:128, 64:128], [rn], [rn + "j%d" % j], sem)
+            dma("S", rot[128 - 32 * j:128, c0:c0 + 64], rot[0:32 * j, 64:128], [rn], [rn + "k%d" % j], sem)
+        keys = [rn + jk + str(j) for jk in "jk" for j in range(1, 4)]
+        tt(T.lq[:], rot[:, 64:320].indirect(of[:, O_LQ:O_LQ + 4]), kk[:, K64:K64 + 64], A.add, [rn, "olq", "k5"] + keys, ["lq"], gat(64))
+
+    l1, l2 = cnew(), cnew()
+    tt(T.i3[:, 32:33], col["r1"], col["a"], A.subtract, ["ff"], ["i3x"])
+    ts(T.i3[:, 32:33], T.i3[:, 32:33], 4.0, None, A.add, None, ["i3x"], ["i3x"])
+    ts(T.i3[:, 32:33], T.i3[:, 32:33], 3, None, A.bitwise_and, None, ["i3x"], ["i3x"])
+    af(l1, col["b0"], 32.0, 8.0, ["ff"], ["l1"])
+    af(l2, col["w"], 2.0, l1, ["ff", "l1"], ["l2"])
+    ts(l1, T.i3[:, 32:33], 64.0, l2, A.mult, A.add, ["i3x", "l2"], ["l1"])
+    ts(of[:, O_LQ:O_LQ + 4], kk[:, LQ:LQ + 4], l1, None, A.add, None, ["k9", "l1"], ["olq"])
+
+    cp(T.a1[:], T.landp[:].indirect(of[:, O_R0:O_R0 + 4]), ["lpo", "lpa", "or0"], ["a1"], gat(64))
+    tp(T.gg[:], T.a1[:], ["a1"], ["gg"])
+    cand_lists(0)
+    cp(T.p1[:], T.rot0[:, 64:128], ["rot0"], ["p1"])
+    relabel(64, T.rot0[:, 64:128], "rot0", False)
+    spread(0)
+    dma("S", T.qwc[:].bitcast(dt.uint8), T.wc[:], ["sent", "rot0"], ["qwc"], lat=START + 1.0)
+    dma("S", T.qws[:], T.ws[:], ["sent", "rot0"], ["qws"], lat=START + 1.2)
+    dma("S", T.vin[:], T.v[:], ["sent", "rot0"], ["vin"], lat=START + 1.7)
+
+    ux, uy, val, nt, q4 = cnew(), cnew(), cnew(), cnew(), cnew()
+    af(ux, col["w"], 16.0, 0.0, ["ff"], ["ux"])
+    af(uy, col["r"], 16.0, 0.0, ["ff"], ["uy"])
+    af(nt, col["top"], -256.0, 256.0, ["ff"], ["nt"])
+    ts(val, col["r"], col["lo"], nt, A.is_gt, A.mult, ["ff", "nt"], ["val"])
+    qz("qu", 0, 128, T.uin[:], ["uin"], ["qu"])
+    ts(of[:, O_U:O_U + 8], kk[:, UX:UX + 8], ux, None, A.add, None, ["k7", "ux"], ["ou0"])
+    ts(of[:, O_U + 8:O_U + 16], kk[:, UX:UX + 8], 0.0, uy, A.mult, A.add, ["k7", "uy"], ["ou1"])
+    pick("qup", 0, "qu", 0, 128, of[:, O_U:O_U + 16], 16, ["qu", "ou0", "ou1"], "qup")
+    ts(T.va[:], T.vv[:], col["r"], val, A.is_equal, A.mult, ["vv", "ff", "val"], ["va"])
+    ts(T.vb[:], T.vv[:], col["lo"], val, A.is_equal, A.mult, ["vv", "ff", "val"], ["vb"])
+    tt(T.cb[:, 0:128], T.va[:], T.vb[:], A.subtract, ["va", "vb"], ["cb0"], 256)
+    for a in range(1, 4):
+        act(T.cb[:, 128 * a:128 * a + 128], T.cb[:, 0:128], FN.Copy, ["cb0"], ["cb%d" % a], 128)
+    qz("qc", 0, 128, T.cb[:], ["cb0", "cb1", "cb2", "cb3"], ["qc"])
+    ms(T.fl[:, 256:512], 0.0, ["flz"], 128)
+    ms(T.keep[:], 1.0, ["keep"], 128)
+    ms(T.keep[:, 0:128:8], 0.0, ["keep"])
+    bnd = [cnew() for e in range(3)]
+    for e in range(3):
+        af(bnd[e], a2, 256.0, 256.0 * e, ["a2"], ["bnd%d" % e])
+    csub, c0_ = cnew(16), cnew()
+    af(c0_, a2, 1792.0, 1792.0, ["a2"], ["c0_"])
+    af(csub, kk[:, E16:E16 + 16], 1792.0, c0_, ["k6", "c0_"], ["csub"])
+    af(q4, col["q"], 4.0, 0.0, ["ff"], ["q4"])
+    ts(of[:, O_SG:O_SG + 16], kk[:, SG:SG + 16], q4, None, A.add, None, ["k8", "q4"], ["osg"])
+
+    r8, q16, t8, q32, b16, opc = cnew(), cnew(8), cnew(), cnew(), cnew(), cnew()
+    af(r8, col["r"], 1.0, 8.0, ["ff"], ["r8"])
+    ts(q16, kk[:, B16:B16 + 8], col["q"], float(136 - 8 * me), A.add, A.add, ["k4", "ff"], ["q16"])
+    af(t8, col["cs"], 8.0, 32.0, ["ff"], ["t8"])
+    af(q32, col["q2"], 32.0, 0.0, ["ff"], ["q32"])
+    rk_, ek_ = [], []
+    for x in range(3):
+        h, h2, o = STRIDE[x], STRIDE[min(x + 1, 2)], 32 + 12 * x
+        hw = cnew()
+        af(hw, col["w"], float(h2 - h), float(h), ["ff"], ["hw%d" % x])
+        af(T.w3[:, o:o + 4], kk[:, EC + 2:EC + 6], 8.0, 0.0, ["k1"], ["ea%d" % x])
+        ts(T.i1[:, o:o + 4], dd[:, 10:14], hw, r8, A.mult, A.add, ["dd", "hw%d" % x, "r8"], ["ra%d" % x])
+        rk_.append("ra%d" % x)
+        ek_.append("ea%d" % x)
+        if x < 2:
+            af(T.w3[:, o + 4:o + 12], kk[:, E8:E8 + 8], 8.0, 0.0, ["k3"], ["ec%d" % x])
+            af(T.w1[:, o + 4:o + 12], dd[:, 16:24], float(h), 0.0, ["dd"], ["rw%d" % x])
+            tt(T.i1[:, o + 4:o + 12], T.w1[:, o + 4:o + 12], q16, A.add, ["rw%d" % x, "q16"], ["rb%d" % x])
+            ts(T.i4[:, x:x + 1], dd[:, 15:16], float(h), t8, A.mult, A.add, ["dd", "t8"], ["sf%d" % x])
+            rk_.append("rb%d" % x)
+            ek_.append("ec%d" % x)
+    ts(T.i4[:, 0:2], T.i4[:, 0:2], 31, None, A.bitwise_and, None, ["sf0", "sf1"], ["sf"])
+    for x in range(2):
+        ts(of[:, O_SF + 2 * x:O_SF + 2 * x + 1], T.i4[:, x:x + 1], q32, None, A.add, None, ["sf", "q32"], ["osf%d" % x])
+    s = slice(32, 60)
+    ts(T.i2[:, s], T.i1[:, s], 3, 7, A.logical_shift_right, A.bitwise_and, rk_, ["j2"])
+    ts(T.i3[:, 0:28], T.i1[:, s], 1, None, A.bitwise_and, None, rk_, ["j3"])
+    ts(T.i4[:, s], T.i1[:, s], 1, 3, A.logical_shift_right, A.bitwise_and, rk_, ["j4"])
+    ts(T.w1[:, s], T.i2[:, s], 16.0, None, A.mult, None, ["j2"], ["v1", "rw0", "rw1"])
+    ts(T.w2[:, s], T.i3[:, 0:28], 4.0, None, A.mult, None, ["j3"], ["v2"])
+    tt(T.w3[:, s], T.w3[:, s], T.i4[:, s], A.add, ek_ + ["j4"], ["v3"])
+    tt(T.w2[:, s], T.w2[:, s], T.w3[:, s], A.add, ["v2", "v3"], ["v2"])
+    tt(T.w1[:, s], T.w1[:, s], T.w2[:, s], A.add, ["v1", "v2"], ["v1"])
+    cp(of[:, O_R:O_R + 28], T.w1[:, s], ["v1"], ["or"])
+    cp(of[:, O_RI:O_RI + 16], T.w2[:, 44:60], ["v2"], ["ori"])
+    ts(T.i3[:, 34:35], col["q1"], 6.0, None, A.add, None, ["ff"], ["i3y"])
+    ts(T.i3[:, 34:35], T.i3[:, 34:35], 7, None, A.bitwise_and, None, ["i3y"], ["i3y"])
+    af(b16, col["b0"], 16.0, 0.0, ["ff"], ["b16"])
+    ts(of[:, O_FB:O_FB + 1], T.i3[:, 34:35], b16, None, A.add, None, ["i3y", "b16"], ["ofb"])
+    af(opc, col["b0"], 4.0, col["r1"], ["ff"], ["opc"])
+    ts(of[:, O_OP:O_OP + 1], col["w"], 8.0, opc, A.mult, A.add, ["ff", "opc"], ["oop"])
+    ms(T.po[:, 16:32], 0.0, ["poz"])
+    qz("qv", 0, 128, T.vin[:], ["vin"], ["qv"])
+
+    def chunk(c0, n, off, key, name):
+        for b in range(4):
+            out, win = T.yt[:, 4 * c0 + b:4 * (c0 + n):4], T.bt[:, 256 * b:256 * b + 256].indirect(off)
+            if b % 2:
+                cp(out, win, ["bt%d" % b, key], ["yt%s%d" % (nm, b) for nm in name], gat(n))
+            else:
+                act(out, win, FN.Copy, ["bt%d" % b, key], ["yt%s%d" % (nm, b) for nm in name], gat(n))
+        qz("qy", c0, n, T.yt[:, 4 * c0:4 * (c0 + n)], ["yt%s%d" % (nm, b) for nm in name for b in range(4)], ["qy" + nm for nm in name])
+        for b in range(4):
+            mm(4 + b, n, "qw", 128 * b, "qy", c0, True, True, ["qwc", "qws"] + ["qy" + nm for nm in name])
+        for b in range(4):
+            act(T.tmp[:, 256 * b:256 * b + n], T["ps%d" % (4 + b)][:, 0:n], FN.Relu, ["ps%d" % (4 + b)], ["tmp%d" % b], n, scale=0.015625)
+
+    def adds(pieces):
+        for b in range(4):
+            for t0, c0, n, name in pieces:
+                tt(T.xt[:, 4 * c0 + b:4 * (c0 + n):4], T.tmp[:, 256 * b + t0:256 * b + t0 + n], T["ps%d" % b][:, c0:c0 + n], A.add,
+                   ["tmp%d" % b, "ps%d" % b], ["xt%s%d" % (nm, b) for nm in name], n)
+
+    def quant(name, k, tile, tn, parts, w):
+        qz(name, 256 * k, 256, tile[:, 1024 * k:1024 * k + 1024], ["%s%s%d" % (tn, nm, b) for nm in parts for b in range(4)], [w])
+
+    def read_list(win, keys, rows, x, last, lkey, out, okey):
+        cp(T.a1[:], win.indirect(rows), keys, ["a1"], gat(64))
+        tp(T.gg[:], T.a1[:], ["a1"], ["gg"])
+        cp(T.a2[:], T.gg[:].indirect(of[:, O_C + 10 * x:O_C + 10 * x + 2]), ["gg", "oc"], ["a2_"], gat(32))
+        tp(T.uu[:], T.a2[:], ["a2_"], ["uu"])
+        cp(out, T.uu[:].indirect(of[:, last:last + 1]), ["uu", lkey], [okey], gat(16))
+
+    for x in range(3):
+        rd = x + 1
+        qx, nq, pa, land, ln = "qx%d" % rd, "qx%d" % (rd + 1), "pa%d" % rd, T["land%d" % rd], "land%d" % rd
+        own = ("qa", ["qa"]) if x == 0 else (qx, [qx + "o"])
+        win = ("ls", 0, ["lsoc", "lsos", "lsac", "lsas"]) if x == 0 else (qx, 256, [qx + "s"])
+        for b in range(4):
+            mm(b, 256, "qe", 128 * b, own[0], 0, True, False, ["qe0"] + own[1])
+        for e in range(2):
+            pick(pa, 256 * e, win[0], win[1], 256, T.ol[:, 16 * e:16 * e + 16], 16, win[2] + ["ol"], pa + str(e))
+            for b in range(4):
+                mm(b, 256, "qe", 512 * (e + 1) + 128 * b, pa, 256 * e, False, e == 1, ["qe%d" % (e + 1), pa + str(e) + "c", pa + str(e) + "s"])
+        for b in range(4):
+            out, src = T.zt[:, b:1024:4], T["ps%d" % b][:, 0:256]
+            if b % 2 == 0:
+                act(out, src, FN.Copy, ["ps%d" % b], ["zt0%d" % b], 256, scale=-1.0)
+            else:
+                ts(out, src, -1.0, None, A.mult, None, ["ps%d" % b], ["zt0%d" % b], 256)
+        quant("qz", 0, T.zt, "zt", "0", "qz")
+        mm(4, 256, "qup", 128, "qz", 0, True, True, ["qupc", "qups", "qz"])
+        mm(5, 256, "qup", 0, "qz", 0, True, True, ["qupc", "qups", "qz"])
+        act(T.sy[:], T.ps4[:, 0:256], FN.Copy, ["ps4"], ["sy"], 256)
+        for t in range(4):
+            tt(T.fl[:, t:256:4], T.ps5[:, 64 * t:64 * t + 64], T.sy[:, 64 * t:64 * t + 64], A.is_ge, ["ps5", "sy"], ["fl%d" % t])
+        qz("qf", 0, 128, T.fl[:], ["fl0", "fl1", "fl2", "fl3", "flz"], ["qf"])
+        mm(6, 128, "qc", 0, "qf", 0, True, True, ["qc", "qf"])
+        tp(T.rk[:], T.ps6[:, 0:64], ["ps6"], ["rk"])
+        tt(T.key[:], T.rk[:], T.lq[:], A.add, ["rk", "lq"], ["key"], 128)
+        for e in range(2):
+            ts(T.cl[:, 64 * e:64 * e + 64], T.key[:], bnd[e], bnd[e + 1], A.max, A.min, ["key", "bnd0", "bnd1", "bnd2"], ["cl%d" % e])
+        rec("V", lambda: g.vector.tensor_tensor_scan(T.sc[:], T.keep[:], T.cl[:], 0.0, A.mult, A.add), ["keep", "cl0", "cl1"], ["sc"], size(128))
+        mine = land[:, 16:32]
+        tt(mine, T.sc[:, 7:128:8], csub, A.subtract, ["sc", "csub"], [ln + "o"])
+
+        def slot(o, ld=land):
+            return ld[:, 16 * ((me - o + 1) % N):16 * ((me - o + 1) % N) + 16]
+
+        send(mine, slot, 0, "an%d" % rd, [ln + "o"], ln + "n")
+        if x < 2:
+            send(mine, slot, 1, "af%d" % rd, [ln + "o"], ln + "f", before=2)
+        if x == 0:
+            pick(qx, 256, "ls", 0, 256, of[:, O_SG:O_SG + 16], 16, win[2] + ["osg"], qx + "t")
+        sk = [qx + "tc", qx + "ts"] if x == 0 else [qx + "s"]
+        for b in range(4):
+            mm(b, 512, "qe", 128 * b, qx, 0, True, True, ["qe0", qx + "o", "qz"] + sk)
+        for b in range(4):
+            out, src = T.bt[:, 256 * b:256 * b + 256], T["ps%d" % b][:, 256:512]
+            if b % 2 == 0:
+                act(out, src, FN.Copy, ["ps%d" % b], ["bt%d" % b], 256)
+            else:
+                cp(out, src, ["ps%d" % b], ["bt%d" % b], 256)
+        rows = of[:, O_R + 12 * x:O_R + 12 * x + 4]
+        if x == 0:
+            read_list(land[:, 0:48], [ln + "o", ln + "n", "or"], rows, x, O_FM, "ofm", T.om[:], "om")
+            chunk(0, 256, T.om[:], "om", "ei")
+            adds([(0, 0, 256, "abi")])
+        else:
+            inner = of[:, O_RI + 12 * (x - 1):O_RI + 12 * (x - 1) + 4]
+            read_list(mine, [ln + "o", "ori"], inner, x, O_FB, "ofb", T.oi[:], "oi")
+            chunk(128, 128, T.oi[:, 8:16], "oi", "i")
+            adds([(0, 64, 128, "i")])
+            read_list(land[:, 0:48], [ln + "o", ln + "n", "or"], rows, x, O_FB, "ofb", T.om[:], "om")
+            chunk(0, 128, T.om[:, 0:8], "om", "e")
+            adds([(0, 192, 64, "a"), (64, 0, 64, "b")])
+        quant(nq, 0, T.xt, "xt", "abi", nq + "o")
+        if x < 2:
+            cand_lists(rd)
+            spread(rd)
+            cp(T.s1[:], land[:].indirect(of[:, O_R + 12 * x + 4:O_R + 12 * x + 12]), [ln + "o", ln + "n", ln + "f", "or"], ["s1"], gat(128))
+            tp(T.s2[:], T.s1[:], ["s1"], ["s2"], 128)
+            cp(T.osd[:], T.s2[:].indirect(of[:, O_SF + 2 * x:O_SF + 2 * x + 1]), ["s2", "osf%d" % x], ["os"], gat(16))
+            chunk(256, 256, T.osd[:], "os", "s")
+            adds([(0, 256, 256, "s")])
+            quant(nq, 1, T.xt, "xt", "s", nq + "s")
+        else:
+            cp(T.p1[:, 0:16], mine.indirect(of[:, O_OP:O_OP + 1]), [ln + "o", "oop"], ["p1"])
+            relabel(16, T.po[:, 0:16], "po", True)
+            tp(T.pt[:], T.po[:], ["po", "poz"], ["pt"])
+            sem = newsem("d")
+            for a in range(4):
+                dma("S", T.op[2 * a:2 * a + 2, :], T.pt[32 * a:32 * a + 16, :], ["pt"], [], sem)
+
+    dma("S", T.oc[:], T.qx4c[:].bitcast(dt.uint8), ["qx4o"], [], lat=START + 1.0)
+    for hf in range(2):
+        mm(4 + hf, 128, "qv", 0, "qx4", 128 * hf, True, True, ["qv", "qx4o"])
+    act(T.ysb[:, 0:128], T.ps4[:, 0:128], FN.Copy, ["ps4"], ["y0"], 128)
+    cp(T.ysb[:, 128:256], T.ps5[:, 0:128], ["ps5"], ["y1"], 128)
+    dma("A", T.y[:], T.ysb[:], ["y0", "y1"], [])
+    sem = newsem("d")
+    for k in range(4):
+        dma("S", T.osc[4 * k:4 * k + 4, :], T.qx4s[32 * k:32 * k + 4, :], ["qx4o"], [], sem)
+
+    for op in ops:
+        op["pre"] = list({o["n"]: o for o in [d.get("like", d) for d in op["deps"]] + op.get("after", [])}.values())
+        op["way"], op["users"], op["left"], op["ready"] = 0.0, [], len(op["pre"]), 0.0
+    for op in reversed(ops):
+        op["way"] += op["c"] + op["lat"]
+        for o in op["pre"]:
+            o["way"] = max(o["way"], op["way"] + WAKE)
+            o["users"].append(op)
+    free, order, pool = {q: 0.0 for q in Q}, [], [op for op in ops if not op["left"]]
+    while pool:
+        best = None
+        for q in Q:
+            mine_ = sorted((o for o in pool if o["q"] == q), key=lambda o: (-o["way"], o["n"]))
+            limit = 1e9
+            for o in mine_:
+                st = max(free[q], o["ready"])
+                if st + o["c"] <= limit + 0.03 and (best is None or st < best[0] - 1e-9):
+                    best = (st, o)
+                limit = min(limit, st)
+        st, op = best
+        pool = [o for o in pool if o is not op]
+        order.append(op)
+        free[op["q"]] = st + op["c"]
+        for o in op["users"]:
+            issued = any(op is a for a in o.get("after", [])) or (o["q"] == "P" and op["q"] == "P")
+            o["ready"] = max(o["ready"], st + op["c"] + (0.0 if issued else op["lat"] + WAKE))
+            o["left"] -= 1
+            if not o["left"]:
+                pool.append(o)
+
+    for op in ops:
+        op["deps"] = [o for o in op["deps"] if not (op["q"] == "P" and o["q"] == "P")]
+        for o in op["deps"]:
+            o["need"] = True
+    count = {"V": 0, "A": 0, "P": 0, "G": 0}
+    for op in order:
+        if op["tok"] is None and op["need"]:
+            count[op["q"]] += 1
+            op["at"] = ("e" + op["q"], count[op["q"]])
+    for q in count:
+        totals["e" + q] = count[q]
+    seen = {q: {} for q in Q}
+    for op in order:
+        want = {}
+        for o in op["deps"]:
+            s, v = (o["tok"], totals[o["tok"]]) if o["tok"] else o["at"]
+            want[s] = max(want.get(s, 0), v)
+        for s, v in want.items():
+            if seen[op["q"]].get(s, 0) < v:
+                Q[op["q"]].wait_ge(T.sem[s], v)
+                seen[op["q"]][s] = v
+        ins = op["fn"]()
+        if op["tok"] is None and op["need"]:
+            ins.then_inc(T.sem[op["at"][0]], 1)
+    for s, v in totals.items():
+        if v and max(seen[q].get(s, 0) for q in Q) < v:
+            g.sync.wait_ge(T.sem[s], v)

@@ -4,6 +4,8 @@ from concourse.mybir import dt, AluOpType, ActivationFunctionType
 F32, BF, I32, U16, U8, CODE = "float32", "bfloat16", "int32", "uint16", "uint8", "float8_e4m3fn_x4"
 N = 8
 STRIDE = [4, 2, 1]
+HAND = (4, 3, 5)
+USE = ("ac", "asc")
 
 SCRATCH = {}
 for _n, _w, _d in [
@@ -32,16 +34,46 @@ for _b in range(8):
     SCRATCH["ps%d" % _b] = ("psum", [128, 512], F32)
 
 SEMAPHORES = (["eV", "eA", "eP", "eG"] + ["d%d" % _i for _i in range(24)] + ["l%d" % _i for _i in range(8)]
-              + ["ap", "ac", "asc", "an1", "an2", "an3", "af1", "af2"])
+              + ["ap", "ac", "asc", "an1", "an2", "an3", "af1", "af2", "hac", "hasc", "haf1", "haf2"])
 
 A = AluOpType
 FN = ActivationFunctionType
-CY, WAKE, ROW, START = 0.001, 0.08, 0.025, 2.0
+CY, WAKE, ROW, START = 0.001, 0.12, 0.02, 2.5
 
 
 def rank_program(g, core, T, topo):
     me = T.rank_of(core)
+
+    def helpers(k):
+        out = []
+        for d in HAND:
+            out.append([c for c in reversed(topo.cores_of(T.cores[k]))
+                        if T.rank_of(c) is None and c not in out and topo.may_write(c, T.cores[(k + d) % N])][0])
+        return out
+
+    def dst(c):
+        return DstId(rid=topo.addr(c)[0], pnc=topo.addr(c)[1])
+
+    def ones(m):
+        return bin(m).count("1")
+
+    def inside(k):
+        return topo.mask(T.cores[k], helpers(k)[0]) & ~topo.mask(T.cores[k], T.cores[(k + 1) % N])
+
     if me is None:
+        for k in range(N):
+            if core in helpers(k):
+                d = HAND[helpers(k).index(core)]
+                to = T.cores[(k + d) % N]
+                m, sl = topo.mask(core, to), 16 * ((1 - d) % N)
+                msgs = [("ac", T.lsc[:, 32 * k:32 * k + 32].bitcast(dt.uint8)), ("asc", T.lss[:, 32 * k:32 * k + 32]),
+                        ("af1", T.land1[:, sl:sl + 16]), ("af2", T.land2[:, sl:sl + 16])]
+                msgs = [x for x in msgs if x[0] in USE]
+                for nm, ap in msgs:
+                    g.wait_ge(T.sem["h" + nm], ones(inside(k)))
+                    g.remote_dma_fused([RemoteDMATransfer(dst_ids=[dst(to)], dma_engine_mask=m, remote_sem=T.sem[nm], srcs=[ap], dsts=[ap])],
+                                       local_sem=T.sem["l0"])
+                g.wait_ge(T.sem["l0"], ones(m) * len(msgs))
         return
     Q = {"V": g.vector, "A": g.scalar, "P": g.tensor, "G": g, "S": g.sync}
     ops, lastw, readers, totals, used = [], {}, {}, {}, {"d": 0, "l": 0}
@@ -83,16 +115,23 @@ def rank_program(g, core, T, topo):
             m &= topo.mask(T.cores[k], T.cores[o])
         return m
 
-    def send(src, place, which, rsem, r, key, before=0):
+    def send(src, place, which, rsem, r, key, before=0, hand=None):
         to, m = group(me)[which], engines(me, which)
-        ids = [DstId(rid=topo.addr(T.cores[o])[0], pnc=topo.addr(T.cores[o])[1]) for o in to]
+        handed = [(me + d) % N for d in HAND]
+        if rsem in USE:
+            to = [o for o in to if o not in handed]
         sem = newsem("l")
-        totals[sem] = bin(m).count("1")
-        tr = RemoteDMATransfer(dst_ids=ids, dma_engine_mask=m, remote_sem=T.sem[rsem], srcs=[src], dsts=[place(o) for o in to])
-        op = rec("G", lambda: g.remote_dma_fused([tr], local_sem=T.sem[sem]), r + ["gq"], ["gq"], 0.4, tok=sem,
-                 lat=START + ROW * 128 * (len(to) + before) / totals[sem])
+        totals[sem] = ones(m)
+        trs = [RemoteDMATransfer(dst_ids=[dst(T.cores[o]) for o in to], dma_engine_mask=m, remote_sem=T.sem[rsem], srcs=[src],
+                                 dsts=[place(o) for o in to])]
+        if hand in USE:
+            trs.append(RemoteDMATransfer(dst_ids=[dst(c) for c in helpers(me)], dma_engine_mask=inside(me), remote_sem=T.sem["h" + hand],
+                                         srcs=[src], dsts=[place(o) for o in handed]))
+            totals[sem] += ones(inside(me))
+        op = rec("G", lambda: g.remote_dma_fused(trs, local_sem=T.sem[sem]), r + ["gq"], ["gq"], 0.4, tok=sem,
+                 lat=START + ROW * 128 * (len(group(me)[which]) + before) / ones(m))
         op["deps"], op["after"] = op["deps"][:len(r)], op["deps"][len(r):]
-        totals[rsem] = sum(bin(engines(s, which)).count("1") for s in to)
+        totals[rsem] = sum(ones(engines(s, which)) for s in group(me)[which])
         lastw[key] = {"q": "R", "tok": rsem, "like": op}
         return op
 
@@ -146,7 +185,7 @@ def rank_program(g, core, T, topo):
 
     dma("A", T.landp[:, 16:32], T.p[:], [], ["lpo"])
     dma("S", T.xin[:], T.x[:], [], ["xin"], lat=START + 1.0)
-    dma("S", T.uin[:], T.u[:], [], ["uin"], lat=START + 1.5)
+    dma("S", T.uin[:], T.u[:], ["lpo"], ["uin"], lat=START + 0.5)
 
     lastw["gq"] = rec("G", lambda: g.iota(T.pi[:, 0:1], [[0, 1]], 0, 1), [], ["pi"], 0.13)
     EC, X4, E8, B16, K64, E16, UX, SG, LQ = 0, 10, 14, 22, 32, 96, 112, 120, 136
@@ -183,8 +222,8 @@ def rank_program(g, core, T, topo):
     qz("qa", 0, 256, T.xin[:], ["xin"], ["qa"])
     osp = of[:, O_SP:O_SP + 2]
     pick("snd", 0, "qa", 0, 256, osp, 2, ["qa", "osp0", "osp1"], "snd")
-    send(T.sndc[:].bitcast(dt.uint8), lambda o: T.lsc[:, 32 * me:32 * me + 32].bitcast(dt.uint8), 2, "ac", ["sndc"], "lsac", before=4)
-    lastw["sent"] = send(T.snds[:], lambda o: T.lss[:, 32 * me:32 * me + 32], 2, "asc", ["snds"], "lsas", before=10)
+    send(T.sndc[:].bitcast(dt.uint8), lambda o: T.lsc[:, 32 * me:32 * me + 32].bitcast(dt.uint8), 2, "ac", ["sndc"], "lsac", before=4, hand="ac")
+    lastw["sent"] = send(T.snds[:], lambda o: T.lss[:, 32 * me:32 * me + 32], 2, "asc", ["snds"], "lsas", before=10, hand="asc")
     pick("ls", 32 * me, "qa", 0, 256, osp, 2, ["qa", "osp0", "osp1"], "lso")
     qz("qx1", 0, 256, T.xin[:], ["xin"], ["qx1o"])
 
@@ -241,7 +280,7 @@ def rank_program(g, core, T, topo):
 
     def cand_lists(x):
         rot, rn = T["rot%d" % x], "rot%d" % x
-        cp(T.a3[:], T.gg[:].indirect(of[:, O_C + 10 * x + 2:O_C + 10 * x + 10]), ["gg", "oc"], ["a3"], gat(128))
+        act(T.a3[:], T.gg[:].indirect(of[:, O_C + 10 * x + 2:O_C + 10 * x + 10]), FN.Copy, ["gg", "oc"], ["a3"], gat(128))
         tp(rot[:, 0:128], T.a3[:], ["a3"], [rn, rn + "l"], 128)
         cp(T.ol[:], rot[:, 0:64].indirect(of[:, O_FL:O_FL + 2]), [rn + "l", "ofl0", "ofl1"], ["ol"], gat(32))
 
@@ -259,8 +298,8 @@ def rank_program(g, core, T, topo):
         rot, rn, sem = T["rot%d" % x], "rot%d" % x, newsem("d")
         for j in range(1, 4):
             c0 = 64 + 64 * j
-            dma("S", rot[0:128 - 32 * j, c0:c0 + 64], rot[32 * j:128, 64:128], [rn], [rn + "j%d" % j], sem)
-            dma("S", rot[128 - 32 * j:128, c0:c0 + 64], rot[0:32 * j, 64:128], [rn], [rn + "k%d" % j], sem)
+            dma("S", rot[0:128 - 32 * j, c0:c0 + 64], rot[32 * j:128, 64:128], [rn], [rn + "j%d" % j], sem, lat=START + 1.0)
+            dma("S", rot[128 - 32 * j:128, c0:c0 + 64], rot[0:32 * j, 64:128], [rn], [rn + "k%d" % j], sem, lat=START + 1.0)
         keys = [rn + jk + str(j) for jk in "jk" for j in range(1, 4)]
         tt(T.lq[:], rot[:, 64:320].indirect(of[:, O_LQ:O_LQ + 4]), kk[:, K64:K64 + 64], A.add, [rn, "olq", "k5"] + keys, ["lq"], gat(64))
 
@@ -403,9 +442,10 @@ def rank_program(g, core, T, topo):
         quant("qz", 0, T.zt, "zt", "0", "qz")
         mm(4, 256, "qup", 128, "qz", 0, True, True, ["qupc", "qups", "qz"])
         mm(5, 256, "qup", 0, "qz", 0, True, True, ["qupc", "qups", "qz"])
-        act(T.sy[:], T.ps4[:, 0:256], FN.Copy, ["ps4"], ["sy"], 256)
+        for hf in range(2):
+            act(T.sy[:, 128 * hf:128 * hf + 128], T.ps4[:, 128 * hf:128 * hf + 128], FN.Copy, ["ps4"], ["sy%d" % hf], 128)
         for t in range(4):
-            tt(T.fl[:, t:256:4], T.ps5[:, 64 * t:64 * t + 64], T.sy[:, 64 * t:64 * t + 64], A.is_ge, ["ps5", "sy"], ["fl%d" % t])
+            tt(T.fl[:, t:256:4], T.ps5[:, 64 * t:64 * t + 64], T.sy[:, 64 * t:64 * t + 64], A.is_ge, ["ps5", "sy%d" % (t // 2)], ["fl%d" % t])
         qz("qf", 0, 128, T.fl[:], ["fl0", "fl1", "fl2", "fl3", "flz"], ["qf"])
         mm(6, 128, "qc", 0, "qf", 0, True, True, ["qc", "qf"])
         tp(T.rk[:], T.ps6[:, 0:64], ["ps6"], ["rk"])
@@ -419,7 +459,7 @@ def rank_program(g, core, T, topo):
         def slot(o, ld=land):
             return ld[:, 16 * ((me - o + 1) % N):16 * ((me - o + 1) % N) + 16]
 
-        send(mine, slot, 0, "an%d" % rd, [ln + "o"], ln + "n")
+        send(mine, slot, 0, "an%d" % rd, [ln + "o"], ln + "n", hand="af%d" % rd)
         if x < 2:
             send(mine, slot, 1, "af%d" % rd, [ln + "o"], ln + "f", before=2)
         if x == 0:
@@ -450,7 +490,7 @@ def rank_program(g, core, T, topo):
         if x < 2:
             cand_lists(rd)
             spread(rd)
-            cp(T.s1[:], land[:].indirect(of[:, O_R + 12 * x + 4:O_R + 12 * x + 12]), [ln + "o", ln + "n", ln + "f", "or"], ["s1"], gat(128))
+            act(T.s1[:], land[:].indirect(of[:, O_R + 12 * x + 4:O_R + 12 * x + 12]), FN.Copy, [ln + "o", ln + "n", ln + "f", "or"], ["s1"], gat(128))
             tp(T.s2[:], T.s1[:], ["s1"], ["s2"], 128)
             cp(T.osd[:], T.s2[:].indirect(of[:, O_SF + 2 * x:O_SF + 2 * x + 1]), ["s2", "osf%d" % x], ["os"], gat(16))
             chunk(256, 256, T.osd[:], "os", "s")

@@ -4,8 +4,7 @@ from concourse.mybir import dt, AluOpType, ActivationFunctionType
 F32, BF, I32, U16, U8, CODE = "float32", "bfloat16", "int32", "uint16", "uint8", "float8_e4m3fn_x4"
 N = 8
 STRIDE = [4, 2, 1]
-HAND = (4, 3, 5)
-USE = ("ac", "asc")
+HAND = {"ac": (4, 3, 5), "asc": (4, 3, 5), "af1": (4,), "af2": (4,)}
 
 SCRATCH = {}
 for _n, _w, _d in [
@@ -38,7 +37,7 @@ SEMAPHORES = (["eV", "eA", "eP", "eG"] + ["d%d" % _i for _i in range(24)] + ["l%
 
 A = AluOpType
 FN = ActivationFunctionType
-CY, WAKE, ROW, START = 0.001, 0.12, 0.02, 2.5
+CY, WAKE, ROW, START = 0.001, 0.2, 0.025, 1.2
 
 
 def rank_program(g, core, T, topo):
@@ -46,9 +45,9 @@ def rank_program(g, core, T, topo):
 
     def helpers(k):
         out = []
-        for d in HAND:
-            out.append([c for c in reversed(topo.cores_of(T.cores[k]))
-                        if T.rank_of(c) is None and c not in out and topo.may_write(c, T.cores[(k + d) % N])][0])
+        for j in range(max(len(v) for v in HAND.values())):
+            out.append([c for c in reversed(topo.cores_of(T.cores[k])) if T.rank_of(c) is None and c not in out
+                        and all(topo.may_write(c, T.cores[(k + v[j]) % N]) for v in HAND.values() if j < len(v))][0])
         return out
 
     def dst(c):
@@ -63,17 +62,22 @@ def rank_program(g, core, T, topo):
     if me is None:
         for k in range(N):
             if core in helpers(k):
-                d = HAND[helpers(k).index(core)]
-                to = T.cores[(k + d) % N]
-                m, sl = topo.mask(core, to), 16 * ((1 - d) % N)
-                msgs = [("ac", T.lsc[:, 32 * k:32 * k + 32].bitcast(dt.uint8)), ("asc", T.lss[:, 32 * k:32 * k + 32]),
-                        ("af1", T.land1[:, sl:sl + 16]), ("af2", T.land2[:, sl:sl + 16])]
-                msgs = [x for x in msgs if x[0] in USE]
-                for nm, ap in msgs:
+                j, sent = helpers(k).index(core), 0
+                for nm in [x for x in HAND if j < len(HAND[x])]:
+                    d = HAND[nm][j]
+                    to = T.cores[(k + d) % N]
+                    m, sl = topo.mask(core, to), 16 * ((1 - d) % N)
+                    if nm == "ac":
+                        ap = T.lsc[:, 32 * k:32 * k + 32].bitcast(dt.uint8)
+                    elif nm == "asc":
+                        ap = T.lss[:, 32 * k:32 * k + 32]
+                    else:
+                        ap = {"af1": T.land1, "af2": T.land2}[nm][:, sl:sl + 16]
+                    sent += ones(m)
                     g.wait_ge(T.sem["h" + nm], ones(inside(k)))
                     g.remote_dma_fused([RemoteDMATransfer(dst_ids=[dst(to)], dma_engine_mask=m, remote_sem=T.sem[nm], srcs=[ap], dsts=[ap])],
                                        local_sem=T.sem["l0"])
-                g.wait_ge(T.sem["l0"], ones(m) * len(msgs))
+                g.wait_ge(T.sem["l0"], sent)
         return
     Q = {"V": g.vector, "A": g.scalar, "P": g.tensor, "G": g, "S": g.sync}
     ops, lastw, readers, totals, used = [], {}, {}, {}, {"d": 0, "l": 0}
@@ -117,17 +121,16 @@ def rank_program(g, core, T, topo):
 
     def send(src, place, which, rsem, r, key, before=0, hand=None):
         to, m = group(me)[which], engines(me, which)
-        handed = [(me + d) % N for d in HAND]
-        if rsem in USE:
+        handed = [(me + d) % N for d in HAND.get(hand or rsem, ())]
+        if rsem in HAND:
             to = [o for o in to if o not in handed]
         sem = newsem("l")
-        totals[sem] = ones(m)
         trs = [RemoteDMATransfer(dst_ids=[dst(T.cores[o]) for o in to], dma_engine_mask=m, remote_sem=T.sem[rsem], srcs=[src],
                                  dsts=[place(o) for o in to])]
-        if hand in USE:
-            trs.append(RemoteDMATransfer(dst_ids=[dst(c) for c in helpers(me)], dma_engine_mask=inside(me), remote_sem=T.sem["h" + hand],
-                                         srcs=[src], dsts=[place(o) for o in handed]))
-            totals[sem] += ones(inside(me))
+        if hand in HAND:
+            trs.append(RemoteDMATransfer(dst_ids=[dst(c) for c in helpers(me)[:len(handed)]], dma_engine_mask=inside(me),
+                                         remote_sem=T.sem["h" + hand], srcs=[src], dsts=[place(o) for o in handed]))
+        totals[sem] = ones(m) + (ones(inside(me)) if hand in HAND else 0)
         op = rec("G", lambda: g.remote_dma_fused(trs, local_sem=T.sem[sem]), r + ["gq"], ["gq"], 0.4, tok=sem,
                  lat=START + ROW * 128 * (len(group(me)[which]) + before) / ones(m))
         op["deps"], op["after"] = op["deps"][:len(r)], op["deps"][len(r):]
@@ -300,7 +303,10 @@ def rank_program(g, core, T, topo):
             c0 = 64 + 64 * j
             dma("S", rot[0:128 - 32 * j, c0:c0 + 64], rot[32 * j:128, 64:128], [rn], [rn + "j%d" % j], sem, lat=START + 1.0)
             dma("S", rot[128 - 32 * j:128, c0:c0 + 64], rot[0:32 * j, 64:128], [rn], [rn + "k%d" % j], sem, lat=START + 1.0)
-        keys = [rn + jk + str(j) for jk in "jk" for j in range(1, 4)]
+
+    def keys_of(x, after):
+        rot, rn = T["rot%d" % x], "rot%d" % x
+        keys = [after] + [rn + jk + str(j) for jk in "jk" for j in range(1, 4)]
         tt(T.lq[:], rot[:, 64:320].indirect(of[:, O_LQ:O_LQ + 4]), kk[:, K64:K64 + 64], A.add, [rn, "olq", "k5"] + keys, ["lq"], gat(64))
 
     l1, l2 = cnew(), cnew()
@@ -393,7 +399,7 @@ def rank_program(g, core, T, topo):
     ms(T.po[:, 16:32], 0.0, ["poz"])
     qz("qv", 0, 128, T.vin[:], ["vin"], ["qv"])
 
-    def chunk(c0, n, off, key, name):
+    def chunk(c0, n, off, key, name, t0=0):
         for b in range(4):
             out, win = T.yt[:, 4 * c0 + b:4 * (c0 + n):4], T.bt[:, 256 * b:256 * b + 256].indirect(off)
             if b % 2:
@@ -404,13 +410,15 @@ def rank_program(g, core, T, topo):
         for b in range(4):
             mm(4 + b, n, "qw", 128 * b, "qy", c0, True, True, ["qwc", "qws"] + ["qy" + nm for nm in name])
         for b in range(4):
-            act(T.tmp[:, 256 * b:256 * b + n], T["ps%d" % (4 + b)][:, 0:n], FN.Relu, ["ps%d" % (4 + b)], ["tmp%d" % b], n, scale=0.015625)
+            act(T.tmp[:, 256 * b + t0:256 * b + t0 + n], T["ps%d" % (4 + b)][:, 0:n], FN.Relu, ["ps%d" % (4 + b)],
+                ["tmp%d%d" % (b, k) for k in range(t0 // 128, (t0 + n) // 128)], n, scale=0.015625)
 
     def adds(pieces):
         for b in range(4):
             for t0, c0, n, name in pieces:
                 tt(T.xt[:, 4 * c0 + b:4 * (c0 + n):4], T.tmp[:, 256 * b + t0:256 * b + t0 + n], T["ps%d" % b][:, c0:c0 + n], A.add,
-                   ["tmp%d" % b, "ps%d" % b], ["xt%s%d" % (nm, b) for nm in name], n)
+                   ["tmp%d%d" % (b, k) for k in range(t0 // 128, (t0 + n + 127) // 128)] + ["ps%d" % b],
+                   ["xt%s%d" % (nm, b) for nm in name], n)
 
     def quant(name, k, tile, tn, parts, w):
         qz(name, 256 * k, 256, tile[:, 1024 * k:1024 * k + 1024], ["%s%s%d" % (tn, nm, b) for nm in parts for b in range(4)], [w])
@@ -426,7 +434,7 @@ def rank_program(g, core, T, topo):
         rd = x + 1
         qx, nq, pa, land, ln = "qx%d" % rd, "qx%d" % (rd + 1), "pa%d" % rd, T["land%d" % rd], "land%d" % rd
         own = ("qa", ["qa"]) if x == 0 else (qx, [qx + "o"])
-        win = ("ls", 0, ["lsoc", "lsos", "lsac", "lsas"]) if x == 0 else (qx, 256, [qx + "s"])
+        win = ("ls", 0, ["lsoc", "lsos", "lsac", "lsas"]) if x == 0 else (qx, 256, [qx + "s", qx + "t"])
         for b in range(4):
             mm(b, 256, "qe", 128 * b, own[0], 0, True, False, ["qe0"] + own[1])
         for e in range(2):
@@ -440,6 +448,7 @@ def rank_program(g, core, T, topo):
             else:
                 ts(out, src, -1.0, None, A.mult, None, ["ps%d" % b], ["zt0%d" % b], 256)
         quant("qz", 0, T.zt, "zt", "0", "qz")
+        keys_of(x, "qz")
         mm(4, 256, "qup", 128, "qz", 0, True, True, ["qupc", "qups", "qz"])
         mm(5, 256, "qup", 0, "qz", 0, True, True, ["qupc", "qups", "qz"])
         for hf in range(2):
@@ -464,7 +473,7 @@ def rank_program(g, core, T, topo):
             send(mine, slot, 1, "af%d" % rd, [ln + "o"], ln + "f", before=2)
         if x == 0:
             pick(qx, 256, "ls", 0, 256, of[:, O_SG:O_SG + 16], 16, win[2] + ["osg"], qx + "t")
-        sk = [qx + "tc", qx + "ts"] if x == 0 else [qx + "s"]
+        sk = [qx + "tc", qx + "ts"] if x == 0 else [qx + "s", qx + "t"]
         for b in range(4):
             mm(b, 512, "qe", 128 * b, qx, 0, True, True, ["qe0", qx + "o", "qz"] + sk)
         for b in range(4):
@@ -493,9 +502,11 @@ def rank_program(g, core, T, topo):
             act(T.s1[:], land[:].indirect(of[:, O_R + 12 * x + 4:O_R + 12 * x + 12]), FN.Copy, [ln + "o", ln + "n", ln + "f", "or"], ["s1"], gat(128))
             tp(T.s2[:], T.s1[:], ["s1"], ["s2"], 128)
             cp(T.osd[:], T.s2[:].indirect(of[:, O_SF + 2 * x:O_SF + 2 * x + 1]), ["s2", "osf%d" % x], ["os"], gat(16))
-            chunk(256, 256, T.osd[:], "os", "s")
-            adds([(0, 256, 256, "s")])
-            quant(nq, 1, T.xt, "xt", "s", nq + "s")
+            for hf in range(2):
+                nm = "st"[hf]
+                chunk(256 + 128 * hf, 128, T.osd[:, 8 * hf:8 * hf + 8], "os", nm, 128 * hf)
+                adds([(128 * hf, 256 + 128 * hf, 128, nm)])
+                qz(nq, 256 + 128 * hf, 128, T.xt[:, 1024 + 512 * hf:1536 + 512 * hf], ["xt%s%d" % (nm, b) for b in range(4)], [nq + nm])
         else:
             cp(T.p1[:, 0:16], mine.indirect(of[:, O_OP:O_OP + 1]), [ln + "o", "oop"], ["p1"])
             relabel(16, T.po[:, 0:16], "po", True)

@@ -4,23 +4,24 @@ from concourse.mybir import dt, AluOpType, ActivationFunctionType
 F32, BF, I32, U16, U8, CODE = "float32", "bfloat16", "int32", "uint16", "uint8", "float8_e4m3fn_x4"
 N = 8
 STRIDE = [4, 2, 1]
+DIR = [(-1, 0), (-1, 1), (0, 1), (1, 1), (1, 0), (1, -1), (0, -1), (-1, -1)]
 HAND = {"ac": (4, 3, 5), "asc": (4, 3, 5), "af1": (4,), "af2": (4,)}
+GATHER = {"own": "AVAV", "inner": "AVAV", "edge": "AVAV", "s": "AVAV", "t": "AAAA"}
 
 SCRATCH = {}
 for _n, _w, _d in [
     ("xin", 1024, BF), ("uin", 512, BF), ("vin", 512, BF), ("landp", 48, I32),
     ("land1", 128, BF), ("land2", 128, BF), ("land3", 48, BF),
-    ("eb", 2048, BF), ("idn", 128, BF), ("vv", 128, BF), ("va", 128, BF), ("vb", 128, BF), ("cb", 512, BF),
-    ("pi", 2, I32), ("fi", 16, I32), ("ff", 16, F32), ("kk", 192, F32), ("cc", 64, F32),
-    ("gi", 32, I32), ("g1", 32, F32), ("g2", 32, F32), ("dd", 32, F32),
-    ("w1", 64, F32), ("w2", 64, F32), ("w3", 64, F32), ("i1", 64, I32), ("i2", 64, I32), ("i3", 64, I32), ("i4", 64, I32),
-    ("of", 128, U16), ("keep", 128, F32),
-    ("zt", 1024, BF), ("yt", 2048, BF), ("xt", 2048, BF), ("bt", 1024, BF), ("tmp", 1024, F32),
-    ("sy", 256, F32), ("fl", 512, BF), ("rk", 64, F32), ("key", 64, F32), ("cl", 128, F32), ("sc", 128, F32),
-    ("lq", 64, F32), ("a1", 64, BF), ("gg", 64, BF), ("a2", 32, F32), ("uu", 32, F32), ("a3", 128, F32),
-    ("s1", 128, F32), ("s2", 128, F32), ("rot0", 320, F32), ("rot1", 320, F32), ("rot2", 320, F32),
+    ("ez", 520, BF), ("idn", 128, BF), ("vv", 128, BF), ("va", 128, BF), ("vb", 128, BF), ("cb", 512, BF),
+    ("pi", 4, I32), ("fi", 16, I32), ("ff", 16, F32), ("kk", 64, F32), ("cc", 64, F32), ("dd", 32, F32),
+    ("w1", 48, F32), ("w2", 48, F32), ("w3", 48, F32), ("i1", 48, I32), ("i2", 16, I32), ("i3", 16, I32),
+    ("of", 128, U16),
+    ("zt", 1024, BF), ("yt", 2048, BF), ("xt", 2048, BF), ("bt", 1024, BF), ("fo", 1024, BF),
+    ("sy", 256, F32), ("fl", 512, BF), ("ns", 128, BF), ("nt", 128, BF), ("sc", 128, BF),
+    ("lq", 72, BF), ("df", 128, BF), ("a1", 64, BF), ("gg", 64, BF), ("a2", 32, BF), ("uu", 32, BF), ("a3", 128, BF),
+    ("s1", 128, BF), ("s2", 128, BF), ("rot0", 320, BF), ("rot1", 320, BF), ("rot2", 320, BF),
     ("om", 16, U16), ("oi", 16, U16), ("osd", 16, U16), ("ol", 32, U16),
-    ("p1", 64, I32), ("p2", 64, I32), ("p3", 64, I32), ("p4", 64, F32), ("p5", 64, F32), ("po", 32, F32), ("pt", 32, F32),
+    ("p1", 64, F32), ("p2", 64, F32), ("p3", 64, F32), ("po", 32, F32), ("pt", 32, F32),
     ("ysb", 256, F32),
 ]:
     SCRATCH[_n] = ("sbuf", [128, _w], _d)
@@ -37,7 +38,7 @@ SEMAPHORES = (["eV", "eA", "eP", "eG"] + ["d%d" % _i for _i in range(24)] + ["l%
 
 A = AluOpType
 FN = ActivationFunctionType
-CY, WAKE, ROW, START = 0.001, 0.2, 0.025, 1.2
+CY, PE, WAKE, ROW, START = 0.00085, 0.0006, 0.2, 0.025, 1.2
 
 
 def rank_program(g, core, T, topo):
@@ -132,7 +133,7 @@ def rank_program(g, core, T, topo):
                                          remote_sem=T.sem["h" + hand], srcs=[src], dsts=[place(o) for o in handed]))
         totals[sem] = ones(m) + (ones(inside(me)) if hand in HAND else 0)
         op = rec("G", lambda: g.remote_dma_fused(trs, local_sem=T.sem[sem]), r + ["gq"], ["gq"], 0.4, tok=sem,
-                 lat=START + ROW * 128 * (len(group(me)[which]) + before) / ones(m))
+                 lat=START + ROW * 128 * (len(to) + before) / ones(m))
         op["deps"], op["after"] = op["deps"][:len(r)], op["deps"][len(r):]
         totals[rsem] = sum(ones(engines(s, which)) for s in group(me)[which])
         lastw[key] = {"q": "R", "tok": rsem, "like": op}
@@ -168,134 +169,141 @@ def rank_program(g, core, T, topo):
         return rec("G", lambda: g.iota(out, pat, base, cm, allow_small_or_imprecise_dtypes=True), [], w, 0.13 + 2 * n * CY)
 
     def qz(name, a, n, tile, r, w):
-        return rec("V", lambda: g.vector.quantize_mx(T[name + "c"][:, a:a + n], T[name + "s"][:, a:a + n], tile), r, w, 1.1 * n * CY)
+        return rec("V", lambda: g.vector.quantize_mx(T[name + "c"][:, a:a + n], T[name + "s"][:, a:a + n], tile), r, w, 0.012 + 0.0009 * n)
 
     def mm(bank, n, sn, sa, mn, ma, start, stop, r):
         return rec("P", lambda: g.tensor.matmul_mx(T["ps%d" % bank][:, 0:n], T[sn + "c"][:, sa:sa + 128], T[sn + "s"][:, sa:sa + 128],
                                                    T[mn + "c"][:, ma:ma + n], T[mn + "s"][:, ma:ma + n], start, stop),
-                   r, ["ps%d" % bank], 0.6 * (n + 16) * CY)
+                   r, ["ps%d" % bank], (n + 16) * PE)
 
     def gat(n):
-        return int(55 + 1.5 * n)
+        return int(65 + 1.5 * n)
 
     def pick(dn, da, sn, sa, sw, off, k, r, w):
         n = 16 * k
         cp(T[dn + "c"][:, da:da + n].bitcast(dt.uint32), T[sn + "c"][:, sa:sa + sw].bitcast(dt.uint32).indirect(off), r, [w + "c"], gat(n))
         act(T[dn + "s"][:, da:da + n], T[sn + "s"][:, sa:sa + sw].indirect(off), FN.Copy, r, [w + "s"], gat(n))
 
+    def units(name, c0, n, bs=range(4)):
+        return ["%s%d_%d" % (name, k, b) for k in range(c0 // 64, (c0 + n) // 64) for b in bs]
+
     prv, nxt = group(me)[0]
     ff, kk, cc, of, dd = T.ff, T.kk, T.cc, T.of, T.dd
 
     dma("A", T.landp[:, 16:32], T.p[:], [], ["lpo"])
-    dma("S", T.xin[:], T.x[:], [], ["xin"], lat=START + 1.0)
+    dma("S", T.xin[:, 256:1024], T.x[:, 0:768], [], ["xin0"], lat=START + 1.0)
+    dma("A", T.xin[:, 0:256], T.x[:, 768:1024], [], ["xin1"], lat=START + 0.5)
     dma("S", T.uin[:], T.u[:], ["lpo"], ["uin"], lat=START + 0.5)
 
-    lastw["gq"] = rec("G", lambda: g.iota(T.pi[:, 0:1], [[0, 1]], 0, 1), [], ["pi"], 0.13)
-    EC, X4, E8, B16, K64, E16, UX, SG, LQ = 0, 10, 14, 22, 32, 96, 112, 120, 136
+    lastw["gq"] = rec("G", lambda: g.iota(T.pi[:], [[2, 4]], 0, 1), [], ["pi"], 0.13)
+    EC, UX, SG, LQ = 0, 10, 18, 34
     iota(T.idn[:], [[-1, 128]], 0, 1, ["idn"], 128)
     iota(kk[:, EC:EC + 2], [[1, 2]], 0, 0, ["k0"])
     iota(kk[:, EC + 2:EC + 10], [[0, 2], [1, 2], [0, 2]], 0, 0, ["k1"])
-    iota(kk[:, X4:X4 + 4], [[0, 2], [16, 2]], 0, 0, ["k2"])
     iota(T.vv[:], [[1, 32], [-8, 4]], 0, 0, ["vv"], 128)
     iota(kk[:, UX:UX + 8], [[0, 2], [32, 4]], 0, 0, ["k7"])
     iota(kk[:, LQ:LQ + 4], [[1, 2], [4, 2]], 0, 0, ["k9"])
-    iota(kk[:, K64:K64 + 64], [[0, 8], [-256, 8]], 1792, 0, ["k5"], 64)
-    iota(kk[:, E16:E16 + 16], [[1, 2], [0, 8]], 0, 0, ["k6"])
-    iota(kk[:, SG:SG + 16], [[64, 4], [1, 4]], 0, 0, ["k8"])
-    iota(kk[:, E8:E8 + 8], [[0, 4], [1, 2]], 0, 0, ["k3"])
-    iota(kk[:, B16:B16 + 8], [[16, 4], [0, 2]], 0, 0, ["k4"])
-    send(T.landp[:, 16:32], lambda o: T.landp[:, 32:48] if o == prv else T.landp[:, 0:16], 0, "ap", ["lpo"], "lpa", before=6)
+    iota(kk[:, SG:SG + 16], [[1, 4], [64, 4]], 0, 0, ["k8"])
+    for a in range(4):
+        dr, dc = DIR[2 * a]
+        for i, c in enumerate((dr, dc, -dr)):
+            ms(dd[32 * a:32 * a + 32, i:i + 1], float(c), ["dd%d%d" % (a, i)])
+    dks = ["dd%d%d" % (a, i) for a in range(4) for i in range(3)]
+    send(T.landp[:, 16:32], lambda o: T.landp[:, 32:48] if o == prv else T.landp[:, 0:16], 0, "ap", ["lpo"], "lpa", before=4)
 
-    fields = {"q": (0, 15), "r": (0, 7), "w": (3, 1), "ch": (4, 1), "a": (5, 3), "g": (4, 7), "lo": (3, 7), "top": (6, 1),
-              "b0": (0, 1), "r1": (1, 3), "q1": (1, 7), "q2": (2, 3), "cs": (0, 3)}
+    fields = {"q": (0, 0, 15), "r": (0, 0, 7), "ch": (0, 4, 1), "r6": (3, 0, 7), "a": (0, 5, 3), "q1": (0, 1, 7), "k2": (0, 2, 3),
+              "lo": (0, 3, 7), "k3": (2, 2, 3)}
     col = {}
-    for i, (nm, (sh, an)) in enumerate(fields.items()):
-        ts(T.fi[:, i:i + 1], T.pi[:, 0:1], sh, an, A.logical_shift_right, A.bitwise_and, ["pi"], ["fi%d" % i])
+    for i, (nm, (j, sh, an)) in enumerate(fields.items()):
+        ts(T.fi[:, i:i + 1], T.pi[:, j:j + 1], sh, an, A.logical_shift_right, A.bitwise_and, ["pi"], ["fi%d" % i])
         col[nm] = ff[:, i:i + 1]
-    cp(ff[:, 0:13], T.fi[:, 0:13], ["fi%d" % i for i in range(13)], ["ff"])
-    O_SP, O_R0, O_C, O_FM, O_FL, O_LQ, O_U, O_SG, O_R, O_SF, O_OP, O_FB, O_RI = 0, 2, 6, 36, 38, 40, 44, 60, 76, 104, 108, 110, 112
-    ts(of[:, O_SP:O_SP + 1], col["q"], 8.0, 0.0, A.mult, A.add, ["ff"], ["osp0"])
-    ts(of[:, O_SP + 1:O_SP + 2], col["q"], 8.0, 128.0, A.mult, A.add, ["ff"], ["osp1"])
+    cp(ff[:, 0:9], T.fi[:, 0:9], ["fi%d" % i for i in range(9)], list(fields))
     taken = [0]
 
-    def cnew(n=1):
-        taken[0] += n
-        return cc[:, taken[0] - n:taken[0]]
+    def lin(name, *terms):
+        taken[0] += 1
+        out = col[name] = cc[:, taken[0] - 1:taken[0]]
+        rest, keys = terms[-1], []
+        if isinstance(rest, str):
+            rest, keys = col[rest], [rest]
+        for f, nm in terms[:-1]:
+            if isinstance(f, str):
+                af(out, col[nm], col[f], rest, [nm, f] + keys, [name])
+            else:
+                af(out, col[nm], float(f), rest, [nm] + keys, [name])
+            rest, keys = out, [name]
+        return out
 
-    qz("qa", 0, 256, T.xin[:], ["xin"], ["qa"])
+    O_SP, O_R0, O_C, O_FM, O_CP, O_OP, O_LQ, O_U, O_SG, O_R, O_RI, O_S = 0, 2, 6, 40, 44, 46, 48, 52, 68, 84, 96, 104
+    ts(of[:, O_SP:O_SP + 1], col["q"], 8.0, 64.0, A.mult, A.add, ["q"], ["osp0"])
+    ts(of[:, O_SP + 1:O_SP + 2], col["r"], 32.0, lin("sp", (-24, "q"), 192.0), A.mult, A.add, ["r", "sp"], ["osp1"])
+
+    qz("qa", 0, 256, T.xin[:], ["xin0", "xin1"], ["qa"])
     osp = of[:, O_SP:O_SP + 2]
     pick("snd", 0, "qa", 0, 256, osp, 2, ["qa", "osp0", "osp1"], "snd")
     send(T.sndc[:].bitcast(dt.uint8), lambda o: T.lsc[:, 32 * me:32 * me + 32].bitcast(dt.uint8), 2, "ac", ["sndc"], "lsac", before=4, hand="ac")
-    lastw["sent"] = send(T.snds[:], lambda o: T.lss[:, 32 * me:32 * me + 32], 2, "asc", ["snds"], "lsas", before=10, hand="asc")
+    lastw["sent"] = send(T.snds[:], lambda o: T.lss[:, 32 * me:32 * me + 32], 2, "asc", ["snds"], "lsas", before=8, hand="asc")
     pick("ls", 32 * me, "qa", 0, 256, osp, 2, ["qa", "osp0", "osp1"], "lso")
-    qz("qx1", 0, 256, T.xin[:], ["xin"], ["qx1o"])
 
-    ms(T.eb[:, 0:512], 0.0, ["eb0"], 256)
-    for b in range(1, 4):
-        act(T.eb[:, 512 * b:512 * b + 512], T.eb[:, 0:512], FN.Copy, ["eb0"], ["eb%d" % b], 512)
+    ms(T.ez[:], 0.0, ["ez"], 260)
     ts(T.idn[:], T.idn[:], 0.0, None, A.is_equal, None, ["idn"], ["idn"])
-    nev, nod = cnew(), cnew()
-    af(nev, col["ch"], 1.0, -1.0, ["ff"], ["nev"])
-    af(nod, col["ch"], -1.0, 0.0, ["ff"], ["nod"])
-    for v, (scale, keys) in enumerate([(1.0, []), (nev, ["nev"]), (nod, ["nod"])]):
+    lin("nev", (1, "ch"), -1.0)
+    lin("nod", (-1, "ch"), 0.0)
+    for v, nm in enumerate([None, "nev", "nod"]):
+        act(T.ez[:, 3:515:4], T.idn[:], FN.Identity, ["idn"] + ([nm] if nm else []), ["ez"], 128, scale=col[nm] if nm else 1.0)
         for b in range(4):
-            act(T.eb[:, 512 * b + b:512 * (b + 1):4], T.idn[:], FN.Identity, ["idn"] + keys, ["eb%d" % b], 128, scale=scale)
-        qz("qe", 512 * v, 512, T.eb[:], ["eb%d" % b for b in range(4)], ["qe%d" % v])
+            qz("qe", 512 * v + 128 * b, 128, T.ez[:, 3 - b:515 - b], ["ez"], ["qe%d%d" % (v, b)])
 
-    a2 = cnew()
-    ts(a2, col["a"], 2.0, None, A.mult, None, ["ff"], ["a2"])
-    ts(T.gi[:, 0:10], kk[:, EC:EC + 10], a2, 2.0, A.add, A.add, ["k0", "k1", "a2"], ["gia"])
-    ts(T.gi[:, 10:14], kk[:, EC + 2:EC + 6], a2, None, A.add, None, ["k1", "a2"], ["gib"])
-    ts(T.gi[:, 14:15], col["g"], 0.0, None, A.add, None, ["ff"], ["gic"])
-    ts(T.gi[:, 15:16], col["g"], 2.0, None, A.add, None, ["ff"], ["gid"])
-    ts(T.gi[:, 16:24], kk[:, E8:E8 + 8], a2, None, A.add, None, ["k3", "a2"], ["gie"])
-    s = slice(0, 24)
-    ts(T.gi[:, s], T.gi[:, s], 7, None, A.bitwise_and, None, ["gia", "gib", "gic", "gid", "gie"], ["gi"])
-    ts(T.g1[:, s], T.gi[:, s], -2.0, 1.0, A.add, A.min, ["gi"], ["g1"])
-    ts(T.g2[:, s], T.gi[:, s], -1.0, 6.0, A.mult, A.add, ["gi"], ["g2"])
-    tt(T.g1[:, s], T.g1[:, s], T.g2[:, s], A.min, ["g1", "g2"], ["g1"])
-    ts(dd[:, s], T.g1[:, s], -1.0, None, A.max, None, ["g1"], ["dd"])
+    for i, nm in enumerate(["dr", "dc", "ndr"]):
+        col[nm] = dd[:, i:i + 1]
+    af(dd[:, 4:8], kk[:, EC + 2:EC + 6], col["dc"], col["dr"], ["k1"] + dks, ["drt", "dr", "dc", "ndr"])
+    af(dd[:, 8:18], kk[:, EC:EC + 10], col["ndr"], col["dc"], ["k0", "k1", "dr"], ["dct"])
+    lin("rg", ("dc", "ch"), "dr")
+    lin("cg", ("ndr", "ch"), "dc")
+    lin("r2", (2, "r6"), 16.0)
+    ts(of[:, O_R0:O_R0 + 4], kk[:, EC + 2:EC + 6], lin("r0c", (8, "rg"), "r2"), None, A.add, None, ["k1", "r0c"], ["or0"])
 
-    c16, r2, fm, r0c = cnew(), cnew(), cnew(), cnew()
-    xa = taken[0]
-    x10 = cnew(10)
-    af(c16, col["ch"], 16.0, col["q"], ["ff"], ["c16"])
-    af(r2, col["r"], 2.0, 16.0, ["ff"], ["r2"])
-    af(fm, col["b0"], 16.0, col["q1"], ["ff"], ["fm"])
-    af(cc[:, xa:xa + 6], kk[:, EC:EC + 6], 0.0, c16, ["k0", "k1", "c16"], ["x10a"])
-    af(cc[:, xa + 6:xa + 10], kk[:, X4:X4 + 4], 1.0, col["q"], ["k2", "ff"], ["x10b"])
-    ts(of[:, O_FM:O_FM + 1], fm, 0.0, None, A.add, None, ["fm"], ["ofm"])
-    ts(of[:, O_FL:O_FL + 1], fm, 8.0, None, A.add, None, ["fm"], ["ofl0"])
-    ts(of[:, O_FL + 1:O_FL + 2], fm, 40.0, None, A.add, None, ["fm"], ["ofl1"])
-    ts(r0c, dd[:, 14:15], 8.0, r2, A.mult, A.add, ["dd", "r2"], ["r0c"])
-    ts(of[:, O_R0:O_R0 + 4], kk[:, EC + 2:EC + 6], r0c, None, A.add, None, ["k1", "r0c"], ["or0"])
-    for i, h in enumerate(STRIDE):
-        s = slice(10 * i, 10 * i + 10)
-        ts(T.w1[:, s], dd[:, 0:10], float(h), 32.0, A.mult, A.add, ["dd"], ["w1%d" % i])
-        af(T.w3[:, s], kk[:, EC:EC + 10], 32.0, 0.0, ["k0", "k1"], ["w3%d" % i])
-        tt(T.i1[:, s], T.w1[:, s], x10, A.add, ["w1%d" % i, "x10a", "x10b"], ["i1%d" % i])
-    ts(T.i1[:, 0:30], T.i1[:, 0:30], 31, None, A.bitwise_and, None, ["i10", "i11", "i12"], ["i1"])
+    lin("q32", (1, "q"), 32.0)
+    lin("q48", (1, "q"), 48.0)
+    lin("c16", (16, "ch"), "q32")
+    lin("t8", (8, "k2"), 32.0)
+    lin("t32", (32, "q"), (-128, "k2"), 0.0)
+    lin("j8", (8, "q1"), (-8, "a"), 32.0)
+    raw, add = [], []
+    for x, h in enumerate(STRIDE):
+        o = 10 * x
+        af(T.w1[:, o:o + 6], dd[:, 8:14], float(h), col["c16"], ["dct", "c16"], ["w1a%d" % x])
+        af(T.w1[:, o + 6:o + 10:2], dd[:, 14:18:2], float(h), col["q32"], ["dct", "q32"], ["w1b%d" % x])
+        af(T.w1[:, o + 7:o + 10:2], dd[:, 15:18:2], float(h), col["q48"], ["dct", "q48"], ["w1c%d" % x])
+        af(T.w2[:, o:o + 10], kk[:, EC:EC + 10], 32.0, 0.0, ["k0", "k1"], ["w2a%d" % x])
+        raw += ["w1a%d" % x, "w1b%d" % x, "w1c%d" % x]
+        add += ["w2a%d" % x]
+    for x in range(2):
+        af(T.w1[:, 30 + 2 * x:31 + 2 * x], col["cg"], float(STRIDE[x]), col["t8"], ["cg", "t8"], ["w1d%d" % x])
+    af(T.w1[:, 31:32], col["j8"], 1.0, 0.0, ["j8"], ["w1e"])
+    af(T.w2[:, 30:33], kk[:, EC:EC + 3], 0.0, col["t32"], ["k0", "k1", "t32"], ["w2b"])
+    cp(T.i1[:, 0:33], T.w1[:, 0:33], raw + ["w1d0", "w1d1", "w1e"], ["i1"])
+    ts(T.i1[:, 0:33], T.i1[:, 0:33], 31, None, A.bitwise_and, None, ["i1"], ["i1"])
     ts(T.i2[:, 2:10], T.i1[:, 2:10], 16, None, A.bitwise_and, None, ["i1"], ["i2"])
-    af(T.w2[:, 2:10], kk[:, EC + 2:EC + 10], 16.0, 0.0, ["k1"], ["w2"])
-    tt(T.w3[:, 2:10], T.w2[:, 2:10], T.i2[:, 2:10], A.add, ["w2", "i2", "w30"], ["w30"])
-    tt(T.w1[:, 0:30], T.w3[:, 0:30], T.i1[:, 0:30], A.add, ["w30", "w31", "w32", "i1"], ["w10", "w11", "w12"])
-    cp(of[:, O_C:O_C + 30], T.w1[:, 0:30], ["w10"], ["oc"])
+    af(T.w3[:, 2:10], kk[:, EC + 2:EC + 10], 16.0, 0.0, ["k1"], ["w3"])
+    tt(T.w2[:, 2:10], T.w3[:, 2:10], T.i2[:, 2:10], A.add, ["w3", "i2"], ["w2a0"])
+    tt(T.w1[:, 0:33], T.w2[:, 0:33], T.i1[:, 0:33], A.add, add + ["w2b", "i1"], ["w1"])
+    cp(of[:, O_C:O_C + 33], T.w1[:, 0:33], ["w1"], ["oc"])
+    ts(of[:, O_FM:O_FM + 4], kk[:, LQ:LQ + 4], 8.0, lin("fm", (16, "q"), (-31, "q1"), 0.0), A.mult, A.add, ["k9", "fm"], ["ofm"])
 
     def cand_lists(x):
         rot, rn = T["rot%d" % x], "rot%d" % x
         act(T.a3[:], T.gg[:].indirect(of[:, O_C + 10 * x + 2:O_C + 10 * x + 10]), FN.Copy, ["gg", "oc"], ["a3"], gat(128))
-        tp(rot[:, 0:128], T.a3[:], ["a3"], [rn, rn + "l"], 128)
-        cp(T.ol[:], rot[:, 0:64].indirect(of[:, O_FL:O_FL + 2]), [rn + "l", "ofl0", "ofl1"], ["ol"], gat(32))
+        tp(rot[:, 0:128], T.a3[:], ["a3"], [rn, rn + "l"])
+        cp(T.ol[:], rot[:, 0:64].indirect(of[:, O_FM + 2:O_FM + 4]), [rn + "l", "ofm"], ["ol"], gat(32))
 
-    def relabel(n, out, wkey, back):
-        s = slice(0, n)
-        ts(T.p2[:, s], T.p1[:, s], 4 if back else 0, 3, A.logical_shift_right, A.bitwise_and, ["p1"], ["p2"])
-        ts(T.p3[:, s], T.p1[:, s], 0 if back else 2, 15, A.logical_shift_right, A.bitwise_and, ["p1"], ["p3"])
-        sg = -1.0 if back else 1.0
-        ts(T.p4[:, s], T.p2[:, s], 15.0 * sg, None, A.mult, None, ["p2"], ["p4"])
-        ts(T.p5[:, s], T.p3[:, s], -3.0 * sg, None, A.mult, None, ["p3"], ["p5"])
-        tt(T.p4[:, s], T.p4[:, s], T.p1[:, s], A.add, ["p4", "p1"], ["p4"], 2 * n)
-        tt(out, T.p4[:, s], T.p5[:, s], A.add, ["p4", "p5"], [wkey], 2 * n)
+    def relabel(src, n, out, rkey, wkey, back):
+        s, step = slice(0, n), 64.0 if back else 4.0
+        big = 1.5 * 2.0 ** 23 * step
+        ts(T.p1[:, s], src, 0.5 - step / 2, big, A.add, A.add, [rkey], ["p1"])
+        ts(T.p2[:, s], T.p1[:, s], -big, -255.0 / step, A.add, A.mult, ["p1"], ["p2"])
+        af(T.p3[:, s], src, 256.0 / step, 0.0, [rkey], ["p3"])
+        tt(out, T.p2[:, s], T.p3[:, s], A.add, ["p2", "p3"], [wkey], 2 * n)
 
     def spread(x):
         rot, rn, sem = T["rot%d" % x], "rot%d" % x, newsem("d")
@@ -304,166 +312,144 @@ def rank_program(g, core, T, topo):
             dma("S", rot[0:128 - 32 * j, c0:c0 + 64], rot[32 * j:128, 64:128], [rn], [rn + "j%d" % j], sem, lat=START + 1.0)
             dma("S", rot[128 - 32 * j:128, c0:c0 + 64], rot[0:32 * j, 64:128], [rn], [rn + "k%d" % j], sem, lat=START + 1.0)
 
-    def keys_of(x, after):
+    def steps_of(x):
         rot, rn = T["rot%d" % x], "rot%d" % x
-        keys = [after] + [rn + jk + str(j) for jk in "jk" for j in range(1, 4)]
-        tt(T.lq[:], rot[:, 64:320].indirect(of[:, O_LQ:O_LQ + 4]), kk[:, K64:K64 + 64], A.add, [rn, "olq", "k5"] + keys, ["lq"], gat(64))
+        keys = [rn + jk + str(j) for jk in "jk" for j in range(1, 4)]
+        act(T.lq[:, 0:64], rot[:, 64:320].indirect(of[:, O_LQ:O_LQ + 4]), FN.Copy, [rn, "olq"] + keys, ["lq"], gat(64))
+        tt(T.df[:, 0:64], T.lq[:, 0:64], T.lq[:, 1:65], A.subtract, ["lq", "lqz"], ["df0"], 128)
+        act(T.df[:, 7:64:8], T.lq[:, 7:64:8], FN.Copy, ["lq"], ["df0"])
+        act(T.df[:, 64:128], T.df[:, 0:64], FN.Copy, ["df0"], ["df1"])
 
-    l1, l2 = cnew(), cnew()
-    tt(T.i3[:, 32:33], col["r1"], col["a"], A.subtract, ["ff"], ["i3x"])
-    ts(T.i3[:, 32:33], T.i3[:, 32:33], 4.0, None, A.add, None, ["i3x"], ["i3x"])
-    ts(T.i3[:, 32:33], T.i3[:, 32:33], 3, None, A.bitwise_and, None, ["i3x"], ["i3x"])
-    af(l1, col["b0"], 32.0, 8.0, ["ff"], ["l1"])
-    af(l2, col["w"], 2.0, l1, ["ff", "l1"], ["l2"])
-    ts(l1, T.i3[:, 32:33], 64.0, l2, A.mult, A.add, ["i3x", "l2"], ["l1"])
-    ts(of[:, O_LQ:O_LQ + 4], kk[:, LQ:LQ + 4], l1, None, A.add, None, ["k9", "l1"], ["olq"])
+    lin("w", (0.125, "q"), (-0.125, "r"), 0.0)
+    lin("l2", (32, "q"), (-64, "q1"), (2, "w"), 8.0)
+    ts(T.w3[:, 0:1], T.i1[:, 31:32], 8.0, col["l2"], A.mult, A.add, ["i1", "l2"], ["l1"])
+    ts(of[:, O_LQ:O_LQ + 4], kk[:, LQ:LQ + 4], T.w3[:, 0:1], None, A.add, None, ["k9", "l1"], ["olq"])
+    ms(T.lq[:, 64:72], 0.0, ["lqz"])
 
     cp(T.a1[:], T.landp[:].indirect(of[:, O_R0:O_R0 + 4]), ["lpo", "lpa", "or0"], ["a1"], gat(64))
     tp(T.gg[:], T.a1[:], ["a1"], ["gg"])
     cand_lists(0)
-    cp(T.p1[:], T.rot0[:, 64:128], ["rot0"], ["p1"])
-    relabel(64, T.rot0[:, 64:128], "rot0", False)
+    relabel(T.rot0[:, 64:128], 64, T.rot0[:, 64:128], "rot0", "rot0", False)
     spread(0)
     dma("S", T.qwc[:].bitcast(dt.uint8), T.wc[:], ["sent", "rot0"], ["qwc"], lat=START + 1.0)
     dma("S", T.qws[:], T.ws[:], ["sent", "rot0"], ["qws"], lat=START + 1.2)
     dma("S", T.vin[:], T.v[:], ["sent", "rot0"], ["vin"], lat=START + 1.7)
 
-    ux, uy, val, nt, q4 = cnew(), cnew(), cnew(), cnew(), cnew()
-    af(ux, col["w"], 16.0, 0.0, ["ff"], ["ux"])
-    af(uy, col["r"], 16.0, 0.0, ["ff"], ["uy"])
-    af(nt, col["top"], -256.0, 256.0, ["ff"], ["nt"])
-    ts(val, col["r"], col["lo"], nt, A.is_gt, A.mult, ["ff", "nt"], ["val"])
+    val = cc[:, 63:64]
+    ts(val, col["r"], col["lo"], None, A.is_gt, None, ["r", "lo"], ["val"])
     qz("qu", 0, 128, T.uin[:], ["uin"], ["qu"])
-    ts(of[:, O_U:O_U + 8], kk[:, UX:UX + 8], ux, None, A.add, None, ["k7", "ux"], ["ou0"])
-    ts(of[:, O_U + 8:O_U + 16], kk[:, UX:UX + 8], 0.0, uy, A.mult, A.add, ["k7", "uy"], ["ou1"])
+    ts(of[:, O_U:O_U + 8], kk[:, UX:UX + 8], lin("ux", (16, "w"), 0.0), None, A.add, None, ["k7", "ux"], ["ou0"])
+    ts(of[:, O_U + 8:O_U + 16], kk[:, UX:UX + 8], 0.0, lin("uy", (16, "r"), 0.0), A.mult, A.add, ["k7", "uy"], ["ou1"])
     pick("qup", 0, "qu", 0, 128, of[:, O_U:O_U + 16], 16, ["qu", "ou0", "ou1"], "qup")
-    ts(T.va[:], T.vv[:], col["r"], val, A.is_equal, A.mult, ["vv", "ff", "val"], ["va"])
-    ts(T.vb[:], T.vv[:], col["lo"], val, A.is_equal, A.mult, ["vv", "ff", "val"], ["vb"])
-    tt(T.cb[:, 0:128], T.va[:], T.vb[:], A.subtract, ["va", "vb"], ["cb0"], 256)
-    for a in range(1, 4):
-        act(T.cb[:, 128 * a:128 * a + 128], T.cb[:, 0:128], FN.Copy, ["cb0"], ["cb%d" % a], 128)
+    ts(T.va[:], T.vv[:], col["r"], None, A.is_equal, None, ["vv", "r"], ["va"])
+    ts(T.vb[:], T.vv[:], col["lo"], None, A.is_equal, None, ["vv", "lo"], ["vb"])
+    tt(T.va[:], T.va[:], T.vb[:], A.subtract, ["va", "vb"], ["va"], 256)
+    for a in range(4):
+        act(T.cb[:, 128 * a:128 * a + 128], T.va[:], FN.Identity, ["va", "val"], ["cb%d" % a], 128, scale=val)
     qz("qc", 0, 128, T.cb[:], ["cb0", "cb1", "cb2", "cb3"], ["qc"])
     ms(T.fl[:, 256:512], 0.0, ["flz"], 128)
-    ms(T.keep[:], 1.0, ["keep"], 128)
-    ms(T.keep[:, 0:128:8], 0.0, ["keep"])
-    bnd = [cnew() for e in range(3)]
-    for e in range(3):
-        af(bnd[e], a2, 256.0, 256.0 * e, ["a2"], ["bnd%d" % e])
-    csub, c0_ = cnew(16), cnew()
-    af(c0_, a2, 1792.0, 1792.0, ["a2"], ["c0_"])
-    af(csub, kk[:, E16:E16 + 16], 1792.0, c0_, ["k6", "c0_"], ["csub"])
-    af(q4, col["q"], 4.0, 0.0, ["ff"], ["q4"])
-    ts(of[:, O_SG:O_SG + 16], kk[:, SG:SG + 16], q4, None, A.add, None, ["k8", "q4"], ["osg"])
+    lin("tg0", (2, "r"), (4, "a"), -14.0)
+    lin("tg1", (1, "tg0"), 2.0)
+    ts(of[:, O_SG:O_SG + 16], kk[:, SG:SG + 16], lin("q4", (4, "q"), 0.0), None, A.add, None, ["k8", "q4"], ["osg"])
+    ts(of[:, O_CP:O_CP + 1], col["k3"], 8.0, lin("cpb", (64, "q"), (-96, "q1"), (-64, "k2"), 7.0), A.mult, A.add, ["k3", "cpb"], ["ocp"])
 
-    r8, q16, t8, q32, b16, opc = cnew(), cnew(8), cnew(), cnew(), cnew(), cnew()
-    af(r8, col["r"], 1.0, 8.0, ["ff"], ["r8"])
-    ts(q16, kk[:, B16:B16 + 8], col["q"], float(136 - 8 * me), A.add, A.add, ["k4", "ff"], ["q16"])
-    af(t8, col["cs"], 8.0, 32.0, ["ff"], ["t8"])
-    af(q32, col["q2"], 32.0, 0.0, ["ff"], ["q32"])
-    rk_, ek_ = [], []
+    lin("r3", (1, "r2"), 1.0)
+    lin("qq0", (2, "q"), float(2 * (72 - 8 * me)))
+    lin("qq1", (1, "qq0"), 1.0)
+    rk_, sk_ = [], []
     for x in range(3):
-        h, h2, o = STRIDE[x], STRIDE[min(x + 1, 2)], 32 + 12 * x
-        hw = cnew()
-        af(hw, col["w"], float(h2 - h), float(h), ["ff"], ["hw%d" % x])
-        af(T.w3[:, o:o + 4], kk[:, EC + 2:EC + 6], 8.0, 0.0, ["k1"], ["ea%d" % x])
-        ts(T.i1[:, o:o + 4], dd[:, 10:14], hw, r8, A.mult, A.add, ["dd", "hw%d" % x, "r8"], ["ra%d" % x])
-        rk_.append("ra%d" % x)
-        ek_.append("ea%d" % x)
-        if x < 2:
-            af(T.w3[:, o + 4:o + 12], kk[:, E8:E8 + 8], 8.0, 0.0, ["k3"], ["ec%d" % x])
-            af(T.w1[:, o + 4:o + 12], dd[:, 16:24], float(h), 0.0, ["dd"], ["rw%d" % x])
-            tt(T.i1[:, o + 4:o + 12], T.w1[:, o + 4:o + 12], q16, A.add, ["rw%d" % x, "q16"], ["rb%d" % x])
-            ts(T.i4[:, x:x + 1], dd[:, 15:16], float(h), t8, A.mult, A.add, ["dd", "t8"], ["sf%d" % x])
-            rk_.append("rb%d" % x)
-            ek_.append("ec%d" % x)
-    ts(T.i4[:, 0:2], T.i4[:, 0:2], 31, None, A.bitwise_and, None, ["sf0", "sf1"], ["sf"])
-    for x in range(2):
-        ts(of[:, O_SF + 2 * x:O_SF + 2 * x + 1], T.i4[:, x:x + 1], q32, None, A.add, None, ["sf", "q32"], ["osf%d" % x])
-    s = slice(32, 60)
-    ts(T.i2[:, s], T.i1[:, s], 3, 7, A.logical_shift_right, A.bitwise_and, rk_, ["j2"])
-    ts(T.i3[:, 0:28], T.i1[:, s], 1, None, A.bitwise_and, None, rk_, ["j3"])
-    ts(T.i4[:, s], T.i1[:, s], 1, 3, A.logical_shift_right, A.bitwise_and, rk_, ["j4"])
-    ts(T.w1[:, s], T.i2[:, s], 16.0, None, A.mult, None, ["j2"], ["v1", "rw0", "rw1"])
-    ts(T.w2[:, s], T.i3[:, 0:28], 4.0, None, A.mult, None, ["j3"], ["v2"])
-    tt(T.w3[:, s], T.w3[:, s], T.i4[:, s], A.add, ek_ + ["j4"], ["v3"])
-    tt(T.w2[:, s], T.w2[:, s], T.w3[:, s], A.add, ["v2", "v3"], ["v2"])
-    tt(T.w1[:, s], T.w1[:, s], T.w2[:, s], A.add, ["v1", "v2"], ["v1"])
-    cp(of[:, O_R:O_R + 28], T.w1[:, s], ["v1"], ["or"])
-    cp(of[:, O_RI:O_RI + 16], T.w2[:, 44:60], ["v2"], ["ori"])
-    ts(T.i3[:, 34:35], col["q1"], 6.0, None, A.add, None, ["ff"], ["i3y"])
-    ts(T.i3[:, 34:35], T.i3[:, 34:35], 7, None, A.bitwise_and, None, ["i3y"], ["i3y"])
-    af(b16, col["b0"], 16.0, 0.0, ["ff"], ["b16"])
-    ts(of[:, O_FB:O_FB + 1], T.i3[:, 34:35], b16, None, A.add, None, ["i3y", "b16"], ["ofb"])
-    af(opc, col["b0"], 4.0, col["r1"], ["ff"], ["opc"])
-    ts(of[:, O_OP:O_OP + 1], col["w"], 8.0, opc, A.mult, A.add, ["ff", "opc"], ["oop"])
+        h, h2 = STRIDE[x], STRIDE[min(x + 1, 2)]
+        lin("hw%d" % x, (2 * (h2 - h), "w"), 2.0 * h)
+        for e in range(2):
+            o = 12 + 4 * x + 2 * e
+            af(T.w3[:, o:o + 2], dd[:, 4 + 2 * e:6 + 2 * e], col["hw%d" % x], col["r%d" % (2 + e)], ["drt", "hw%d" % x, "r%d" % (2 + e)],
+               ["ra%d%d" % (x, e)])
+            rk_.append("ra%d%d" % (x, e))
+            if x < 2:
+                nm, o = "sb%d%d" % (x, e), 24 + 8 * x + e
+                col["dre"] = dd[:, 4 + 2 * e:5 + 2 * e]
+                lastw["dre"] = lastw["drt"]
+                lin(nm, (2 * h, "dre"), "qq%d" % e)
+                af(T.w3[:, o:o + 8 - e:2], kk[:, UX:UX + 4], 1.0, col[nm], ["k7", nm], [nm + "w"])
+                sk_.append(nm + "w")
+    cp(of[:, O_R:O_R + 12], T.w3[:, 12:24], rk_, ["or"])
+    ts(of[:, O_RI:O_RI + 8], T.w3[:, 16:24], -16.0, 15.0, A.add, A.min, rk_, ["ori"])
+    cp(T.i3[:], T.w3[:, 24:40], sk_, ["i3"])
+    ts(T.i3[:], T.i3[:], 127, None, A.bitwise_and, None, ["i3"], ["i3"])
+    cp(of[:, O_S:O_S + 16], T.i3[:], ["i3"], ["os_"])
+    ts(of[:, O_OP:O_OP + 1], col["r"], 2.0, col["w"], A.mult, A.add, ["r", "w"], ["oop"])
     ms(T.po[:, 16:32], 0.0, ["poz"])
     qz("qv", 0, 128, T.vin[:], ["vin"], ["qv"])
 
-    def chunk(c0, n, off, key, name, t0=0):
+    def unpack(bank, src, to, name):
+        for b in range(4):
+            mm(bank + b, 256, "qe", 128 * b, src[0], src[1], True, True, ["qe0%d" % b] + src[2])
+        for b in range(4):
+            act(to[:, 256 * b:256 * b + 256], T["ps%d" % (bank + b)][:, 0:256], FN.Copy, ["ps%d" % (bank + b)], ["%s%d" % (name, b)], 256)
+
+    def chunk(kind, bank, c0, n, off, key, src, fs, fname, pieces):
+        f0 = c0 % 256
+        for b in range(4):
+            mm(bank + b, n, "qe", 128 * b, src[0], src[1] + f0, True, False, ["qe0%d" % b] + src[2])
         for b in range(4):
             out, win = T.yt[:, 4 * c0 + b:4 * (c0 + n):4], T.bt[:, 256 * b:256 * b + 256].indirect(off)
-            if b % 2:
-                cp(out, win, ["bt%d" % b, key], ["yt%s%d" % (nm, b) for nm in name], gat(n))
+            if GATHER[kind][b] == "V":
+                ts(out, win, 0.015625, None, A.mult, None, ["bt%d" % b, key], units("yt", c0, n, [b]), gat(n))
             else:
-                act(out, win, FN.Copy, ["bt%d" % b, key], ["yt%s%d" % (nm, b) for nm in name], gat(n))
-        qz("qy", c0, n, T.yt[:, 4 * c0:4 * (c0 + n)], ["yt%s%d" % (nm, b) for nm in name for b in range(4)], ["qy" + nm for nm in name])
+                act(out, win, FN.Copy, ["bt%d" % b, key], units("yt", c0, n, [b]), gat(n), scale=0.015625)
+        qz("qy", c0, n, T.yt[:, 4 * c0:4 * (c0 + n)], units("yt", c0, n), units("qy", c0, n, [0]))
         for b in range(4):
-            mm(4 + b, n, "qw", 128 * b, "qy", c0, True, True, ["qwc", "qws"] + ["qy" + nm for nm in name])
+            mm(bank + b, n, "qw", 128 * b, "qy", c0, False, True, ["qwc", "qws"] + units("qy", c0, n, [0]))
         for b in range(4):
-            act(T.tmp[:, 256 * b + t0:256 * b + t0 + n], T["ps%d" % (4 + b)][:, 0:n], FN.Relu, ["ps%d" % (4 + b)],
-                ["tmp%d%d" % (b, k) for k in range(t0 // 128, (t0 + n) // 128)], n, scale=0.015625)
+            for t0, x0, m in pieces:
+                tt(T.xt[:, 4 * x0 + b:4 * (x0 + m):4], T["ps%d" % (bank + b)][:, t0:t0 + m],
+                   fs[:, 256 * b + f0 + t0:256 * b + f0 + t0 + m], A.max, ["ps%d" % (bank + b), "%s%d" % (fname, b)], units("xt", x0, m, [b]), m)
 
-    def adds(pieces):
-        for b in range(4):
-            for t0, c0, n, name in pieces:
-                tt(T.xt[:, 4 * c0 + b:4 * (c0 + n):4], T.tmp[:, 256 * b + t0:256 * b + t0 + n], T["ps%d" % b][:, c0:c0 + n], A.add,
-                   ["tmp%d%d" % (b, k) for k in range(t0 // 128, (t0 + n + 127) // 128)] + ["ps%d" % b],
-                   ["xt%s%d" % (nm, b) for nm in name], n)
-
-    def quant(name, k, tile, tn, parts, w):
-        qz(name, 256 * k, 256, tile[:, 1024 * k:1024 * k + 1024], ["%s%s%d" % (tn, nm, b) for nm in parts for b in range(4)], [w])
-
-    def read_list(win, keys, rows, x, last, lkey, out, okey):
+    def read_list(win, keys, rows, x, out, okey):
         cp(T.a1[:], win.indirect(rows), keys, ["a1"], gat(64))
         tp(T.gg[:], T.a1[:], ["a1"], ["gg"])
         cp(T.a2[:], T.gg[:].indirect(of[:, O_C + 10 * x:O_C + 10 * x + 2]), ["gg", "oc"], ["a2_"], gat(32))
         tp(T.uu[:], T.a2[:], ["a2_"], ["uu"])
-        cp(out, T.uu[:].indirect(of[:, last:last + 1]), ["uu", lkey], [okey], gat(16))
+        cp(out, T.uu[:].indirect(of[:, O_FM:O_FM + 1]), ["uu", "ofm"], [okey], gat(16))
 
     for x in range(3):
         rd = x + 1
         qx, nq, pa, land, ln = "qx%d" % rd, "qx%d" % (rd + 1), "pa%d" % rd, T["land%d" % rd], "land%d" % rd
-        own = ("qa", ["qa"]) if x == 0 else (qx, [qx + "o"])
+        own = ("qa", 0, ["qa"]) if x == 0 else (qx, 0, [qx + "o"])
         win = ("ls", 0, ["lsoc", "lsos", "lsac", "lsas"]) if x == 0 else (qx, 256, [qx + "s", qx + "t"])
+        seeds = (qx, 256, [qx + "tc", qx + "ts"]) if x == 0 else win
+        za = 4 if x == 2 else 0
+        zb = 4 - za
         for b in range(4):
-            mm(b, 256, "qe", 128 * b, own[0], 0, True, False, ["qe0"] + own[1])
+            mm(za + b, 256, "qe", 128 * b, own[0], 0, True, False, ["qe0%d" % b] + own[2])
         for e in range(2):
             pick(pa, 256 * e, win[0], win[1], 256, T.ol[:, 16 * e:16 * e + 16], 16, win[2] + ["ol"], pa + str(e))
             for b in range(4):
-                mm(b, 256, "qe", 512 * (e + 1) + 128 * b, pa, 256 * e, False, e == 1, ["qe%d" % (e + 1), pa + str(e) + "c", pa + str(e) + "s"])
+                mm(za + b, 256, "qe", 512 * (e + 1) + 128 * b, pa, 256 * e, False, e == 1,
+                   ["qe%d%d" % (e + 1, b), pa + str(e) + "c", pa + str(e) + "s"])
         for b in range(4):
-            out, src = T.zt[:, b:1024:4], T["ps%d" % b][:, 0:256]
+            out, src = T.zt[:, b:1024:4], T["ps%d" % (za + b)][:, 0:256]
             if b % 2 == 0:
-                act(out, src, FN.Copy, ["ps%d" % b], ["zt0%d" % b], 256, scale=-1.0)
+                act(out, src, FN.Copy, ["ps%d" % (za + b)], ["zt%d" % b], 256, scale=-1.0)
             else:
-                ts(out, src, -1.0, None, A.mult, None, ["ps%d" % b], ["zt0%d" % b], 256)
-        quant("qz", 0, T.zt, "zt", "0", "qz")
-        keys_of(x, "qz")
-        mm(4, 256, "qup", 128, "qz", 0, True, True, ["qupc", "qups", "qz"])
-        mm(5, 256, "qup", 0, "qz", 0, True, True, ["qupc", "qups", "qz"])
+                ts(out, src, -1.0, None, A.mult, None, ["ps%d" % (za + b)], ["zt%d" % b], 256)
+        qz("qz", 0, 256, T.zt[:], ["zt%d" % b for b in range(4)], ["qz"])
+        steps_of(x)
+        p0, p1, p2 = T["ps%d" % zb], T["ps%d" % (zb + 1)], T["ps%d" % (zb + 2)]
+        mm(zb, 256, "qup", 128, "qz", 0, True, True, ["qupc", "qups", "qz"])
+        mm(zb + 1, 256, "qup", 0, "qz", 0, True, True, ["qupc", "qups", "qz"])
         for hf in range(2):
-            act(T.sy[:, 128 * hf:128 * hf + 128], T.ps4[:, 128 * hf:128 * hf + 128], FN.Copy, ["ps4"], ["sy%d" % hf], 128)
+            act(T.sy[:, 128 * hf:128 * hf + 128], p0[:, 128 * hf:128 * hf + 128], FN.Copy, ["ps%d" % zb], ["sy%d" % hf], 128)
         for t in range(4):
-            tt(T.fl[:, t:256:4], T.ps5[:, 64 * t:64 * t + 64], T.sy[:, 64 * t:64 * t + 64], A.is_ge, ["ps5", "sy%d" % (t // 2)], ["fl%d" % t])
+            tt(T.fl[:, t:256:4], p1[:, 64 * t:64 * t + 64], T.sy[:, 64 * t:64 * t + 64], A.is_ge, ["ps%d" % (zb + 1), "sy%d" % (t // 2)], ["fl%d" % t])
         qz("qf", 0, 128, T.fl[:], ["fl0", "fl1", "fl2", "fl3", "flz"], ["qf"])
-        mm(6, 128, "qc", 0, "qf", 0, True, True, ["qc", "qf"])
-        tp(T.rk[:], T.ps6[:, 0:64], ["ps6"], ["rk"])
-        tt(T.key[:], T.rk[:], T.lq[:], A.add, ["rk", "lq"], ["key"], 128)
+        mm(zb + 2, 128, "qc", 0, "qf", 0, True, True, ["qc", "qf"])
         for e in range(2):
-            ts(T.cl[:, 64 * e:64 * e + 64], T.key[:], bnd[e], bnd[e + 1], A.max, A.min, ["key", "bnd0", "bnd1", "bnd2"], ["cl%d" % e])
-        rec("V", lambda: g.vector.tensor_tensor_scan(T.sc[:], T.keep[:], T.cl[:], 0.0, A.mult, A.add), ["keep", "cl0", "cl1"], ["sc"], size(128))
+            ts(T.ns[:, 64 * e:64 * e + 64], p2[:, 0:64], col["tg%d" % e], None, A.not_equal, None, ["ps%d" % (zb + 2), "tg%d" % e], ["ns%d" % e])
+        tp(T.nt[:], T.ns[:], ["ns0", "ns1"], ["nt"])
+        rec("V", lambda: g.vector.tensor_tensor_scan(T.sc[:], T.nt[:], T.df[:], 0.0, A.mult, A.add), ["nt", "df0", "df1"], ["sc"], size(64))
         mine = land[:, 16:32]
-        tt(mine, T.sc[:, 7:128:8], csub, A.subtract, ["sc", "csub"], [ln + "o"])
+        cp(mine, T.sc[:].indirect(of[:, O_CP:O_CP + 1]), ["sc", "ocp"], [ln + "o"], gat(16))
 
         def slot(o, ld=land):
             return ld[:, 16 * ((me - o + 1) % N):16 * ((me - o + 1) % N) + 16]
@@ -473,43 +459,32 @@ def rank_program(g, core, T, topo):
             send(mine, slot, 1, "af%d" % rd, [ln + "o"], ln + "f", before=2)
         if x == 0:
             pick(qx, 256, "ls", 0, 256, of[:, O_SG:O_SG + 16], 16, win[2] + ["osg"], qx + "t")
-        sk = [qx + "tc", qx + "ts"] if x == 0 else [qx + "s", qx + "t"]
-        for b in range(4):
-            mm(b, 512, "qe", 128 * b, qx, 0, True, True, ["qe0", qx + "o", "qz"] + sk)
-        for b in range(4):
-            out, src = T.bt[:, 256 * b:256 * b + 256], T["ps%d" % b][:, 256:512]
-            if b % 2 == 0:
-                act(out, src, FN.Copy, ["ps%d" % b], ["bt%d" % b], 256)
-            else:
-                cp(out, src, ["ps%d" % b], ["bt%d" % b], 256)
-        rows = of[:, O_R + 12 * x:O_R + 12 * x + 4]
+        unpack(za, seeds, T.bt, "bt")
+        unpack(za, own, T.fo, "fo")
+        rows = of[:, O_R + 4 * x:O_R + 4 * x + 4]
         if x == 0:
-            read_list(land[:, 0:48], [ln + "o", ln + "n", "or"], rows, x, O_FM, "ofm", T.om[:], "om")
-            chunk(0, 256, T.om[:], "om", "ei")
-            adds([(0, 0, 256, "abi")])
+            read_list(land[:, 0:48], [ln + "o", ln + "n", "or"], rows, x, T.om[:], "om")
+            chunk("own", zb, 0, 256, T.om[:], "om", own, T.fo, "fo", [(0, 0, 256)])
         else:
-            inner = of[:, O_RI + 12 * (x - 1):O_RI + 12 * (x - 1) + 4]
-            read_list(mine, [ln + "o", "ori"], inner, x, O_FB, "ofb", T.oi[:], "oi")
-            chunk(128, 128, T.oi[:, 8:16], "oi", "i")
-            adds([(0, 64, 128, "i")])
-            read_list(land[:, 0:48], [ln + "o", ln + "n", "or"], rows, x, O_FB, "ofb", T.om[:], "om")
-            chunk(0, 128, T.om[:, 0:8], "om", "e")
-            adds([(0, 192, 64, "a"), (64, 0, 64, "b")])
-        quant(nq, 0, T.xt, "xt", "abi", nq + "o")
+            inner = of[:, O_RI + 4 * (x - 1):O_RI + 4 * (x - 1) + 4]
+            read_list(mine, [ln + "o", "ori"], inner, x, T.oi[:], "oi")
+            chunk("inner", zb, 128, 128, T.oi[:, 8:16], "oi", own, T.fo, "fo", [(0, 128 if x < 2 else 64, 128)])
+            read_list(land[:, 0:48], [ln + "o", ln + "n", "or"], rows, x, T.om[:], "om")
+            chunk("edge", za, 0, 128, T.om[:, 0:8], "om", own, T.fo, "fo", [(0, 0, 128)] if x < 2 else [(0, 192, 64), (64, 0, 64)])
+        qz(nq, 0, 256, T.xt[:, 0:1024], units("xt", 0, 256), [nq + "o"])
         if x < 2:
             cand_lists(rd)
             spread(rd)
-            act(T.s1[:], land[:].indirect(of[:, O_R + 12 * x + 4:O_R + 12 * x + 12]), FN.Copy, [ln + "o", ln + "n", ln + "f", "or"], ["s1"], gat(128))
-            tp(T.s2[:], T.s1[:], ["s1"], ["s2"], 128)
-            cp(T.osd[:], T.s2[:].indirect(of[:, O_SF + 2 * x:O_SF + 2 * x + 1]), ["s2", "osf%d" % x], ["os"], gat(16))
+            act(T.s1[:], land[:].indirect(of[:, O_S + 8 * x:O_S + 8 * x + 8]), FN.Copy, [ln + "o", ln + "n", ln + "f", "os_"], ["s1"], gat(128))
+            tp(T.s2[:], T.s1[:], ["s1"], ["s2"])
+            cp(T.osd[:], T.s2[:].indirect(of[:, O_C + 30 + 2 * x:O_C + 31 + 2 * x]), ["s2", "oc"], ["os"], gat(16))
             for hf in range(2):
-                nm = "st"[hf]
-                chunk(256 + 128 * hf, 128, T.osd[:, 8 * hf:8 * hf + 8], "os", nm, 128 * hf)
-                adds([(128 * hf, 256 + 128 * hf, 128, nm)])
-                qz(nq, 256 + 128 * hf, 128, T.xt[:, 1024 + 512 * hf:1536 + 512 * hf], ["xt%s%d" % (nm, b) for b in range(4)], [nq + nm])
+                nm, c0 = "st"[hf], 256 + 128 * hf
+                chunk(nm, za if (hf + x) % 2 == 0 else zb, c0, 128, T.osd[:, 8 * hf:8 * hf + 8], "os", seeds, T.bt, "bt", [(0, c0, 128)])
+                qz(nq, c0, 128, T.xt[:, 4 * c0:4 * c0 + 512], units("xt", c0, 128), [nq + nm])
         else:
-            cp(T.p1[:, 0:16], mine.indirect(of[:, O_OP:O_OP + 1]), [ln + "o", "oop"], ["p1"])
-            relabel(16, T.po[:, 0:16], "po", True)
+            act(T.pt[:, 0:16], mine.indirect(of[:, O_OP:O_OP + 1]), FN.Copy, [ln + "o", "oop"], ["pt"])
+            relabel(T.pt[:, 0:16], 16, T.po[:, 0:16], "pt", "po", True)
             tp(T.pt[:], T.po[:], ["po", "poz"], ["pt"])
             sem = newsem("d")
             for a in range(4):
@@ -517,9 +492,9 @@ def rank_program(g, core, T, topo):
 
     dma("S", T.oc[:], T.qx4c[:].bitcast(dt.uint8), ["qx4o"], [], lat=START + 1.0)
     for hf in range(2):
-        mm(4 + hf, 128, "qv", 0, "qx4", 128 * hf, True, True, ["qv", "qx4o"])
-    act(T.ysb[:, 0:128], T.ps4[:, 0:128], FN.Copy, ["ps4"], ["y0"], 128)
-    cp(T.ysb[:, 128:256], T.ps5[:, 0:128], ["ps5"], ["y1"], 128)
+        mm(hf, 128, "qv", 0, "qx4", 128 * hf, True, True, ["qv", "qx4o"])
+    act(T.ysb[:, 0:128], T.ps0[:, 0:128], FN.Copy, ["ps0"], ["y0"], 128)
+    cp(T.ysb[:, 128:256], T.ps1[:, 0:128], ["ps1"], ["y1"], 128)
     dma("A", T.y[:], T.ysb[:], ["y0", "y1"], [])
     sem = newsem("d")
     for k in range(4):

@@ -6,14 +6,15 @@ N = 8
 STRIDE = [4, 2, 1]
 DIR = [(-1, 0), (-1, 1), (0, 1), (1, 1), (1, 0), (1, -1), (0, -1), (-1, -1)]
 HAND = {"ac": (4, 3, 5), "asc": (4, 3, 5), "af1": (4,), "af2": (4,)}
-GATHER = {"own": "AVAV", "inner": "AVAV", "edge": "AVAV", "s": "AVAV", "t": "AAAA"}
+GATHER = {"inner0": "AVAV", "inner": "AVAV", "edge0": "AVAV", "edge1": "AVAV", "edge2": "AVAV", "s": "AVAV", "t": "AAAA"}
+TURN = ["AVAV", "AVAV"]
 
 SCRATCH = {}
 for _n, _w, _d in [
     ("xin", 1024, BF), ("uin", 512, BF), ("vin", 512, BF), ("landp", 48, I32),
-    ("land1", 128, BF), ("land2", 128, BF), ("land3", 48, BF),
+    ("land1", 128, BF), ("land2", 128, BF), ("land3", 96, BF),
     ("ez", 520, BF), ("idn", 128, BF), ("vv", 128, BF), ("va", 128, BF), ("vb", 128, BF), ("cb", 512, BF),
-    ("pi", 4, I32), ("fi", 16, I32), ("ff", 16, F32), ("kk", 64, F32), ("cc", 64, F32), ("dd", 32, F32),
+    ("pi", 8, I32), ("fi", 16, I32), ("ff", 16, F32), ("kk", 64, F32), ("cc", 64, F32), ("dd", 32, F32),
     ("w1", 48, F32), ("w2", 48, F32), ("w3", 48, F32), ("i1", 48, I32), ("i2", 16, I32), ("i3", 16, I32),
     ("of", 128, U16),
     ("zt", 1024, BF), ("yt", 2048, BF), ("xt", 2048, BF), ("bt", 1024, BF), ("fo", 1024, BF),
@@ -36,9 +37,10 @@ for _b in range(8):
 SEMAPHORES = (["eV", "eA", "eP", "eG"] + ["d%d" % _i for _i in range(24)] + ["l%d" % _i for _i in range(8)]
               + ["ap", "ac", "asc", "an1", "an2", "an3", "af1", "af2", "hac", "hasc", "haf1", "haf2"])
 
+ORDER = []
 A = AluOpType
 FN = ActivationFunctionType
-CY, PE, WAKE, ROW, START = 0.00085, 0.0006, 0.2, 0.025, 1.2
+CY, PE, WAKE, ROW, START, ISSUE, SLACK = 0.00085, 0.0006, 0.2, 0.025, 1.2, 0.3, 1.0
 
 
 def rank_program(g, core, T, topo):
@@ -81,10 +83,13 @@ def rank_program(g, core, T, topo):
                 g.wait_ge(T.sem["l0"], sent)
         return
     Q = {"V": g.vector, "A": g.scalar, "P": g.tensor, "G": g, "S": g.sync}
-    ops, lastw, readers, totals, used = [], {}, {}, {}, {"d": 0, "l": 0}
+    ops, lastw, readers, totals, used, line = [], {}, {}, {}, {"d": 0, "l": 0}, {"on": None}
 
     def rec(q, fn, r, w, c, tok=None, lat=0.0):
-        op = {"q": q, "fn": fn, "deps": [], "need": False, "tok": tok, "c": c, "lat": lat, "n": len(ops)}
+        op = {"q": q, "fn": fn, "deps": [], "need": False, "tok": tok, "c": c, "lat": lat, "n": len(ops), "after": []}
+        if line["on"]:
+            op["after"] = line.get((line["on"], q), [])
+            line[(line["on"], q)] = [op]
         for k in r:
             op["deps"].append(lastw[k])
             if k.startswith("ps"):
@@ -132,8 +137,8 @@ def rank_program(g, core, T, topo):
             trs.append(RemoteDMATransfer(dst_ids=[dst(c) for c in helpers(me)[:len(handed)]], dma_engine_mask=inside(me),
                                          remote_sem=T.sem["h" + hand], srcs=[src], dsts=[place(o) for o in handed]))
         totals[sem] = ones(m) + (ones(inside(me)) if hand in HAND else 0)
-        op = rec("G", lambda: g.remote_dma_fused(trs, local_sem=T.sem[sem]), r + ["gq"], ["gq"], 0.4, tok=sem,
-                 lat=START + ROW * 128 * (len(to) + before) / ones(m))
+        op = rec("G", lambda: g.remote_dma_fused(trs, local_sem=T.sem[sem]), r + ["gq"], ["gq"], ISSUE, tok=sem,
+                 lat=START - ISSUE + ROW * 128 * (len(to) + before) / ones(m))
         op["deps"], op["after"] = op["deps"][:len(r)], op["deps"][len(r):]
         totals[rsem] = sum(ones(engines(s, which)) for s in group(me)[which])
         lastw[key] = {"q": "R", "tok": rsem, "like": op}
@@ -195,7 +200,7 @@ def rank_program(g, core, T, topo):
     dma("A", T.xin[:, 0:256], T.x[:, 768:1024], [], ["xin1"], lat=START + 0.5)
     dma("S", T.uin[:], T.u[:], ["lpo"], ["uin"], lat=START + 0.5)
 
-    lastw["gq"] = rec("G", lambda: g.iota(T.pi[:], [[2, 4]], 0, 1), [], ["pi"], 0.13)
+    lastw["gq"] = rec("G", lambda: g.iota(T.pi[:], [[2, 8]], 0, 1), [], ["pi"], 0.13)
     EC, UX, SG, LQ = 0, 10, 18, 34
     iota(T.idn[:], [[-1, 128]], 0, 1, ["idn"], 128)
     iota(kk[:, EC:EC + 2], [[1, 2]], 0, 0, ["k0"])
@@ -212,12 +217,12 @@ def rank_program(g, core, T, topo):
     send(T.landp[:, 16:32], lambda o: T.landp[:, 32:48] if o == prv else T.landp[:, 0:16], 0, "ap", ["lpo"], "lpa", before=4)
 
     fields = {"q": (0, 0, 15), "r": (0, 0, 7), "ch": (0, 4, 1), "r6": (3, 0, 7), "a": (0, 5, 3), "q1": (0, 1, 7), "k2": (0, 2, 3),
-              "lo": (0, 3, 7), "k3": (2, 2, 3)}
+              "lo": (0, 3, 7), "k3": (2, 2, 3), "k4": (1, 1, 3), "r7": (6, 1, 7)}
     col = {}
     for i, (nm, (j, sh, an)) in enumerate(fields.items()):
         ts(T.fi[:, i:i + 1], T.pi[:, j:j + 1], sh, an, A.logical_shift_right, A.bitwise_and, ["pi"], ["fi%d" % i])
         col[nm] = ff[:, i:i + 1]
-    cp(ff[:, 0:9], T.fi[:, 0:9], ["fi%d" % i for i in range(9)], list(fields))
+    cp(ff[:, 0:11], T.fi[:, 0:11], ["fi%d" % i for i in range(11)], list(fields))
     taken = [0]
 
     def lin(name, *terms):
@@ -234,7 +239,7 @@ def rank_program(g, core, T, topo):
             rest, keys = out, [name]
         return out
 
-    O_SP, O_R0, O_C, O_FM, O_CP, O_OP, O_LQ, O_U, O_SG, O_R, O_RI, O_S = 0, 2, 6, 40, 44, 46, 48, 52, 68, 84, 96, 104
+    O_SP, O_R0, O_C, O_FM, O_CP, O_OP, O_LQ, O_U, O_SG, O_R, O_RI, O_CQ, O_L, O_S = 0, 2, 6, 40, 44, 46, 48, 52, 68, 84, 92, 96, 100, 104
     ts(of[:, O_SP:O_SP + 1], col["q"], 8.0, 64.0, A.mult, A.add, ["q"], ["osp0"])
     ts(of[:, O_SP + 1:O_SP + 2], col["r"], 32.0, lin("sp", (-24, "q"), 192.0), A.mult, A.add, ["r", "sp"], ["osp1"])
 
@@ -357,27 +362,34 @@ def rank_program(g, core, T, topo):
     lin("qq0", (2, "q"), float(2 * (72 - 8 * me)))
     lin("qq1", (1, "qq0"), 1.0)
     rk_, sk_ = [], []
-    for x in range(3):
-        h, h2 = STRIDE[x], STRIDE[min(x + 1, 2)]
+    for x in range(2):
+        h, h2 = STRIDE[x], STRIDE[x + 1]
         lin("hw%d" % x, (2 * (h2 - h), "w"), 2.0 * h)
         for e in range(2):
             o = 12 + 4 * x + 2 * e
             af(T.w3[:, o:o + 2], dd[:, 4 + 2 * e:6 + 2 * e], col["hw%d" % x], col["r%d" % (2 + e)], ["drt", "hw%d" % x, "r%d" % (2 + e)],
                ["ra%d%d" % (x, e)])
             rk_.append("ra%d%d" % (x, e))
-            if x < 2:
-                nm, o = "sb%d%d" % (x, e), 24 + 8 * x + e
-                col["dre"] = dd[:, 4 + 2 * e:5 + 2 * e]
-                lastw["dre"] = lastw["drt"]
-                lin(nm, (2 * h, "dre"), "qq%d" % e)
-                af(T.w3[:, o:o + 8 - e:2], kk[:, UX:UX + 4], 1.0, col[nm], ["k7", nm], [nm + "w"])
-                sk_.append(nm + "w")
-    cp(of[:, O_R:O_R + 12], T.w3[:, 12:24], rk_, ["or"])
-    ts(of[:, O_RI:O_RI + 8], T.w3[:, 16:24], -16.0, 15.0, A.add, A.min, rk_, ["ori"])
+            nm, o = "sb%d%d" % (x, e), 24 + 8 * x + e
+            col["dre"] = dd[:, 4 + 2 * e:5 + 2 * e]
+            lastw["dre"] = lastw["drt"]
+            lin(nm, (2 * h, "dre"), "qq%d" % e)
+            af(T.w3[:, o:o + 8 - e:2], kk[:, UX:UX + 4], 1.0, col[nm], ["k7", nm], [nm + "w"])
+            sk_.append(nm + "w")
+    cp(of[:, O_R:O_R + 8], T.w3[:, 12:20], rk_, ["or"])
+    ts(of[:, O_RI:O_RI + 4], T.w3[:, 16:20], -16.0, 15.0, A.add, A.min, rk_, ["ori"])
     cp(T.i3[:], T.w3[:, 24:40], sk_, ["i3"])
     ts(T.i3[:], T.i3[:], 127, None, A.bitwise_and, None, ["i3"], ["i3"])
     cp(of[:, O_S:O_S + 16], T.i3[:], ["i3"], ["os_"])
-    ts(of[:, O_OP:O_OP + 1], col["r"], 2.0, col["w"], A.mult, A.add, ["r", "w"], ["oop"])
+    lin("cq", (32, "q"), (-64, "q1"), (8, "k4"), 7.0)
+    ts(of[:, O_CQ:O_CQ + 4], kk[:, EC + 2:EC + 6], 64.0, col["cq"], A.mult, A.add, ["k1", "cq"], ["ocq"])
+    ts(of[:, O_OP:O_OP + 1], col["w"], 64.0, col["cq"], A.mult, A.add, ["w", "cq"], ["oop"])
+    lin("row", (STRIDE[2], "rg"), "r7")
+    lin("b16", (16, "q"), (-32, "q1"), 0.0)
+    lin("lx", (25, "row"), (1, "b16"), 32.0)
+    ts(T.w3[:, 20:21], col["row"], 0.0, 7.0, A.max, A.min, ["row"], ["in7"])
+    ts(of[:, O_L:O_L + 1], T.w3[:, 20:21], -24.0, col["lx"], A.mult, A.add, ["in7", "lx"], ["oll"])
+    ts(of[:, O_L + 2:O_L + 3], T.w3[:, 20:21], col["b16"], None, A.add, None, ["in7", "b16"], ["oli"])
     ms(T.po[:, 16:32], 0.0, ["poz"])
     qz("qv", 0, 128, T.vin[:], ["vin"], ["qv"])
 
@@ -405,74 +417,89 @@ def rank_program(g, core, T, topo):
                 tt(T.xt[:, 4 * x0 + b:4 * (x0 + m):4], T["ps%d" % (bank + b)][:, t0:t0 + m],
                    fs[:, 256 * b + f0 + t0:256 * b + f0 + t0 + m], A.max, ["ps%d" % (bank + b), "%s%d" % (fname, b)], units("xt", x0, m, [b]), m)
 
-    def read_list(win, keys, rows, x, out, okey):
+    def shift_columns(win, keys, rows, x, out, okey):
         cp(T.a1[:], win.indirect(rows), keys, ["a1"], gat(64))
         tp(T.gg[:], T.a1[:], ["a1"], ["gg"])
         cp(T.a2[:], T.gg[:].indirect(of[:, O_C + 10 * x:O_C + 10 * x + 2]), ["gg", "oc"], ["a2_"], gat(32))
-        tp(T.uu[:], T.a2[:], ["a2_"], ["uu"])
+        tp(out, T.a2[:], ["a2_"], [okey])
+
+    def read_list(win, keys, rows, x, out, okey):
+        shift_columns(win, keys, rows, x, T.uu[:], "uu")
         cp(out, T.uu[:].indirect(of[:, O_FM:O_FM + 1]), ["uu", "ofm"], [okey], gat(16))
 
     for x in range(3):
         rd = x + 1
         qx, nq, pa, land, ln = "qx%d" % rd, "qx%d" % (rd + 1), "pa%d" % rd, T["land%d" % rd], "land%d" % rd
-        own = ("qa", 0, ["qa"]) if x == 0 else (qx, 0, [qx + "o"])
+        half = [("qa", 0, ["qa"])] * 2 if x == 0 else [(qx, 0, [qx + "e"]), (qx, 0, [qx + "i"])]
+        own = (half[0][0], 0, half[0][2] + half[1][2])
         win = ("ls", 0, ["lsoc", "lsos", "lsac", "lsas"]) if x == 0 else (qx, 256, [qx + "s", qx + "t"])
         seeds = (qx, 256, [qx + "tc", qx + "ts"]) if x == 0 else win
-        za = 4 if x == 2 else 0
-        zb = 4 - za
-        for b in range(4):
-            mm(za + b, 256, "qe", 128 * b, own[0], 0, True, False, ["qe0%d" % b] + own[2])
-        for e in range(2):
-            pick(pa, 256 * e, win[0], win[1], 256, T.ol[:, 16 * e:16 * e + 16], 16, win[2] + ["ol"], pa + str(e))
-            for b in range(4):
-                mm(za + b, 256, "qe", 512 * (e + 1) + 128 * b, pa, 256 * e, False, e == 1,
-                   ["qe%d%d" % (e + 1, b), pa + str(e) + "c", pa + str(e) + "s"])
-        for b in range(4):
-            out, src = T.zt[:, b:1024:4], T["ps%d" % (za + b)][:, 0:256]
-            if b % 2 == 0:
-                act(out, src, FN.Copy, ["ps%d" % (za + b)], ["zt%d" % b], 256, scale=-1.0)
-            else:
-                ts(out, src, -1.0, None, A.mult, None, ["ps%d" % (za + b)], ["zt%d" % b], 256)
-        qz("qz", 0, 256, T.zt[:], ["zt%d" % b for b in range(4)], ["qz"])
-        steps_of(x)
-        p0, p1, p2 = T["ps%d" % zb], T["ps%d" % (zb + 1)], T["ps%d" % (zb + 2)]
-        mm(zb, 256, "qup", 128, "qz", 0, True, True, ["qupc", "qups", "qz"])
-        mm(zb + 1, 256, "qup", 0, "qz", 0, True, True, ["qupc", "qups", "qz"])
         for hf in range(2):
-            act(T.sy[:, 128 * hf:128 * hf + 128], p0[:, 128 * hf:128 * hf + 128], FN.Copy, ["ps%d" % zb], ["sy%d" % hf], 128)
-        for t in range(4):
-            tt(T.fl[:, t:256:4], p1[:, 64 * t:64 * t + 64], T.sy[:, 64 * t:64 * t + 64], A.is_ge, ["ps%d" % (zb + 1), "sy%d" % (t // 2)], ["fl%d" % t])
+            for b in range(4):
+                mm(4 * hf + b, 128, "qe", 128 * b, own[0], 128 * hf, True, False, ["qe0%d" % b] + half[hf][2])
+        line["on"] = pa
+        for hf in range(2):
+            for e in range(2):
+                c0, nm = 256 * hf + 128 * e, pa + str(2 * hf + e)
+                pick(pa, c0, win[0], win[1], 256, T.ol[:, 16 * e + 8 * hf:16 * e + 8 * hf + 8], 8, win[2] + ["ol"], nm)
+                for b in range(4):
+                    mm(4 * hf + b, 128, "qe", 512 * (e + 1) + 128 * b, pa, c0, False, e == 1, ["qe%d%d" % (e + 1, b), nm + "c", nm + "s"])
+        line["on"] = None
+        for hf in range(2):
+            for b in range(4):
+                out, src, bank = T.zt[:, 512 * hf + b:512 * hf + 512:4], T["ps%d" % (4 * hf + b)][:, 0:128], "ps%d" % (4 * hf + b)
+                if TURN[hf][b] == "A":
+                    act(out, src, FN.Copy, [bank], ["zt%d%d" % (hf, b)], 128, scale=-1.0)
+                else:
+                    ts(out, src, -1.0, None, A.mult, None, [bank], ["zt%d%d" % (hf, b)], 128)
+            qz("qz", 128 * hf, 128, T.zt[:, 512 * hf:512 * hf + 512], ["zt%d%d" % (hf, b) for b in range(4)], ["qz%d" % hf])
+        steps_of(x)
+        for hf in range(2):
+            mm(2 * hf, 128, "qup", 128, "qz", 128 * hf, True, True, ["qupc", "qups", "qz%d" % hf])
+            mm(2 * hf + 1, 128, "qup", 0, "qz", 128 * hf, True, True, ["qupc", "qups", "qz%d" % hf])
+            act(T.sy[:, 128 * hf:128 * hf + 128], T["ps%d" % (2 * hf)][:, 0:128], FN.Copy, ["ps%d" % (2 * hf)], ["sy%d" % hf], 128)
+            for t in (2 * hf, 2 * hf + 1):
+                tt(T.fl[:, t:256:4], T["ps%d" % (2 * hf + 1)][:, 64 * (t % 2):64 * (t % 2) + 64], T.sy[:, 64 * t:64 * t + 64], A.is_ge,
+                   ["ps%d" % (2 * hf + 1), "sy%d" % hf], ["fl%d" % t])
         qz("qf", 0, 128, T.fl[:], ["fl0", "fl1", "fl2", "fl3", "flz"], ["qf"])
-        mm(zb + 2, 128, "qc", 0, "qf", 0, True, True, ["qc", "qf"])
+        mm(0, 128, "qc", 0, "qf", 0, True, True, ["qc", "qf"])
         for e in range(2):
-            ts(T.ns[:, 64 * e:64 * e + 64], p2[:, 0:64], col["tg%d" % e], None, A.not_equal, None, ["ps%d" % (zb + 2), "tg%d" % e], ["ns%d" % e])
+            ts(T.ns[:, 64 * e:64 * e + 64], T.ps0[:, 0:64], col["tg%d" % e], None, A.not_equal, None, ["ps0", "tg%d" % e], ["ns%d" % e])
         tp(T.nt[:], T.ns[:], ["ns0", "ns1"], ["nt"])
         rec("V", lambda: g.vector.tensor_tensor_scan(T.sc[:], T.nt[:], T.df[:], 0.0, A.mult, A.add), ["nt", "df0", "df1"], ["sc"], size(64))
-        mine = land[:, 16:32]
-        cp(mine, T.sc[:].indirect(of[:, O_CP:O_CP + 1]), ["sc", "ocp"], [ln + "o"], gat(16))
+        wide = 16 if x < 2 else 32
+        mine = land[:, wide:2 * wide]
 
-        def slot(o, ld=land):
-            return ld[:, 16 * ((me - o + 1) % N):16 * ((me - o + 1) % N) + 16]
+        def slot(o, ld=land, n=wide):
+            return ld[:, n * ((me - o + 1) % N):n * ((me - o + 1) % N) + n]
 
+        if x < 2:
+            cp(mine, T.sc[:].indirect(of[:, O_CP:O_CP + 1]), ["sc", "ocp"], [ln + "o"], gat(16))
+        else:
+            shift_columns(T.sc[:], ["sc", "ocq"], of[:, O_CQ:O_CQ + 4], x, mine, ln + "o")
         send(mine, slot, 0, "an%d" % rd, [ln + "o"], ln + "n", hand="af%d" % rd)
         if x < 2:
             send(mine, slot, 1, "af%d" % rd, [ln + "o"], ln + "f", before=2)
         if x == 0:
             pick(qx, 256, "ls", 0, 256, of[:, O_SG:O_SG + 16], 16, win[2] + ["osg"], qx + "t")
-        unpack(za, seeds, T.bt, "bt")
-        unpack(za, own, T.fo, "fo")
-        rows = of[:, O_R + 4 * x:O_R + 4 * x + 4]
-        if x == 0:
-            read_list(land[:, 0:48], [ln + "o", ln + "n", "or"], rows, x, T.om[:], "om")
-            chunk("own", zb, 0, 256, T.om[:], "om", own, T.fo, "fo", [(0, 0, 256)])
-        else:
-            inner = of[:, O_RI + 4 * (x - 1):O_RI + 4 * (x - 1) + 4]
-            read_list(mine, [ln + "o", "ori"], inner, x, T.oi[:], "oi")
-            chunk("inner", zb, 128, 128, T.oi[:, 8:16], "oi", own, T.fo, "fo", [(0, 128 if x < 2 else 64, 128)])
-            read_list(land[:, 0:48], [ln + "o", ln + "n", "or"], rows, x, T.om[:], "om")
-            chunk("edge", za, 0, 128, T.om[:, 0:8], "om", own, T.fo, "fo", [(0, 0, 128)] if x < 2 else [(0, 192, 64), (64, 0, 64)])
-        qz(nq, 0, 256, T.xt[:, 0:1024], units("xt", 0, 256), [nq + "o"])
+        unpack(4, seeds, T.bt, "bt")
+        unpack(4, own, T.fo, "fo")
+        if x == 1:
+            read_list(mine, [ln + "o", "ori"], of[:, O_RI:O_RI + 4], x, T.oi[:], "oi")
+        if x == 2:
+            cp(T.oi[:], mine.indirect(of[:, O_L + 2:O_L + 3]), [ln + "o", "oli"], ["oi"], gat(16))
+        if x > 0:
+            chunk("inner", 0, 128, 128, T.oi[:, 8:16], "oi", half[1], T.fo, "fo", [(0, 128 if x < 2 else 64, 128)])
         if x < 2:
+            read_list(land[:, 0:48], [ln + "o", ln + "n", "or"], of[:, O_R + 4 * x:O_R + 4 * x + 4], x, T.om[:], "om")
+        else:
+            cp(T.om[:], land[:].indirect(of[:, O_L:O_L + 1]), [ln + "o", ln + "n", "oll"], ["om"], gat(16))
+        if x == 0:
+            chunk("inner0", 0, 128, 128, T.om[:, 8:16], "om", half[1], T.fo, "fo", [(0, 128, 128)])
+        chunk("edge%d" % x, 4, 0, 128, T.om[:, 0:8], "om", half[0], T.fo, "fo", [(0, 0, 128)] if x < 2 else [(0, 192, 64), (64, 0, 64)])
+        if x < 2:
+            for hf in range(2):
+                qz(nq, 128 * hf, 128, T.xt[:, 512 * hf:512 * hf + 512], units("xt", 128 * hf, 128), [nq + "ei"[hf]])
             cand_lists(rd)
             spread(rd)
             act(T.s1[:], land[:].indirect(of[:, O_S + 8 * x:O_S + 8 * x + 8]), FN.Copy, [ln + "o", ln + "n", ln + "f", "os_"], ["s1"], gat(128))
@@ -480,10 +507,11 @@ def rank_program(g, core, T, topo):
             cp(T.osd[:], T.s2[:].indirect(of[:, O_C + 30 + 2 * x:O_C + 31 + 2 * x]), ["s2", "oc"], ["os"], gat(16))
             for hf in range(2):
                 nm, c0 = "st"[hf], 256 + 128 * hf
-                chunk(nm, za if (hf + x) % 2 == 0 else zb, c0, 128, T.osd[:, 8 * hf:8 * hf + 8], "os", seeds, T.bt, "bt", [(0, c0, 128)])
+                chunk(nm, 4 * hf, c0, 128, T.osd[:, 8 * hf:8 * hf + 8], "os", seeds, T.bt, "bt", [(0, c0, 128)])
                 qz(nq, c0, 128, T.xt[:, 4 * c0:4 * c0 + 512], units("xt", c0, 128), [nq + nm])
         else:
-            act(T.pt[:, 0:16], mine.indirect(of[:, O_OP:O_OP + 1]), FN.Copy, [ln + "o", "oop"], ["pt"])
+            qz(nq, 0, 256, T.xt[:, 0:1024], units("xt", 0, 256), [nq + "o"])
+            act(T.pt[:, 0:16], T.sc[:].indirect(of[:, O_OP:O_OP + 1]), FN.Copy, ["sc", "oop"], ["pt"])
             relabel(T.pt[:, 0:16], 16, T.po[:, 0:16], "pt", "po", True)
             tp(T.pt[:], T.po[:], ["po", "poz"], ["pt"])
             sem = newsem("d")
@@ -508,27 +536,33 @@ def rank_program(g, core, T, topo):
         for o in op["pre"]:
             o["way"] = max(o["way"], op["way"] + WAKE)
             o["users"].append(op)
-    free, order, pool = {q: 0.0 for q in Q}, [], [op for op in ops if not op["left"]]
-    while pool:
+    free, order, pool, rest = {q: 0.0 for q in Q}, [], [op for op in ops if not op["left"]], list(ops)
+
+    def gap(a, o):
+        return 0.0 if any(a is z for z in o.get("after", [])) or (o["q"] == "P" and a["q"] == "P") else a["lat"] + WAKE
+
+    for op in ops:
+        op["in"] = [(a, a["c"] + gap(a, op)) for a in op["pre"]]
+    while pool and len(ORDER) < len(ops):
+        bound = 0.0
+        for o in rest:
+            o["est"] = max([free[o["q"]]] + [a["est"] + d for a, d in o["in"]])
+            bound = max(bound, o["est"] + o["way"])
         best = None
-        for q in Q:
-            mine_ = sorted((o for o in pool if o["q"] == q), key=lambda o: (-o["way"], o["n"]))
-            limit = 1e9
-            for o in mine_:
-                st = max(free[q], o["ready"])
-                if st + o["c"] <= limit + 0.03 and (best is None or st < best[0] - 1e-9):
-                    best = (st, o)
-                limit = min(limit, st)
-        st, op = best
-        pool = [o for o in pool if o is not op]
-        order.append(op)
-        free[op["q"]] = st + op["c"]
-        for o in op["users"]:
-            issued = any(op is a for a in o.get("after", [])) or (o["q"] == "P" and op["q"] == "P")
-            o["ready"] = max(o["ready"], st + op["c"] + (0.0 if issued else op["lat"] + WAKE))
+        for o in pool:
+            end = o["est"] + o["c"]
+            if (best is None or (o["est"], -o["way"]) < (best["est"], -best["way"])) and not any(
+                    z["q"] == o["q"] and z["way"] > o["way"] and z["est"] < end - 0.03 and end + z["way"] > bound - SLACK for z in rest):
+                best = o
+        pool = [o for o in pool if o is not best]
+        rest = [o for o in rest if o is not best]
+        ORDER.append(best["n"])
+        free[best["q"]] = best["est"] + best["c"]
+        for o in best["users"]:
             o["left"] -= 1
             if not o["left"]:
                 pool.append(o)
+    order = [ops[n] for n in ORDER]
 
     for op in ops:
         op["deps"] = [o for o in op["deps"] if not (op["q"] == "P" and o["q"] == "P")]

@@ -5,21 +5,22 @@ F32, BF, I32, U16, U8, CODE = "float32", "bfloat16", "int32", "uint16", "uint8",
 N = 8
 STRIDE = [4, 2, 1]
 DIR = [(-1, 0), (-1, 1), (0, 1), (1, 1), (1, 0), (1, -1), (0, -1), (-1, -1)]
-HAND = {"ac": (4, 3, 5), "asc": (4, 3, 5), "af1": (4,), "af2": (4,)}
-GATHER = {"inner0": "AVAV", "inner": "AVAV", "edge0": "AVAV", "edge1": "AVAV", "edge2": "AVAV", "s": "AVAV", "t": "AAAA"}
-TURN = ["AVAV", "AVAV"]
+HAND = {"ac": [(0, (4, 2)), (1, (3,)), (2, (5,))], "asc": [(0, (4,)), (1, (3,))], "af1": [(0, (4,))], "af2": [(0, (4,))]}
+ACROSS = (False, True, False)
+GATHER = {"own": "AVAV", "inner1": "AAAV", "inner2": "AVAV", "edge1": "AAAV", "edge2": "AVAV", "s0": "AVAV", "t0": "AAAA", "s1": "AVAV", "t1": "AAAA"}
+TURN = ["VVVV", "AVAV"]
 
 SCRATCH = {}
 for _n, _w, _d in [
     ("xin", 1024, BF), ("uin", 512, BF), ("vin", 512, BF), ("landp", 48, I32),
     ("land1", 128, BF), ("land2", 128, BF), ("land3", 96, BF),
     ("ez", 520, BF), ("idn", 128, BF), ("vv", 128, BF), ("va", 128, BF), ("vb", 128, BF), ("cb", 512, BF),
-    ("pi", 8, I32), ("fi", 16, I32), ("ff", 16, F32), ("kk", 64, F32), ("cc", 64, F32), ("dd", 32, F32),
+    ("pi", 16, I32), ("fi", 24, I32), ("ff", 24, F32), ("kk", 96, F32), ("cc", 64, F32), ("dd", 32, F32),
     ("w1", 48, F32), ("w2", 48, F32), ("w3", 48, F32), ("i1", 48, I32), ("i2", 16, I32), ("i3", 16, I32),
     ("of", 128, U16),
     ("zt", 1024, BF), ("yt", 2048, BF), ("xt", 2048, BF), ("bt", 1024, BF), ("fo", 1024, BF),
     ("sy", 256, F32), ("fl", 512, BF), ("ns", 128, BF), ("nt", 128, BF), ("sc", 128, BF),
-    ("lq", 72, BF), ("df", 128, BF), ("a1", 64, BF), ("gg", 64, BF), ("a2", 32, BF), ("uu", 32, BF), ("a3", 128, BF),
+    ("lq", 72, BF), ("df", 128, BF), ("a1", 64, BF), ("gg", 64, BF), ("a2", 32, BF), ("uu", 32, BF), ("a3", 64, BF),
     ("s1", 128, BF), ("s2", 128, BF), ("rot0", 320, BF), ("rot1", 320, BF), ("rot2", 320, BF),
     ("om", 16, U16), ("oi", 16, U16), ("osd", 16, U16), ("ol", 32, U16),
     ("p1", 64, F32), ("p2", 64, F32), ("p3", 64, F32), ("po", 32, F32), ("pt", 32, F32),
@@ -38,9 +39,13 @@ SEMAPHORES = (["eV", "eA", "eP", "eG"] + ["d%d" % _i for _i in range(24)] + ["l%
               + ["ap", "ac", "asc", "an1", "an2", "an3", "af1", "af2", "hac", "hasc", "haf1", "haf2"])
 
 ORDER = []
+MARGIN, TURNS, ROOM = 0.1, 4, {"V": 0.0, "A": 0.0, "P": 0.2, "G": 0.0, "S": 0.0}
+FARB, FIRSTB, PB = 1, 7, 7
+CASES = [(1.0, 1.0, 1.0, 1.0, 0.22, 1.0), (1.3, 1.4, 1.4, 1.3, 0.22, 1.3)]
+AHEAD = {"s1": 1.0, "s2": 1.0, "os": 1.0, "yt08": 0.8, "qy08": 0.3, "qy12": 0.3, "yt04/2": 0.4, "qx3e/2": 0.4, "lpo": 2.0}
 A = AluOpType
 FN = ActivationFunctionType
-CY, PE, WAKE, ROW, START, ISSUE, SLACK = 0.00085, 0.0006, 0.2, 0.025, 1.2, 0.3, 1.0
+CY, PE, WAKE, ROW, START, ISSUE, SLACK = 0.00085, 0.0005, 0.22, 0.018, 0.9, 0.3, 1.0
 
 
 def rank_program(g, core, T, topo):
@@ -48,10 +53,18 @@ def rank_program(g, core, T, topo):
 
     def helpers(k):
         out = []
-        for j in range(max(len(v) for v in HAND.values())):
-            out.append([c for c in reversed(topo.cores_of(T.cores[k])) if T.rank_of(c) is None and c not in out
-                        and all(topo.may_write(c, T.cores[(k + v[j]) % N]) for v in HAND.values() if j < len(v))][0])
+        for j, across in enumerate(ACROSS):
+            serves = [T.cores[(k + d) % N] for v in HAND.values() for i, ds in v if i == j for d in ds]
+            out.append([c for c in topo.cores_of(T.cores[k]) if T.rank_of(c) is None and c not in out
+                        and (topo.die(c) != topo.die(T.cores[k])) == across and all(topo.may_write(c, o) for o in serves)][0])
         return out
+
+    def handed_ap(nm, k, d):
+        if nm == "ac":
+            return T.lsc[:, 32 * k:32 * k + 32].bitcast(dt.uint8)
+        if nm == "asc":
+            return T.lss[:, 32 * k:32 * k + 32]
+        return {"af1": T.land1, "af2": T.land2}[nm][:, 16 * ((1 - d) % N):16 * ((1 - d) % N) + 16]
 
     def dst(c):
         return DstId(rid=topo.addr(c)[0], pnc=topo.addr(c)[1])
@@ -66,27 +79,22 @@ def rank_program(g, core, T, topo):
         for k in range(N):
             if core in helpers(k):
                 j, sent = helpers(k).index(core), 0
-                for nm in [x for x in HAND if j < len(HAND[x])]:
-                    d = HAND[nm][j]
-                    to = T.cores[(k + d) % N]
-                    m, sl = topo.mask(core, to), 16 * ((1 - d) % N)
-                    if nm == "ac":
-                        ap = T.lsc[:, 32 * k:32 * k + 32].bitcast(dt.uint8)
-                    elif nm == "asc":
-                        ap = T.lss[:, 32 * k:32 * k + 32]
-                    else:
-                        ap = {"af1": T.land1, "af2": T.land2}[nm][:, sl:sl + 16]
+                for nm, ds in [(x, ds) for x in HAND for i, ds in HAND[x] if i == j]:
+                    to = [T.cores[(k + d) % N] for d in ds]
+                    m = topo.mask(core, to[0])
                     sent += ones(m)
                     g.wait_ge(T.sem["h" + nm], ones(inside(k)))
-                    g.remote_dma_fused([RemoteDMATransfer(dst_ids=[dst(to)], dma_engine_mask=m, remote_sem=T.sem[nm], srcs=[ap], dsts=[ap])],
+                    g.remote_dma_fused([RemoteDMATransfer(dst_ids=[dst(c) for c in to], dma_engine_mask=m, remote_sem=T.sem[nm],
+                                                          srcs=[handed_ap(nm, k, 0)], dsts=[handed_ap(nm, k, d) for d in ds])],
                                        local_sem=T.sem["l0"])
                 g.wait_ge(T.sem["l0"], sent)
         return
     Q = {"V": g.vector, "A": g.scalar, "P": g.tensor, "G": g, "S": g.sync}
-    ops, lastw, readers, totals, used, line = [], {}, {}, {}, {"d": 0, "l": 0}, {"on": None}
+    ops, lastw, readers, totals, used, line = [], {}, {}, {}, {"d": 0, "l": 0}, {"on": None, "rd": "/0"}
 
     def rec(q, fn, r, w, c, tok=None, lat=0.0):
-        op = {"q": q, "fn": fn, "deps": [], "need": False, "tok": tok, "c": c, "lat": lat, "n": len(ops), "after": []}
+        op = {"q": q, "fn": fn, "deps": [], "need": False, "tok": tok, "c": c, "lat": lat, "n": len(ops), "after": [], "gather": line.pop("gather", False),
+              "ahead": sum([AHEAD.get(k[:4] + line["rd"], AHEAD.get(k[:4], 0.0) + AHEAD.get(line["rd"], 0.0)) for k in w[:1]])}
         if line["on"]:
             op["after"] = line.get((line["on"], q), [])
             line[(line["on"], q)] = [op]
@@ -127,15 +135,15 @@ def rank_program(g, core, T, topo):
 
     def send(src, place, which, rsem, r, key, before=0, hand=None):
         to, m = group(me)[which], engines(me, which)
-        handed = [(me + d) % N for d in HAND.get(hand or rsem, ())]
+        handed = [(me + d) % N for i, ds in HAND.get(hand or rsem, ()) for d in ds]
         if rsem in HAND:
             to = [o for o in to if o not in handed]
         sem = newsem("l")
         trs = [RemoteDMATransfer(dst_ids=[dst(T.cores[o]) for o in to], dma_engine_mask=m, remote_sem=T.sem[rsem], srcs=[src],
                                  dsts=[place(o) for o in to])]
         if hand in HAND:
-            trs.append(RemoteDMATransfer(dst_ids=[dst(c) for c in helpers(me)[:len(handed)]], dma_engine_mask=inside(me),
-                                         remote_sem=T.sem["h" + hand], srcs=[src], dsts=[place(o) for o in handed]))
+            trs.append(RemoteDMATransfer(dst_ids=[dst(helpers(me)[i]) for i, ds in HAND[hand]], dma_engine_mask=inside(me),
+                                         remote_sem=T.sem["h" + hand], srcs=[src], dsts=[handed_ap(hand, me, 0) for i in HAND[hand]]))
         totals[sem] = ones(m) + (ones(inside(me)) if hand in HAND else 0)
         op = rec("G", lambda: g.remote_dma_fused(trs, local_sem=T.sem[sem]), r + ["gq"], ["gq"], ISSUE, tok=sem,
                  lat=START - ISSUE + ROW * 128 * (len(to) + before) / ones(m))
@@ -182,6 +190,7 @@ def rank_program(g, core, T, topo):
                    r, ["ps%d" % bank], (n + 16) * PE)
 
     def gat(n):
+        line["gather"] = True
         return int(65 + 1.5 * n)
 
     def pick(dn, da, sn, sa, sw, off, k, r, w):
@@ -190,39 +199,46 @@ def rank_program(g, core, T, topo):
         act(T[dn + "s"][:, da:da + n], T[sn + "s"][:, sa:sa + sw].indirect(off), FN.Copy, r, [w + "s"], gat(n))
 
     def units(name, c0, n, bs=range(4)):
-        return ["%s%d_%d" % (name, k, b) for k in range(c0 // 64, (c0 + n) // 64) for b in bs]
+        return ["%s%02d_%d" % (name, k, b) for k in range(c0 // 32, (c0 + n) // 32) for b in bs]
 
     prv, nxt = group(me)[0]
     ff, kk, cc, of, dd = T.ff, T.kk, T.cc, T.of, T.dd
 
-    dma("A", T.landp[:, 16:32], T.p[:], [], ["lpo"])
-    dma("S", T.xin[:, 256:1024], T.x[:, 0:768], [], ["xin0"], lat=START + 1.0)
-    dma("A", T.xin[:, 0:256], T.x[:, 768:1024], [], ["xin1"], lat=START + 0.5)
+    dma("A", T.landp[:, 16:32], T.p[:], [], ["lpo"], lat=START + 0.5)
+    dma("S", T.xin[:], T.x[:], [], ["xin"], lat=START + 1.2)
     dma("S", T.uin[:], T.u[:], ["lpo"], ["uin"], lat=START + 0.5)
 
-    lastw["gq"] = rec("G", lambda: g.iota(T.pi[:], [[2, 8]], 0, 1), [], ["pi"], 0.13)
-    EC, UX, SG, LQ = 0, 10, 18, 34
+    lastw["gq"] = rec("G", lambda: g.iota(T.pi[:], [[1, 16]], 0, 1), [], ["pi"], 0.13)
+    EA, EC, UX, SG, LQ, PC, E16, TE = 0, 8, 16, 24, 40, 44, 46, 50
     iota(T.idn[:], [[-1, 128]], 0, 1, ["idn"], 128)
-    iota(kk[:, EC:EC + 2], [[1, 2]], 0, 0, ["k0"])
-    iota(kk[:, EC + 2:EC + 10], [[0, 2], [1, 2], [0, 2]], 0, 0, ["k1"])
+    iota(kk[:, EA:EA + 8], [[0, 4], [1, 2]], 0, 0, ["k0"])
+    iota(kk[:, EC:EC + 8], [[0, 2], [1, 2], [0, 2]], 0, 0, ["k1"])
+    iota(kk[:, PC:PC + 1], [[0, 1]], 32, 1, ["p32"])
+    iota(kk[:, E16:E16 + 4], [[16, 2], [0, 2]], 0, 0, ["k2_"])
     iota(T.vv[:], [[1, 32], [-8, 4]], 0, 0, ["vv"], 128)
     iota(kk[:, UX:UX + 8], [[0, 2], [32, 4]], 0, 0, ["k7"])
     iota(kk[:, LQ:LQ + 4], [[1, 2], [4, 2]], 0, 0, ["k9"])
-    iota(kk[:, SG:SG + 16], [[1, 4], [64, 4]], 0, 0, ["k8"])
+    ms(dd[:, 0:3], 0.0, ["dd%d%d" % (a, i) for a in range(4) for i in range(3)])
     for a in range(4):
         dr, dc = DIR[2 * a]
         for i, c in enumerate((dr, dc, -dr)):
-            ms(dd[32 * a:32 * a + 32, i:i + 1], float(c), ["dd%d%d" % (a, i)])
+            if c:
+                ms(dd[32 * a:32 * a + 32, i:i + 1], float(c), ["dd%d%d" % (a, i)])
     dks = ["dd%d%d" % (a, i) for a in range(4) for i in range(3)]
-    send(T.landp[:, 16:32], lambda o: T.landp[:, 32:48] if o == prv else T.landp[:, 0:16], 0, "ap", ["lpo"], "lpa", before=4)
+    send(T.landp[:, 16:32], lambda o: T.landp[:, 32:48] if o == prv else T.landp[:, 0:16], 0, "ap", ["lpo"], "lpa", before=PB)
 
-    fields = {"q": (0, 0, 15), "r": (0, 0, 7), "ch": (0, 4, 1), "r6": (3, 0, 7), "a": (0, 5, 3), "q1": (0, 1, 7), "k2": (0, 2, 3),
-              "lo": (0, 3, 7), "k3": (2, 2, 3), "k4": (1, 1, 3), "r7": (6, 1, 7)}
-    col = {}
-    for i, (nm, (j, sh, an)) in enumerate(fields.items()):
-        ts(T.fi[:, i:i + 1], T.pi[:, j:j + 1], sh, an, A.logical_shift_right, A.bitwise_and, ["pi"], ["fi%d" % i])
-        col[nm] = ff[:, i:i + 1]
-    cp(ff[:, 0:11], T.fi[:, 0:11], ["fi%d" % i for i in range(11)], list(fields))
+    fields = [[(0, 15, 0, 1, 1, ["q"]), (0, 7, 0, 8, 1, ["r", 1, 2, 3, 4, 5, "r6", "r7"]), (4, 1, 0, 1, 1, ["ch"]),
+               (1, 7, 0, 15, 14, ["q1", "q7"]), (5, 3, 0, 1, 1, ["a"])],
+              [(2, 3, 0, 5, 4, ["k2", "k3"]), (3, 7, 0, 1, 1, ["lo"]), (1, 3, 1, 2, 1, ["k5"]), (3, 1, 0, 1, 1, ["w"])]]
+    col, i = {"p32": kk[:, PC:PC + 1]}, 0
+    for part in fields:
+        i0, names = i, []
+        for sh, an, j0, j1, st, nms in part:
+            ts(T.fi[:, i:i + len(nms)], T.pi[:, j0:j1:st], sh, an, A.logical_shift_right, A.bitwise_and, ["pi"], ["fi%d" % i])
+            names.append("fi%d" % i)
+            for nm in nms:
+                col[nm], i = ff[:, i:i + 1], i + 1
+        cp(ff[:, i0:i], T.fi[:, i0:i], names, [nm for f in part for nm in f[5] if isinstance(nm, str)])
     taken = [0]
 
     def lin(name, *terms):
@@ -239,16 +255,20 @@ def rank_program(g, core, T, topo):
             rest, keys = out, [name]
         return out
 
-    O_SP, O_R0, O_C, O_FM, O_CP, O_OP, O_LQ, O_U, O_SG, O_R, O_RI, O_CQ, O_L, O_S = 0, 2, 6, 40, 44, 46, 48, 52, 68, 84, 92, 96, 100, 104
-    ts(of[:, O_SP:O_SP + 1], col["q"], 8.0, 64.0, A.mult, A.add, ["q"], ["osp0"])
-    ts(of[:, O_SP + 1:O_SP + 2], col["r"], 32.0, lin("sp", (-24, "q"), 192.0), A.mult, A.add, ["r", "sp"], ["osp1"])
+    O_SP, O_R0, O_LC, O_FM, O_CP, O_OP, O_LQ, O_U, O_SG, O_R, O_RI, O_CQ, O_L, O_S = 0, 2, 6, 40, 120, 46, 48, 52, 68, 84, 92, 96, 100, 104
+    for i in range(2):
+        ts(of[:, O_SP + i:O_SP + i + 1], col["q"], 8.0, 128.0 * i, A.mult, A.add, ["q"], ["osp%d" % i])
 
-    qz("qa", 0, 256, T.xin[:], ["xin0", "xin1"], ["qa"])
+    qz("qa", 0, 256, T.xin[:], ["xin"], ["qa"])
     osp = of[:, O_SP:O_SP + 2]
     pick("snd", 0, "qa", 0, 256, osp, 2, ["qa", "osp0", "osp1"], "snd")
-    send(T.sndc[:].bitcast(dt.uint8), lambda o: T.lsc[:, 32 * me:32 * me + 32].bitcast(dt.uint8), 2, "ac", ["sndc"], "lsac", before=4, hand="ac")
-    lastw["sent"] = send(T.snds[:], lambda o: T.lss[:, 32 * me:32 * me + 32], 2, "asc", ["snds"], "lsas", before=8, hand="asc")
+    for nm in [m for m in HAND if m in ("ac", "asc")]:
+        src, key = (T.snds[:], "snds") if nm == "asc" else (T.sndc[:].bitcast(dt.uint8), "sndc")
+        lastw["sent"] = send(src, lambda o: handed_ap(nm, me, 0), 2, nm, [key], "ls" + nm[0:3:2], before=FIRSTB, hand=nm)
     pick("ls", 32 * me, "qa", 0, 256, osp, 2, ["qa", "osp0", "osp1"], "lso")
+    for o in [iota(kk[:, SG:SG + 16], [[1, 4], [64, 4]], 0, 0, ["k8"]), iota(kk[:, TE:TE + 16], [[0, 2], [32, 4], [1, 2]], 0, 0, ["k3_"]),
+              iota(T.w2[:, 0:6], [[0, 3], [32, 2]], 0, 0, ["w2a"]), iota(T.w2[:, 6:14], [[0, 2], [32, 2], [0, 2]], 0, 0, ["w2b"])]:
+        o["after"] = [lastw["sent"]]
 
     ms(T.ez[:], 0.0, ["ez"], 260)
     ts(T.idn[:], T.idn[:], 0.0, None, A.is_equal, None, ["idn"], ["idn"])
@@ -261,45 +281,27 @@ def rank_program(g, core, T, topo):
 
     for i, nm in enumerate(["dr", "dc", "ndr"]):
         col[nm] = dd[:, i:i + 1]
-    af(dd[:, 4:8], kk[:, EC + 2:EC + 6], col["dc"], col["dr"], ["k1"] + dks, ["drt", "dr", "dc", "ndr"])
-    af(dd[:, 8:18], kk[:, EC:EC + 10], col["ndr"], col["dc"], ["k0", "k1", "dr"], ["dct"])
+    af(dd[:, 10:14], kk[:, EC:EC + 4], col["ndr"], col["dc"], ["k1"] + dks, ["dcl", "dr", "dc", "ndr"])
     lin("rg", ("dc", "ch"), "dr")
-    lin("cg", ("ndr", "ch"), "dc")
-    lin("r2", (2, "r6"), 16.0)
-    ts(of[:, O_R0:O_R0 + 4], kk[:, EC + 2:EC + 6], lin("r0c", (8, "rg"), "r2"), None, A.add, None, ["k1", "r0c"], ["or0"])
+    lin("r2", (2, "r"), 16.0)
+    ts(of[:, O_R0:O_R0 + 4], kk[:, EC:EC + 4], lin("r0c", (8, "rg"), "r2"), None, A.add, None, ["k1", "r0c"], ["or0"])
 
-    lin("q32", (1, "q"), 32.0)
-    lin("q48", (1, "q"), 48.0)
-    lin("c16", (16, "ch"), "q32")
-    lin("t8", (8, "k2"), 32.0)
-    lin("t32", (32, "q"), (-128, "k2"), 0.0)
-    lin("j8", (8, "q1"), (-8, "a"), 32.0)
-    raw, add = [], []
-    for x, h in enumerate(STRIDE):
-        o = 10 * x
-        af(T.w1[:, o:o + 6], dd[:, 8:14], float(h), col["c16"], ["dct", "c16"], ["w1a%d" % x])
-        af(T.w1[:, o + 6:o + 10:2], dd[:, 14:18:2], float(h), col["q32"], ["dct", "q32"], ["w1b%d" % x])
-        af(T.w1[:, o + 7:o + 10:2], dd[:, 15:18:2], float(h), col["q48"], ["dct", "q48"], ["w1c%d" % x])
-        af(T.w2[:, o:o + 10], kk[:, EC:EC + 10], 32.0, 0.0, ["k0", "k1"], ["w2a%d" % x])
-        raw += ["w1a%d" % x, "w1b%d" % x, "w1c%d" % x]
-        add += ["w2a%d" % x]
-    for x in range(2):
-        af(T.w1[:, 30 + 2 * x:31 + 2 * x], col["cg"], float(STRIDE[x]), col["t8"], ["cg", "t8"], ["w1d%d" % x])
-    af(T.w1[:, 31:32], col["j8"], 1.0, 0.0, ["j8"], ["w1e"])
-    af(T.w2[:, 30:33], kk[:, EC:EC + 3], 0.0, col["t32"], ["k0", "k1", "t32"], ["w2b"])
-    cp(T.i1[:, 0:33], T.w1[:, 0:33], raw + ["w1d0", "w1d1", "w1e"], ["i1"])
-    ts(T.i1[:, 0:33], T.i1[:, 0:33], 31, None, A.bitwise_and, None, ["i1"], ["i1"])
-    ts(T.i2[:, 2:10], T.i1[:, 2:10], 16, None, A.bitwise_and, None, ["i1"], ["i2"])
-    af(T.w3[:, 2:10], kk[:, EC + 2:EC + 10], 16.0, 0.0, ["k1"], ["w3"])
-    tt(T.w2[:, 2:10], T.w3[:, 2:10], T.i2[:, 2:10], A.add, ["w3", "i2"], ["w2a0"])
-    tt(T.w1[:, 0:33], T.w2[:, 0:33], T.i1[:, 0:33], A.add, add + ["w2b", "i1"], ["w1"])
-    cp(of[:, O_C:O_C + 33], T.w1[:, 0:33], ["w1"], ["oc"])
-    ts(of[:, O_FM:O_FM + 4], kk[:, LQ:LQ + 4], 8.0, lin("fm", (16, "q"), (-31, "q1"), 0.0), A.mult, A.add, ["k9", "fm"], ["ofm"])
+    af(T.w1[:, 0:4], dd[:, 10:14], float(STRIDE[0]), col["p32"], ["dcl", "p32"], ["w1a"])
+    af(T.w1[:, 4:5], col["a"], -8.0, lin("j8", (8, "q1"), 32.0), ["a", "j8"], ["w1b"])
+    cp(T.i1[:, 0:5], T.w1[:, 0:5], ["w1a", "w1b"], ["i1"])
+    ts(T.i1[:, 0:5], T.i1[:, 0:5], 31, None, A.bitwise_and, None, ["i1"], ["i1"])
+    ts(T.i2[:, 0:4], T.i1[:, 0:4], 16, None, A.bitwise_and, None, ["i1"], ["i2"])
+    tt(T.w3[:, 4:8], kk[:, E16:E16 + 4], T.i1[:, 0:4], A.add, ["k2_", "i1"], ["w3"])
+    tt(T.w3[:, 4:8], T.w3[:, 4:8], T.i2[:, 0:4], A.add, ["w3", "i2"], ["w3"])
+    cp(of[:, O_LC:O_LC + 4], T.w3[:, 4:8], ["w3"], ["ol0"])
+    lin("b0", (-2, "q1"), "q")
+    ts(of[:, O_FM:O_FM + 4], kk[:, LQ:LQ + 4], 8.0, lin("fm", (16, "b0"), "q1"), A.mult, A.add, ["k9", "fm"], ["ofm"])
 
     def cand_lists(x):
         rot, rn = T["rot%d" % x], "rot%d" % x
-        act(T.a3[:], T.gg[:].indirect(of[:, O_C + 10 * x + 2:O_C + 10 * x + 10]), FN.Copy, ["gg", "oc"], ["a3"], gat(128))
-        tp(rot[:, 0:128], T.a3[:], ["a3"], [rn, rn + "l"])
+        o = O_LC + (6 + 4 * x if x else 0)
+        act(T.a3[:], T.gg[:].indirect(of[:, o:o + 4]), FN.Copy, ["gg", "oc" if x else "ol0"], ["a3"], gat(64))
+        tp(rot[:, 0:64], T.a3[:], ["a3"], [rn, rn + "l"])
         cp(T.ol[:], rot[:, 0:64].indirect(of[:, O_FM + 2:O_FM + 4]), [rn + "l", "ofm"], ["ol"], gat(32))
 
     def relabel(src, n, out, rkey, wkey, back):
@@ -311,30 +313,29 @@ def rank_program(g, core, T, topo):
         tt(out, T.p2[:, s], T.p3[:, s], A.add, ["p2", "p3"], [wkey], 2 * n)
 
     def spread(x):
-        rot, rn, sem = T["rot%d" % x], "rot%d" % x, newsem("d")
+        rot, rn, sem, s = T["rot%d" % x], "rot%d" % x, newsem("d"), 0 if x else 64
         for j in range(1, 4):
-            c0 = 64 + 64 * j
-            dma("S", rot[0:128 - 32 * j, c0:c0 + 64], rot[32 * j:128, 64:128], [rn], [rn + "j%d" % j], sem, lat=START + 1.0)
-            dma("S", rot[128 - 32 * j:128, c0:c0 + 64], rot[0:32 * j, 64:128], [rn], [rn + "k%d" % j], sem, lat=START + 1.0)
+            c0 = s + 64 * j
+            dma("S", rot[0:128 - 32 * j, c0:c0 + 64], rot[32 * j:128, s:s + 64], [rn], [rn + "j%d" % j], sem, lat=START + 1.0)
+            dma("S", rot[128 - 32 * j:128, c0:c0 + 64], rot[0:32 * j, s:s + 64], [rn], [rn + "k%d" % j], sem, lat=START + 1.0)
 
     def steps_of(x):
         rot, rn = T["rot%d" % x], "rot%d" % x
         keys = [rn + jk + str(j) for jk in "jk" for j in range(1, 4)]
-        act(T.lq[:, 0:64], rot[:, 64:320].indirect(of[:, O_LQ:O_LQ + 4]), FN.Copy, [rn, "olq"] + keys, ["lq"], gat(64))
+        act(T.lq[:, 0:64], rot[:, (0 if x else 64):(256 if x else 320)].indirect(of[:, O_LQ:O_LQ + 4]), FN.Copy, [rn, "olq"] + keys, ["lq"], gat(64))
         tt(T.df[:, 0:64], T.lq[:, 0:64], T.lq[:, 1:65], A.subtract, ["lq", "lqz"], ["df0"], 128)
         act(T.df[:, 7:64:8], T.lq[:, 7:64:8], FN.Copy, ["lq"], ["df0"])
         act(T.df[:, 64:128], T.df[:, 0:64], FN.Copy, ["df0"], ["df1"])
 
-    lin("w", (0.125, "q"), (-0.125, "r"), 0.0)
-    lin("l2", (32, "q"), (-64, "q1"), (2, "w"), 8.0)
-    ts(T.w3[:, 0:1], T.i1[:, 31:32], 8.0, col["l2"], A.mult, A.add, ["i1", "l2"], ["l1"])
+    lin("l2", (32, "b0"), (2, "w"), (16, "ch"), 8.0)
+    ts(T.w3[:, 0:1], T.i1[:, 4:5], 8.0, col["l2"], A.mult, A.add, ["i1", "l2"], ["l1"])
     ts(of[:, O_LQ:O_LQ + 4], kk[:, LQ:LQ + 4], T.w3[:, 0:1], None, A.add, None, ["k9", "l1"], ["olq"])
     ms(T.lq[:, 64:72], 0.0, ["lqz"])
 
     cp(T.a1[:], T.landp[:].indirect(of[:, O_R0:O_R0 + 4]), ["lpo", "lpa", "or0"], ["a1"], gat(64))
     tp(T.gg[:], T.a1[:], ["a1"], ["gg"])
     cand_lists(0)
-    relabel(T.rot0[:, 64:128], 64, T.rot0[:, 64:128], "rot0", "rot0", False)
+    relabel(T.rot0[:, 0:64], 64, T.rot0[:, 64:128], "rot0l", "rot0", False)
     spread(0)
     dma("S", T.qwc[:].bitcast(dt.uint8), T.wc[:], ["sent", "rot0"], ["qwc"], lat=START + 1.0)
     dma("S", T.qws[:], T.ws[:], ["sent", "rot0"], ["qws"], lat=START + 1.2)
@@ -356,71 +357,87 @@ def rank_program(g, core, T, topo):
     lin("tg0", (2, "r"), (4, "a"), -14.0)
     lin("tg1", (1, "tg0"), 2.0)
     ts(of[:, O_SG:O_SG + 16], kk[:, SG:SG + 16], lin("q4", (4, "q"), 0.0), None, A.add, None, ["k8", "q4"], ["osg"])
-    ts(of[:, O_CP:O_CP + 1], col["k3"], 8.0, lin("cpb", (64, "q"), (-96, "q1"), (-64, "k2"), 7.0), A.mult, A.add, ["k3", "cpb"], ["ocp"])
+    lin("cpb", (64, "b0"), (32, "q1"), (-64, "k2"), 7.0)
+    for x, nm in enumerate(["k2", "k3"]):
+        ts(of[:, O_CP + 2 * x:O_CP + 2 * x + 1], col[nm], 8.0, col["cpb"], A.mult, A.add, [nm, "cpb"], ["ocp%d" % x])
 
-    lin("r3", (1, "r2"), 1.0)
-    lin("qq0", (2, "q"), float(2 * (72 - 8 * me)))
-    lin("qq1", (1, "qq0"), 1.0)
-    rk_, sk_ = [], []
-    for x in range(2):
+    af(dd[:, 4:8], kk[:, EC:EC + 4], col["dc"], col["dr"], ["k1", "dr"], ["drt"])
+    af(dd[:, 14:22], kk[:, EA:EA + 8], col["dc"], col["dr"], ["k0", "dr"], ["dra"])
+    lin("qq", (2, "q"), float(2 * (72 - 8 * me)))
+    for x, (now, then) in enumerate([("r", "r6"), ("r6", "r7")]):
         h, h2 = STRIDE[x], STRIDE[x + 1]
-        lin("hw%d" % x, (2 * (h2 - h), "w"), 2.0 * h)
-        for e in range(2):
-            o = 12 + 4 * x + 2 * e
-            af(T.w3[:, o:o + 2], dd[:, 4 + 2 * e:6 + 2 * e], col["hw%d" % x], col["r%d" % (2 + e)], ["drt", "hw%d" % x, "r%d" % (2 + e)],
-               ["ra%d%d" % (x, e)])
-            rk_.append("ra%d%d" % (x, e))
-            nm, o = "sb%d%d" % (x, e), 24 + 8 * x + e
-            col["dre"] = dd[:, 4 + 2 * e:5 + 2 * e]
-            lastw["dre"] = lastw["drt"]
-            lin(nm, (2 * h, "dre"), "qq%d" % e)
-            af(T.w3[:, o:o + 8 - e:2], kk[:, UX:UX + 4], 1.0, col[nm], ["k7", nm], [nm + "w"])
-            sk_.append(nm + "w")
-    cp(of[:, O_R:O_R + 8], T.w3[:, 12:20], rk_, ["or"])
-    ts(of[:, O_RI:O_RI + 4], T.w3[:, 16:20], -16.0, 15.0, A.add, A.min, rk_, ["ori"])
-    cp(T.i3[:], T.w3[:, 24:40], sk_, ["i3"])
+        lin("dw%d" % x, (-1, now), then)
+        lin("rw%d" % x, ("w", "dw%d" % x), now)
+        lin("hw%d" % x, (h2 - h, "w"), float(h))
+        af(T.w3[:, 12 + 4 * x:16 + 4 * x], dd[:, 4:8], col["hw%d" % x], col["rw%d" % x], ["drt", "hw%d" % x, "rw%d" % x], ["ra%d" % x])
+        af(T.w3[:, 24 + 8 * x:32 + 8 * x], dd[:, 14:22], 2.0 * h, col["qq"], ["dra", "qq"], ["sa%d" % x])
+    af(T.w3[:, 40:48], kk[:, EC:EC + 8], 0.5, 0.0, ["k1"], ["eh"])
+    tt(T.w3[:, 12:20], T.w3[:, 12:20], T.w3[:, 40:48], A.add, ["ra0", "ra1", "eh"], ["ra"])
+    ts(of[:, O_R:O_R + 8], T.w3[:, 12:20], 2.0, 16.0, A.mult, A.add, ["ra"], ["or"])
+    ts(of[:, O_RI:O_RI + 4], T.w3[:, 16:20], 2.0, 15.0, A.mult, A.min, ["ra"], ["ori"])
+    tt(T.i3[:], T.w3[:, 24:40], kk[:, TE:TE + 16], A.add, ["sa0", "sa1", "k3_"], ["i3"])
     ts(T.i3[:], T.i3[:], 127, None, A.bitwise_and, None, ["i3"], ["i3"])
     cp(of[:, O_S:O_S + 16], T.i3[:], ["i3"], ["os_"])
-    lin("cq", (32, "q"), (-64, "q1"), (8, "k4"), 7.0)
-    ts(of[:, O_CQ:O_CQ + 4], kk[:, EC + 2:EC + 6], 64.0, col["cq"], A.mult, A.add, ["k1", "cq"], ["ocq"])
+    af(dd[:, 8:10], kk[:, EA:EA + 2], col["ndr"], col["dc"], ["k0", "dr"], ["dcm"])
+    lin("cg", ("ndr", "ch"), "dc")
+    lin("t8", (8, "k2"), 32.0)
+    lin("t32", (32, "q"), (-128, "k2"), 0.0)
+    for x, h in enumerate(STRIDE):
+        af(T.w1[:, 8 + 2 * x:10 + 2 * x], dd[:, 8:10], float(h), col["p32"], ["dcm", "p32"], ["w1m%d" % x])
+        if x:
+            af(T.w1[:, 10 + 4 * x:14 + 4 * x], dd[:, 10:14], float(h), col["p32"], ["dcl", "p32"], ["w1l%d" % x])
+    af(T.w1[:, 22:25], kk[:, E16 + 1:E16 + 4], (STRIDE[1] - STRIDE[0]) / 16, float(STRIDE[0]), ["k2_"], ["hs"])
+    af(T.w1[:, 22:25], T.w1[:, 22:25], col["cg"], col["t8"], ["hs", "cg", "t8"], ["hs"])
+    af(T.w2[:, 14:17], kk[:, EA:EA + 3], 0.0, col["t32"], ["k0", "t32"], ["w2c"])
+    cp(T.i1[:, 8:25], T.w1[:, 8:25], ["w1m0", "w1m1", "w1m2", "w1l1", "w1l2", "hs"], ["i4"])
+    ts(T.i1[:, 8:25], T.i1[:, 8:25], 31, None, A.bitwise_and, None, ["i4"], ["i4"])
+    tt(T.w1[:, 8:25], T.w2[:, 0:17], T.i1[:, 8:25], A.add, ["w2a", "w2b", "w2c", "i4"], ["w4"])
+    cp(of[:, O_LC + 4:O_LC + 21], T.w1[:, 8:25], ["w4"], ["oc"])
+    lin("cq", (-32, "b0"), (8, "k5"), 39.0)
+    ts(of[:, O_CQ:O_CQ + 4], kk[:, EC:EC + 4], 64.0, col["cq"], A.mult, A.add, ["k1", "cq"], ["ocq"])
     ts(of[:, O_OP:O_OP + 1], col["w"], 64.0, col["cq"], A.mult, A.add, ["w", "cq"], ["oop"])
-    lin("row", (STRIDE[2], "rg"), "r7")
-    lin("b16", (16, "q"), (-32, "q1"), 0.0)
-    lin("lx", (25, "row"), (1, "b16"), 32.0)
+    lin("row", (STRIDE[2], "rg"), "q7")
+    lin("b16", (16, "b0"), 32.0)
+    lin("lx", (25, "row"), "b16")
     ts(T.w3[:, 20:21], col["row"], 0.0, 7.0, A.max, A.min, ["row"], ["in7"])
     ts(of[:, O_L:O_L + 1], T.w3[:, 20:21], -24.0, col["lx"], A.mult, A.add, ["in7", "lx"], ["oll"])
-    ts(of[:, O_L + 2:O_L + 3], T.w3[:, 20:21], col["b16"], None, A.add, None, ["in7", "b16"], ["oli"])
+    ts(of[:, O_L + 2:O_L + 3], T.w3[:, 20:21], col["b16"], -32.0, A.add, A.add, ["in7", "b16"], ["oli"])
     ms(T.po[:, 16:32], 0.0, ["poz"])
     qz("qv", 0, 128, T.vin[:], ["vin"], ["qv"])
 
-    def unpack(bank, src, to, name):
+    def unpack(bank, src, to, names, c0=0, n=256):
         for b in range(4):
-            mm(bank + b, 256, "qe", 128 * b, src[0], src[1], True, True, ["qe0%d" % b] + src[2])
+            mm(bank + b, n, "qe", 128 * b, src[0], src[1] + c0, True, True, ["qe0%d" % b] + src[2])
         for b in range(4):
-            act(to[:, 256 * b:256 * b + 256], T["ps%d" % (bank + b)][:, 0:256], FN.Copy, ["ps%d" % (bank + b)], ["%s%d" % (name, b)], 256)
+            act(to[:, 256 * b + c0:256 * b + c0 + n], T["ps%d" % (bank + b)][:, 0:n], FN.Copy, ["ps%d" % (bank + b)],
+                ["%s%d" % (k, b) for k in names], n)
 
-    def chunk(kind, bank, c0, n, off, key, src, fs, fname, pieces):
+    def chunk(kind, bank, c0, n, off, key, src, fs, fname, pieces, new=None):
         f0 = c0 % 256
         for b in range(4):
             mm(bank + b, n, "qe", 128 * b, src[0], src[1] + f0, True, False, ["qe0%d" % b] + src[2])
+        line["on"] = src[0] + key
         for b in range(4):
-            out, win = T.yt[:, 4 * c0 + b:4 * (c0 + n):4], T.bt[:, 256 * b:256 * b + 256].indirect(off)
+            k = new or n
+            out, win = T.yt[:, 4 * c0 + b:4 * (c0 + k):4], T.bt[:, 256 * b:256 * b + 256].indirect(off)
             if GATHER[kind][b] == "V":
-                ts(out, win, 0.015625, None, A.mult, None, ["bt%d" % b, key], units("yt", c0, n, [b]), gat(n))
+                ts(out, win, 0.015625, None, A.mult, None, ["bt%d" % b, key], units("yt", c0, k, [b]), gat(k))
             else:
-                act(out, win, FN.Copy, ["bt%d" % b, key], units("yt", c0, n, [b]), gat(n), scale=0.015625)
+                act(out, win, FN.Copy, ["bt%d" % b, key], units("yt", c0, k, [b]), gat(k), scale=0.015625)
+        line["on"] = None
         qz("qy", c0, n, T.yt[:, 4 * c0:4 * (c0 + n)], units("yt", c0, n), units("qy", c0, n, [0]))
         for b in range(4):
             mm(bank + b, n, "qw", 128 * b, "qy", c0, False, True, ["qwc", "qws"] + units("qy", c0, n, [0]))
         for b in range(4):
-            for t0, x0, m in pieces:
-                tt(T.xt[:, 4 * x0 + b:4 * (x0 + m):4], T["ps%d" % (bank + b)][:, t0:t0 + m],
-                   fs[:, 256 * b + f0 + t0:256 * b + f0 + t0 + m], A.max, ["ps%d" % (bank + b), "%s%d" % (fname, b)], units("xt", x0, m, [b]), m)
+            for t0, x0, m, st in pieces:
+                tt(T.xt[:, 4 * x0 + b:4 * (x0 - x0 % st + st * m):4 * st], T["ps%d" % (bank + b)][:, t0:t0 + m],
+                   fs[:, 256 * b + f0 + t0:256 * b + f0 + t0 + m], A.max, ["ps%d" % (bank + b)] + ["%s%d" % (f, b) for f in fname],
+                   units("xt", x0 - x0 % st, st * m, [b]), m)
 
     def shift_columns(win, keys, rows, x, out, okey):
         cp(T.a1[:], win.indirect(rows), keys, ["a1"], gat(64))
         tp(T.gg[:], T.a1[:], ["a1"], ["gg"])
-        cp(T.a2[:], T.gg[:].indirect(of[:, O_C + 10 * x:O_C + 10 * x + 2]), ["gg", "oc"], ["a2_"], gat(32))
+        cp(T.a2[:], T.gg[:].indirect(of[:, O_LC + 4 + 2 * x:O_LC + 6 + 2 * x]), ["gg", "oc"], ["a2_"], gat(32))
         tp(out, T.a2[:], ["a2_"], [okey])
 
     def read_list(win, keys, rows, x, out, okey):
@@ -429,10 +446,11 @@ def rank_program(g, core, T, topo):
 
     for x in range(3):
         rd = x + 1
+        line["rd"] = "/%d" % rd
         qx, nq, pa, land, ln = "qx%d" % rd, "qx%d" % (rd + 1), "pa%d" % rd, T["land%d" % rd], "land%d" % rd
         half = [("qa", 0, ["qa"])] * 2 if x == 0 else [(qx, 0, [qx + "e"]), (qx, 0, [qx + "i"])]
         own = (half[0][0], 0, half[0][2] + half[1][2])
-        win = ("ls", 0, ["lsoc", "lsos", "lsac", "lsas"]) if x == 0 else (qx, 256, [qx + "s", qx + "t"])
+        win = ("ls", 0, ["lsoc", "lsos", "lsa", "lsac"]) if x == 0 else (qx, 256, [qx + "s", qx + "t"])
         seeds = (qx, 256, [qx + "tc", qx + "ts"]) if x == 0 else win
         for hf in range(2):
             for b in range(4):
@@ -474,29 +492,32 @@ def rank_program(g, core, T, topo):
             return ld[:, n * ((me - o + 1) % N):n * ((me - o + 1) % N) + n]
 
         if x < 2:
-            cp(mine, T.sc[:].indirect(of[:, O_CP:O_CP + 1]), ["sc", "ocp"], [ln + "o"], gat(16))
+            cp(mine, T.sc[:].indirect(of[:, O_CP + 2 * x:O_CP + 2 * x + 1]), ["sc", "ocp%d" % x], [ln + "o"], gat(16))
         else:
             shift_columns(T.sc[:], ["sc", "ocq"], of[:, O_CQ:O_CQ + 4], x, mine, ln + "o")
         send(mine, slot, 0, "an%d" % rd, [ln + "o"], ln + "n", hand="af%d" % rd)
         if x < 2:
-            send(mine, slot, 1, "af%d" % rd, [ln + "o"], ln + "f", before=2)
+            send(mine, slot, 1, "af%d" % rd, [ln + "o"], ln + "f", before=FARB)
         if x == 0:
             pick(qx, 256, "ls", 0, 256, of[:, O_SG:O_SG + 16], 16, win[2] + ["osg"], qx + "t")
-        unpack(4, seeds, T.bt, "bt")
-        unpack(4, own, T.fo, "fo")
+        unpack(4, seeds, T.bt, ["bt"])
+        unpack(4, own, T.fo, ["fo"])
         if x == 1:
             read_list(mine, [ln + "o", "ori"], of[:, O_RI:O_RI + 4], x, T.oi[:], "oi")
+            chunk("inner1", 0, 128, 128, T.oi[:, 8:16], "oi", half[1], T.fo, ["fo"], [(0, 96, 128, 1)])
         if x == 2:
             cp(T.oi[:], mine.indirect(of[:, O_L + 2:O_L + 3]), [ln + "o", "oli"], ["oi"], gat(16))
-        if x > 0:
-            chunk("inner", 0, 128, 128, T.oi[:, 8:16], "oi", half[1], T.fo, "fo", [(0, 128 if x < 2 else 64, 128)])
+            chunk("inner2", 0, 64, 192, T.oi[:, 4:16], "oi", own, T.fo, ["fo"], [(0, 64, 192, 1)])
         if x < 2:
             read_list(land[:, 0:48], [ln + "o", ln + "n", "or"], of[:, O_R + 4 * x:O_R + 4 * x + 4], x, T.om[:], "om")
         else:
             cp(T.om[:], land[:].indirect(of[:, O_L:O_L + 1]), [ln + "o", ln + "n", "oll"], ["om"], gat(16))
         if x == 0:
-            chunk("inner0", 0, 128, 128, T.om[:, 8:16], "om", half[1], T.fo, "fo", [(0, 128, 128)])
-        chunk("edge%d" % x, 4, 0, 128, T.om[:, 0:8], "om", half[0], T.fo, "fo", [(0, 0, 128)] if x < 2 else [(0, 192, 64), (64, 0, 64)])
+            chunk("own", 4, 0, 256, T.om[:], "om", own, T.fo, ["fo"], [(0, 64, 192, 1), (192, 0, 64, 1)])
+        if x == 1:
+            chunk("edge1", 4, 0, 128, T.om[:, 0:8], "om", half[0], T.fo, ["fo"], [(0, 224, 32, 1), (32, 0, 96, 1)])
+        if x == 2:
+            chunk("edge2", 4, 0, 128, T.om[:, 0:4], "om", half[0], T.fo, ["fo"], [(0, 0, 64, 1)], 64)
         if x < 2:
             for hf in range(2):
                 qz(nq, 128 * hf, 128, T.xt[:, 512 * hf:512 * hf + 512], units("xt", 128 * hf, 128), [nq + "ei"[hf]])
@@ -504,13 +525,12 @@ def rank_program(g, core, T, topo):
             spread(rd)
             act(T.s1[:], land[:].indirect(of[:, O_S + 8 * x:O_S + 8 * x + 8]), FN.Copy, [ln + "o", ln + "n", ln + "f", "os_"], ["s1"], gat(128))
             tp(T.s2[:], T.s1[:], ["s1"], ["s2"])
-            cp(T.osd[:], T.s2[:].indirect(of[:, O_C + 30 + 2 * x:O_C + 31 + 2 * x]), ["s2", "oc"], ["os"], gat(16))
+            cp(T.osd[:], T.s2[:].indirect(of[:, O_LC + 18 + 2 * x:O_LC + 19 + 2 * x]), ["s2", "oc"], ["os"], gat(16))
             for hf in range(2):
                 nm, c0 = "st"[hf], 256 + 128 * hf
-                chunk(nm, 4 * hf, c0, 128, T.osd[:, 8 * hf:8 * hf + 8], "os", seeds, T.bt, "bt", [(0, c0, 128)])
+                chunk(nm + str(x), 4 * hf, c0, 128, T.osd[:, 8 * hf:8 * hf + 8], "os", seeds, T.bt, ["bt"], [(0, c0, 128, 1)])
                 qz(nq, c0, 128, T.xt[:, 4 * c0:4 * c0 + 512], units("xt", c0, 128), [nq + nm])
         else:
-            qz(nq, 0, 256, T.xt[:, 0:1024], units("xt", 0, 256), [nq + "o"])
             act(T.pt[:, 0:16], T.sc[:].indirect(of[:, O_OP:O_OP + 1]), FN.Copy, ["sc", "oop"], ["pt"])
             relabel(T.pt[:, 0:16], 16, T.po[:, 0:16], "pt", "po", True)
             tp(T.pt[:], T.po[:], ["po", "poz"], ["pt"])
@@ -518,50 +538,93 @@ def rank_program(g, core, T, topo):
             for a in range(4):
                 dma("S", T.op[2 * a:2 * a + 2, :], T.pt[32 * a:32 * a + 16, :], ["pt"], [], sem)
 
-    dma("S", T.oc[:], T.qx4c[:].bitcast(dt.uint8), ["qx4o"], [], lat=START + 1.0)
-    for hf in range(2):
-        mm(hf, 128, "qv", 0, "qx4", 128 * hf, True, True, ["qv", "qx4o"])
-    act(T.ysb[:, 0:128], T.ps0[:, 0:128], FN.Copy, ["ps0"], ["y0"], 128)
-    cp(T.ysb[:, 128:256], T.ps1[:, 0:128], ["ps1"], ["y1"], 128)
-    dma("A", T.y[:], T.ysb[:], ["y0", "y1"], [])
+    for hf in (1, 0):
+        qz("qx4", 128 * hf, 128, T.xt[:, 512 * hf:512 * hf + 512], units("xt", 128 * hf, 128), ["qx4%d" % hf])
+        mm(hf, 128, "qv", 0, "qx4", 128 * hf, True, True, ["qv", "qx4%d" % hf])
+    cp(T.ysb[:, 96:224], T.ps1[:, 0:128], ["ps1"], ["y1"], 128)
+    cp(T.ysb[:, 224:256], T.ps0[:, 0:32], ["ps0"], ["y2"])
+    cp(T.ysb[:, 0:96], T.ps0[:, 32:128], ["ps0"], ["y0"], 96)
+    dma("A", T.y[:], T.ysb[:], ["y0", "y1", "y2"], [], lat=START + 0.9)
     sem = newsem("d")
-    for k in range(4):
-        dma("S", T.osc[4 * k:4 * k + 4, :], T.qx4s[32 * k:32 * k + 4, :], ["qx4o"], [], sem)
+    for i, (t0, j0, n) in enumerate([(32, 0, 224), (0, 224, 32)]):
+        dma("SA"[i], T.oc[:, 4 * j0:4 * (j0 + n)], T.qx4c[:, t0:t0 + n].bitcast(dt.uint8), ["qx40", "qx41"], [], sem, lat=START + 1.2)
+        for k in range(4):
+            dma("SA"[i and k > 1], T.osc[4 * k:4 * k + 4, j0:j0 + n], T.qx4s[32 * k:32 * k + 4, t0:t0 + n], ["qx40", "qx41"], [], sem, lat=START + 0.5)
 
-    for op in ops:
-        op["pre"] = list({o["n"]: o for o in [d.get("like", d) for d in op["deps"]] + op.get("after", [])}.values())
-        op["way"], op["users"], op["left"], op["ready"] = 0.0, [], len(op["pre"]), 0.0
-    for op in reversed(ops):
-        op["way"] += op["c"] + op["lat"]
-        for o in op["pre"]:
-            o["way"] = max(o["way"], op["way"] + WAKE)
-            o["users"].append(op)
-    free, order, pool, rest = {q: 0.0 for q in Q}, [], [op for op in ops if not op["left"]], list(ops)
+    def place(need, first, rank, careful):
+        start, busy, left = {}, {q: [] for q in Q}, sorted(range(len(ops)), key=lambda n: (rank[n], n))
+        while left:
+            n = [m for m in left if all(a in start for a, d in need[m])][0]
+            left.remove(n)
+            q, c = ops[n]["q"], ops[n]["c"]
+            ready = t = max([first[n]] + [start[a] + ops[a]["c"] + d for a, d in need[n]])
+            for s, e in busy[q]:
+                if max(t, ready + careful * MARGIN) + c + careful * ROOM[q] <= s:
+                    t = max(t, ready + careful * MARGIN)
+                    break
+                t = max(t, e)
+            start[n] = t
+            busy[q] = sorted(busy[q] + [(t, t + c)])
+        return start
 
-    def gap(a, o):
-        return 0.0 if any(a is z for z in o.get("after", [])) or (o["q"] == "P" and a["q"] == "P") else a["lat"] + WAKE
+    def replay(need, lines, case):
+        compute, gather, product, remote, wake, first = case
+        cost = [o["c"] * (product if o["q"] == "P" else gather if o["gather"] else compute if o["q"] in "VA" else 1.0) for o in ops]
+        far = [first if o["tok"] == "l0" else remote if o["q"] == "G" else 1.0 for o in ops]
+        start, why, at, free = {}, {}, {q: 0 for q in Q}, {q: (0.0, None) for q in Q}
+        while len(start) < len(ops):
+            for q in Q:
+                while at[q] < len(lines[q]) and all(a in start for a, d in need[lines[q][at[q]]]):
+                    n = lines[q][at[q]]
+                    t, w = free[q]
+                    for a, d in need[n]:
+                        e = start[a] + cost[a] + (d and (d - WAKE) * far[a] + wake)
+                        if e > t:
+                            t, w = e, -1 - a
+                    start[n], why[n], free[q] = t, w, (t + cost[n], n)
+                    at[q] += 1
+        last = n = max(start, key=lambda m: start[m] + cost[m] + ops[m]["lat"])
+        pairs = []
+        while why[n] is not None:
+            if why[n] >= 0:
+                pairs.append((why[n], n))
+            n = why[n] if why[n] >= 0 else -1 - why[n]
+        return start[last] + cost[last] + ops[last]["lat"], pairs, start
 
-    for op in ops:
-        op["in"] = [(a, a["c"] + gap(a, op)) for a in op["pre"]]
-    while pool and len(ORDER) < len(ops):
-        bound = 0.0
-        for o in rest:
-            o["est"] = max([free[o["q"]]] + [a["est"] + d for a, d in o["in"]])
-            bound = max(bound, o["est"] + o["way"])
-        best = None
-        for o in pool:
-            end = o["est"] + o["c"]
-            if (best is None or (o["est"], -o["way"]) < (best["est"], -best["way"])) and not any(
-                    z["q"] == o["q"] and z["way"] > o["way"] and z["est"] < end - 0.03 and end + z["way"] > bound - SLACK for z in rest):
-                best = o
-        pool = [o for o in pool if o is not best]
-        rest = [o for o in rest if o is not best]
-        ORDER.append(best["n"])
-        free[best["q"]] = best["est"] + best["c"]
-        for o in best["users"]:
-            o["left"] -= 1
-            if not o["left"]:
-                pool.append(o)
+    if not ORDER:
+        before, after = [[] for op in ops], [[] for op in ops]
+        for op in ops:
+            gaps = {a["n"]: 0.0 for a in op["after"]}
+            for a in [d.get("like", d) for d in op["deps"]]:
+                gaps[a["n"]] = 0.0 if op["q"] == "P" and a["q"] == "P" else a["lat"] + WAKE
+            for a, d in gaps.items():
+                before[op["n"]].append((a, d))
+                after[a].append((op["n"], d))
+        rank, best = [-op["n"] for op in ops], None
+        for turn in range(TURNS):
+            back = place(after, [op["lat"] for op in ops], rank, 0)
+            start = place(before, [0.0] * len(ops), [-back[n] - ops[n]["c"] - ops[n]["ahead"] for n in range(len(ops))], 1)
+            rank = [-start[n] - ops[n]["c"] for n in range(len(ops))]
+            end = max(start[n] + ops[n]["c"] + ops[n]["lat"] for n in start)
+            if best is None or end < best[0]:
+                best = (end, start)
+        lines = {q: [n for n in sorted(best[1], key=lambda n: (best[1][n], n)) if ops[n]["q"] == q] for q in Q}
+        runs, moved = [replay(before, lines, case) for case in CASES], True
+        while moved:
+            moved = False
+            for a, b in sorted({pair for run in runs for pair in run[1]}):
+                q, start = ops[a]["q"], runs[0][2]
+                i = lines[q].index(b)
+                for k in range(1, min(i, 8) + 1) if lines[q][i - 1] == a else []:
+                    if any(start[z] >= start[lines[q][i - k]] for z, d in before[b]):
+                        break
+                    trial = dict(lines)
+                    trial[q] = lines[q][:i - k] + [b] + lines[q][i - k:i] + lines[q][i + 1:]
+                    new = [replay(before, trial, case) for case in CASES]
+                    if sum(r[0] / s[0] for r, s in zip(new, runs)) < len(CASES) - 1e-5:
+                        lines, runs, moved = trial, new, True
+                        break
+        ORDER.extend(sorted(runs[0][2], key=lambda n: (runs[0][2][n], n)))
     order = [ops[n] for n in ORDER]
 
     for op in ops:

@@ -1,51 +1,233 @@
+import math
 from concourse.bass import DstId, RemoteDMATransfer
 from concourse.mybir import dt, AluOpType, ActivationFunctionType
 
 F32, BF, I32, U16, U8, CODE = "float32", "bfloat16", "int32", "uint16", "uint8", "float8_e4m3fn_x4"
 N = 8
-STRIDE = [4, 2, 1]
 DIR = [(-1, 0), (-1, 1), (0, 1), (1, 1), (1, 0), (1, -1), (0, -1), (-1, -1)]
 HAND = {"ac": [(0, (4, 2)), (1, (3,)), (2, (5,))], "asc": [(0, (4,)), (1, (3,))], "af1": [(0, (4,))], "af2": [(0, (4,))]}
 ACROSS = (False, True, False)
-GATHER = {"own": "AVAV", "inner1": "AAAV", "inner2": "AVAV", "edge1": "AAAV", "edge2": "AVAV", "s0": "AVAV", "t0": "AAAA", "s1": "AVAV", "t1": "AAAA"}
-TURN = ["VVVV", "AVAV"]
+FO = 288
 
 SCRATCH = {}
 for _n, _w, _d in [
-    ("xin", 1024, BF), ("uin", 512, BF), ("vin", 512, BF), ("landp", 48, I32),
-    ("land1", 128, BF), ("land2", 128, BF), ("land3", 96, BF),
+    ("xin", 1024, BF), ("sx", 512, BF), ("uin", 512, BF), ("vin", 512, BF), ("landp", 96, I32),
+    ("land1", 112, BF), ("land2", 112, BF), ("land3", 128, BF), ("oe", 16, U16),
     ("ez", 520, BF), ("idn", 128, BF), ("vv", 128, BF), ("va", 128, BF), ("vb", 128, BF), ("cb", 512, BF),
-    ("pi", 16, I32), ("fi", 24, I32), ("ff", 24, F32), ("kk", 96, F32), ("cc", 64, F32), ("dd", 32, F32),
-    ("w1", 48, F32), ("w2", 48, F32), ("w3", 48, F32), ("i1", 48, I32), ("i2", 16, I32), ("i3", 16, I32),
-    ("of", 128, U16),
-    ("zt", 1024, BF), ("yt", 2048, BF), ("xt", 2048, BF), ("bt", 1024, BF), ("fo", 1024, BF),
-    ("sy", 256, F32), ("fl", 512, BF), ("ns", 128, BF), ("nt", 128, BF), ("sc", 128, BF),
-    ("lq", 72, BF), ("df", 128, BF), ("a1", 64, BF), ("gg", 64, BF), ("a2", 32, BF), ("uu", 32, BF), ("a3", 64, BF),
-    ("s1", 128, BF), ("s2", 128, BF), ("rot0", 320, BF), ("rot1", 320, BF), ("rot2", 320, BF),
-    ("om", 16, U16), ("oi", 16, U16), ("osd", 16, U16), ("ol", 32, U16),
-    ("p1", 64, F32), ("p2", 64, F32), ("p3", 64, F32), ("po", 32, F32), ("pt", 32, F32),
+    ("pi", 16, I32), ("fi", 24, I32), ("ff", 24, F32), ("kk", 128, F32), ("cc", 64, F32), ("dd", 48, F32),
+    ("w1", 48, F32), ("w2", 48, F32), ("tb", 80, F32), ("kb", 80, F32), ("ti", 80, I32), ("i1", 48, I32), ("i2", 16, I32), ("i3", 16, I32),
+    ("of", 192, U16),
+    ("zt", 1024, BF), ("yt", 2048, BF), ("xt", 2048, BF), ("bt", 1024, BF), ("fo", 4 * FO, BF),
+    ("sy", 256, F32), ("fl", 768, BF), ("ns", 128, BF), ("nt", 128, BF), ("sc", 128, BF),
+    ("lq", 136, BF), ("df", 128, BF), ("a1", 192, BF), ("gg", 192, BF), ("a2", 96, BF), ("uu", 96, BF), ("a3", 128, BF),
+    ("a4", 128, BF), ("g4", 128, BF), ("s1", 64, BF), ("s2", 64, BF), ("rot0", 256, BF), ("rot1", 256, BF), ("rot2", 512, BF),
+    ("om", 16, U16), ("oi", 32, U16), ("osd", 16, U16), ("ol", 96, U16),
+    ("po", 32, F32), ("pt", 32, F32),
     ("ysb", 256, F32),
 ]:
     SCRATCH[_n] = ("sbuf", [128, _w], _d)
-for _n, _w in [("qa", 256), ("snd", 32), ("ls", 256), ("qx1", 512), ("qx2", 512), ("qx3", 512), ("qx4", 256),
-               ("pa1", 512), ("pa2", 512), ("pa3", 512), ("qe", 1536), ("qc", 128), ("qu", 128), ("qup", 256),
-               ("qv", 128), ("qw", 512), ("qz", 256), ("qf", 128), ("qy", 512)]:
+for _n, _w in [("qa", 256), ("snd", 128), ("ls", 256), ("qx1", 256), ("qx2", 256), ("qx3", 288), ("qx4", 256),
+               ("qs1", 256), ("qs2", 256), ("qs3", 256), ("pa1", 512), ("pa2", 512), ("pa3", 512), ("qe", 1536), ("qc", 128),
+               ("qu", 128), ("qup", 256), ("qv", 128), ("qw", 512), ("qz", 256), ("qf", 256), ("qy", 512)]:
     SCRATCH[_n + "c"] = ("sbuf", [128, _w], CODE)
     SCRATCH[_n + "s"] = ("sbuf", [128, _w], U8)
 for _b in range(8):
     SCRATCH["ps%d" % _b] = ("psum", [128, 512], F32)
 
-SEMAPHORES = (["eV", "eA", "eP", "eG"] + ["d%d" % _i for _i in range(24)] + ["l%d" % _i for _i in range(8)]
-              + ["ap", "ac", "asc", "an1", "an2", "an3", "af1", "af2", "hac", "hasc", "haf1", "haf2"])
+SEMAPHORES = (["eV", "eA", "eP", "eG"] + ["d%d" % _i for _i in range(24)] + ["l%d" % _i for _i in range(12)]
+              + ["ap", "ac", "asc", "an1", "an2", "an3", "ao1", "ao2", "af1", "af2", "hac", "hasc", "haf1", "haf2"])
 
-ORDER = []
-MARGIN, TURNS, ROOM = 0.1, 4, {"V": 0.0, "A": 0.0, "P": 0.2, "G": 0.0, "S": 0.0}
+PLAN = {}
 FARB, FIRSTB, PB = 1, 7, 7
-CASES = [(1.0, 1.0, 1.0, 1.0, 0.22, 1.0), (1.3, 1.4, 1.4, 1.3, 0.22, 1.3)]
-AHEAD = {"s1": 1.0, "s2": 1.0, "os": 1.0, "yt08": 0.8, "qy08": 0.3, "qy12": 0.3, "yt04/2": 0.4, "qx3e/2": 0.4, "lpo": 2.0}
+CASES = [(1.0, 1.0, 1.0, 1.0, 0.22, 1.0), (1.45, 1.45, 1.6, 1.15, 0.22, 1.15), (1.1, 1.15, 1.2, 1.3, 0.3, 1.4)]
+TRIES, STEPS = 200, 330000
+PULL, HEAT, BURST = 0.05, 0.1, 200
 A = AluOpType
 FN = ActivationFunctionType
-CY, PE, WAKE, ROW, START, ISSUE, SLACK = 0.00085, 0.0005, 0.22, 0.018, 0.9, 0.3, 1.0
+CY, PE, WAKE, ROW, START, ISSUE = 0.00085, 0.0005, 0.22, 0.018, 0.9, 0.3
+
+
+def lay_out(ops, before):
+    n, seed = len(ops), [6]
+    q = [o["q"] for o in ops]
+    flex = [len(o["fn"]) > 1 for o in ops]
+
+    def rnd():
+        seed[0] = (seed[0] * 1103515245 + 12345) % 2147483648
+        return (seed[0] + 0.5) / 2147483648
+
+    cases = []
+    for compute, gather, product, remote, wake, first in CASES:
+        cost = [o["c"] * (product if o["q"] == "P" else gather if o["gather"] else 1.0 if o["tok"] else compute) for o in ops]
+        far = [first if o["tok"] == "l0" else remote if o["tok"] else 1.0 for o in ops]
+        cases.append((cost, [[(a, cost[a] + (d and (d - WAKE) * far[a] + wake)) for a, d in before[m]] for m in range(n)],
+                      [cost[m] + ops[m]["lat"] for m in range(n)]))
+    pre = [{a for a, d in before[m]} for m in range(n)]
+
+    def replay(order, case):
+        cost, need, tail = case
+        start, why, free, last, end, at = [0.0] * n, [None] * n, {}, {}, 0.0, 0
+        for m in order:
+            k = q[m]
+            t, w, z = free.get(k, 0.0), last.get(k, -1), True
+            for a, d in need[m]:
+                if start[a] + d > t:
+                    t, w, z = start[a] + d, a, False
+            start[m], why[m], free[k], last[k] = t, (w, z), t + cost[m], m
+            if t + tail[m] > end:
+                end, at = t + tail[m], m
+        return end, start, why, at
+
+    def place(cost, need, after, first, rank, choose):
+        left, start, busy = [len(x) for x in need], [0.0] * n, {k: [] for k in "VAPGS"}
+        ready = sorted((rank[m], m) for m in range(n) if not left[m])
+        while ready:
+            m = ready.pop()[1]
+            r, best = max([first[m]] + [start[a] + cost[a] + d for a, d in need[m]]), None
+            for k in ("AV" if choose and flex[m] else q[m]):
+                line, t = busy[k], r
+                i = len(line)
+                while i and line[i - 1][1] > r:
+                    i -= 1
+                while i < len(line) and line[i][0] < t + cost[m]:
+                    t, i = max(t, line[i][1]), i + 1
+                if best is None or t < best[0] - 0.05:
+                    best = (t, k, i)
+            start[m], q[m] = best[0], best[1]
+            busy[best[1]].insert(best[2], (best[0], best[0] + cost[m]))
+            for f, d in after[m]:
+                left[f] -= 1
+                if not left[f]:
+                    ready.append((rank[f], f))
+                    ready.sort()
+        return start
+
+    views = []
+    for cost, need, tail in cases:
+        need = [[(a, d - cost[a]) for a, d in x] for x in need]
+        after = [[] for m in range(n)]
+        for m in range(n):
+            for a, d in need[m]:
+                after[a].append((m, d))
+        lat, way = [tail[m] - cost[m] for m in range(n)], [0.0] * n
+        for m in reversed(range(n)):
+            way[m] = cost[m] + max([lat[m]] + [d + way[f] for f, d in after[m]])
+        views.append((cost, need, after, lat, way))
+    best, kept, base = None, [0.0] * n, None
+    for it in range(TRIES):
+        cost, need, after, lat, way = views[it % len(views)]
+        bias = [b + (rnd() - 0.5 if rnd() < 0.1 else 0.0) for b in kept]
+        rank = [way[m] + bias[m] for m in range(n)]
+        for turn in range(3):
+            start = place(cost, need, after, [0.0] * n, rank, True)
+            order = sorted(range(n), key=lambda m: (start[m], m))
+            ends = [replay(order, c)[0] for c in cases]
+            base = base or ends
+            v = sum(e / b for e, b in zip(ends, base))
+            if best is None or v < best[0]:
+                best, kept = (v, order, list(q)), bias
+            if turn < 2:
+                back = place(cost, after, need, lat, [start[m] + cost[m] for m in range(n)], False)
+                rank = [back[m] + cost[m] + bias[m] for m in range(n)]
+    order, q[:] = list(best[1]), best[2]
+    best, begun, none = (best[0], list(order), list(q)), [0.0] * n, {k: -1 for k in "VAPGS"}
+    for turn in range(STEPS // BURST):
+        heat = HEAT * 0.04 ** (turn * BURST / STEPS)
+        lo = int(rnd() * (n - 40))
+        hi = min(n, lo + 40 + int(rnd() * 50))
+        inside, view = set(order[lo:hi]), []
+        for cost, need, tail in cases:
+            start, way, head, free = replay(order, (cost, need, tail))[1], list(tail), {}, {k: 0.0 for k in none}
+            for m in reversed(order[hi:]):
+                way[m] = head[q[m]] = max(way[m], cost[m] + head.get(q[m], 0.0))
+                for a, d in need[m]:
+                    way[a] = max(way[a], d + way[m])
+            for m in order[:lo]:
+                free[q[m]] = start[m] + cost[m]
+            rest = max([0.0] + [start[m] + way[m] for m in order[:lo]])
+            first = {m: max([0.0] + [start[a] + d for a, d in need[m] if a not in inside]) for m in inside}
+            view.append((cost, {m: [(a, d) for a, d in need[m] if a in inside] for m in inside}, way, head, free, rest, first))
+
+        def run(part):
+            out, v = [], 0.0
+            for (cost, need, way, head, free, end, first), b in zip(view, base):
+                why, free, last, pull, at = {}, dict(free), dict(none), 0.0, part[-1]
+                for m in part:
+                    k = q[m]
+                    t = free[k]
+                    w = last[k]
+                    if first[m] > t:
+                        t = first[m]
+                        w = -1
+                    for a, d in need[m]:
+                        d += begun[a]
+                        if d > t:
+                            t = d
+                            w = a
+                    begun[m] = t
+                    why[m] = w
+                    free[k] = t + cost[m]
+                    last[k] = m
+                    pull += t
+                    if t + way[m] > end:
+                        end, at = t + way[m], m
+                for k in last:
+                    if last[k] >= 0 and free[k] + head.get(k, 0.0) > end:
+                        end, at = free[k] + head.get(k, 0.0), last[k]
+                out.append((end, why, at))
+                v += (end + PULL * pull / len(part)) / b
+            return v * base[0] / len(base), out
+
+        part = order[lo:hi]
+        now, runs = run(part)
+        for it in range(BURST):
+            r = runs[int(rnd() * len(runs))]
+            m, pairs = r[2] if rnd() < 0.6 else part[int(rnd() * len(part))], []
+            while m >= 0:
+                a = r[1][m]
+                if a >= 0 and a not in pre[m]:
+                    pairs.append((a, m))
+                m = a
+            if not pairs:
+                continue
+            a, b = pairs[int(rnd() * len(pairs))]
+            u, k, flip, new = rnd(), (1, 1, 2, 3, 5, 8)[int(rnd() * 6)], None, part
+            if u < 0.15:
+                flip = a if rnd() < 0.6 else b
+                if not flex[flip]:
+                    continue
+                q[flip] = "V" if q[flip] == "A" else "A"
+            else:
+                m, step = (b, -1) if u < 0.55 else (a, 1)
+                i = j = part.index(m)
+                while 0 <= j + step < len(part) and k:
+                    j += step
+                    k -= q[part[j]] == q[m]
+                along, needs, lines = {m}, set(pre[m]), set()
+                for s in (part[j:i][::-1] if step < 0 else part[i + 1:j + 1]):
+                    if q[s] in lines or (s in needs if step < 0 else pre[s] & along):
+                        along.add(s)
+                        needs |= pre[s]
+                        if q[s] != q[m]:
+                            lines.add(q[s])
+                if part[j] in along:
+                    continue
+                i, j = min(i, j), max(i, j) + 1
+                new = part[:i] + [s for side in (step < 0, step > 0) for s in part[i:j] if (s in along) == side] + part[j:]
+            v, tried = run(new)
+            if v < now - heat * math.log(rnd()):
+                part, runs, now = new, tried, v
+                v = sum(r[0] / b for r, b in zip(runs, base))
+                if v < best[0]:
+                    best = (v, order[:lo] + part + order[hi:], list(q))
+            elif flip is not None:
+                q[flip] = "V" if q[flip] == "A" else "A"
+        order[lo:hi] = part
+        start = replay(order, cases[turn % len(cases)])[1]
+        order.sort(key=lambda m: start[m])
+    q[:] = best[2]
+    PLAN["ends"] = [replay(best[1], c) for c in cases]
+    return best[1], best[2]
 
 
 def rank_program(g, core, T, topo):
@@ -64,7 +246,7 @@ def rank_program(g, core, T, topo):
             return T.lsc[:, 32 * k:32 * k + 32].bitcast(dt.uint8)
         if nm == "asc":
             return T.lss[:, 32 * k:32 * k + 32]
-        return {"af1": T.land1, "af2": T.land2}[nm][:, 16 * ((1 - d) % N):16 * ((1 - d) % N) + 16]
+        return {"af1": T.land1, "af2": T.land2}[nm][:, 40 + 8 * ((6 - d) % N):48 + 8 * ((6 - d) % N)]
 
     def dst(c):
         return DstId(rid=topo.addr(c)[0], pnc=topo.addr(c)[1])
@@ -90,18 +272,20 @@ def rank_program(g, core, T, topo):
                 g.wait_ge(T.sem["l0"], sent)
         return
     Q = {"V": g.vector, "A": g.scalar, "P": g.tensor, "G": g, "S": g.sync}
-    ops, lastw, readers, totals, used, line = [], {}, {}, {}, {"d": 0, "l": 0}, {"on": None, "rd": "/0"}
+    ops, lastw, readers, totals, used, line = [], {}, {}, {}, {"d": 0, "l": 0}, {"on": None}
 
-    def rec(q, fn, r, w, c, tok=None, lat=0.0):
-        op = {"q": q, "fn": fn, "deps": [], "need": False, "tok": tok, "c": c, "lat": lat, "n": len(ops), "after": [], "gather": line.pop("gather", False),
-              "ahead": sum([AHEAD.get(k[:4] + line["rd"], AHEAD.get(k[:4], 0.0) + AHEAD.get(line["rd"], 0.0)) for k in w[:1]])}
+    def rec(q, fn, r, w, c, tok=None, lat=0.0, other=None):
+        op = {"q": q, "fn": {q: fn}, "deps": [], "need": False, "tok": tok, "c": c, "lat": lat, "n": len(ops), "after": [],
+              "gather": line.pop("gather", False), "mark": False, "w": w[:1]}
+        if other:
+            op["fn"]["A" if q == "V" else "V"] = other
         if line["on"]:
             op["after"] = line.get((line["on"], q), [])
             line[(line["on"], q)] = [op]
         for k in r:
             op["deps"].append(lastw[k])
             if k.startswith("ps"):
-                op["deps"].extend(o for o in readers.get(k, []) if o["q"] != q)
+                op["deps"].extend(o for o in readers.get(k, []) if o["q"] != q or other or len(o["fn"]) > 1)
         for k in w:
             if k in lastw:
                 op["deps"].append(lastw[k])
@@ -123,33 +307,29 @@ def rank_program(g, core, T, topo):
         totals[sem] = totals.get(sem, 0) + 16
         return rec(q, lambda: Q[q].dma_start(out, in_).then_inc(T.sem[sem], 16), r, w, 0.1, tok=sem, lat=lat)
 
-    def group(k):
-        prv_, nxt_ = (k - 1) % N, (k + 1) % N
-        return [prv_, nxt_], [o for o in range(N) if o not in (k, prv_, nxt_)], [o for o in range(N) if o != k]
+    prv, nxt = (me - 1) % N, (me + 1) % N
+    near, others = [prv, nxt], [o for o in range(N) if o != me]
 
-    def engines(k, which):
-        m = -1
-        for o in group(k)[which]:
-            m &= topo.mask(T.cores[k], T.cores[o])
-        return m
-
-    def send(src, place, which, rsem, r, key, before=0, hand=None):
-        to, m = group(me)[which], engines(me, which)
-        handed = [(me + d) % N for i, ds in HAND.get(hand or rsem, ()) for d in ds]
-        if rsem in HAND:
-            to = [o for o in to if o not in handed]
+    def send(src, place, to, rsem, r, key, before=0, hand=None, behind=None):
+        m, senders = -1, len(to)
+        for o in to:
+            m &= topo.mask(T.cores[me], T.cores[o])
+        to = [o for o in to if o not in [(me + d) % N for i, ds in HAND.get(rsem, ()) for d in ds]]
         sem = newsem("l")
         trs = [RemoteDMATransfer(dst_ids=[dst(T.cores[o]) for o in to], dma_engine_mask=m, remote_sem=T.sem[rsem], srcs=[src],
                                  dsts=[place(o) for o in to])]
-        if hand in HAND:
+        if hand:
             trs.append(RemoteDMATransfer(dst_ids=[dst(helpers(me)[i]) for i, ds in HAND[hand]], dma_engine_mask=inside(me),
                                          remote_sem=T.sem["h" + hand], srcs=[src], dsts=[handed_ap(hand, me, 0) for i in HAND[hand]]))
-        totals[sem] = ones(m) + (ones(inside(me)) if hand in HAND else 0)
+        totals[sem] = ones(m) + (ones(inside(me)) if hand else 0)
         op = rec("G", lambda: g.remote_dma_fused(trs, local_sem=T.sem[sem]), r + ["gq"], ["gq"], ISSUE, tok=sem,
                  lat=START - ISSUE + ROW * 128 * (len(to) + before) / ones(m))
         op["deps"], op["after"] = op["deps"][:len(r)], op["deps"][len(r):]
-        totals[rsem] = sum(ones(engines(s, which)) for s in group(me)[which])
-        lastw[key] = {"q": "R", "tok": rsem, "like": op}
+        for k in r:
+            if k[:2] == "yt":
+                readers[k].remove(op)
+        totals[rsem] = ones(m) * senders
+        lastw[key] = {"q": "R", "tok": rsem, "like": op, "behind": behind and (behind[0], ROW * 128 * behind[1] / ones(m))}
         return op
 
     def size(n):
@@ -160,8 +340,15 @@ def rank_program(g, core, T, topo):
             return rec("V", lambda: g.vector.tensor_scalar(out, in0, s1, None, o0), r, w, size(n))
         return rec("V", lambda: g.vector.tensor_scalar(out, in0, s1, s2, o0, o1), r, w, size(n))
 
-    def af(out, in0, scale, bias, r, w):
-        return rec("A", lambda: g.scalar.activation(out, in0, FN.Identity, bias=bias, scale=scale), r, w, size(64))
+    def af(out, in0, scale, bias, r, w, n=64):
+        return rec("A", lambda: g.scalar.activation(out, in0, FN.Identity, bias=bias, scale=scale), r, w, size(n),
+                   other=lambda: g.vector.tensor_scalar(out, in0, scale, bias, A.mult, A.add))
+
+    def mv(out, in_, r, w, n=64, scale=None):
+        if scale is None:
+            return rec("A", lambda: g.scalar.activation(out, in_, FN.Copy), r, w, size(n), other=lambda: g.vector.tensor_copy(out, in_))
+        return rec("A", lambda: g.scalar.activation(out, in_, FN.Copy, scale=scale), r, w, size(n),
+                   other=lambda: g.vector.tensor_scalar(out, in_, scale, None, A.mult))
 
     def tt(out, a, b, o, r, w, n=64):
         return rec("V", lambda: g.vector.tensor_tensor(out, a, b, o), r, w, size(n))
@@ -196,41 +383,36 @@ def rank_program(g, core, T, topo):
     def pick(dn, da, sn, sa, sw, off, k, r, w):
         n = 16 * k
         cp(T[dn + "c"][:, da:da + n].bitcast(dt.uint32), T[sn + "c"][:, sa:sa + sw].bitcast(dt.uint32).indirect(off), r, [w + "c"], gat(n))
-        act(T[dn + "s"][:, da:da + n], T[sn + "s"][:, sa:sa + sw].indirect(off), FN.Copy, r, [w + "s"], gat(n))
+        mv(T[dn + "s"][:, da:da + n], T[sn + "s"][:, sa:sa + sw].indirect(off), r, [w + "s"], gat(n))
 
-    def units(name, c0, n, bs=range(4)):
-        return ["%s%02d_%d" % (name, k, b) for k in range(c0 // 32, (c0 + n) // 32) for b in bs]
-
-    prv, nxt = group(me)[0]
-    ff, kk, cc, of, dd = T.ff, T.kk, T.cc, T.of, T.dd
+    ff, kk, cc, of, dd, tb, kb, ti = T.ff, T.kk, T.cc, T.of, T.dd, T.tb, T.kb, T.ti
 
     dma("A", T.landp[:, 16:32], T.p[:], [], ["lpo"], lat=START + 0.5)
     dma("S", T.xin[:], T.x[:], [], ["xin"], lat=START + 1.2)
     dma("S", T.uin[:], T.u[:], ["lpo"], ["uin"], lat=START + 0.5)
 
     lastw["gq"] = rec("G", lambda: g.iota(T.pi[:], [[1, 16]], 0, 1), [], ["pi"], 0.13)
-    EA, EC, UX, SG, LQ, PC, E16, TE = 0, 8, 16, 24, 40, 44, 46, 50
+    EA, EC, UX, SG, PC, E8, L0, L1, L2 = 0, 8, 16, 24, 40, 44, 52, 60, 68
     iota(T.idn[:], [[-1, 128]], 0, 1, ["idn"], 128)
     iota(kk[:, EA:EA + 8], [[0, 4], [1, 2]], 0, 0, ["k0"])
     iota(kk[:, EC:EC + 8], [[0, 2], [1, 2], [0, 2]], 0, 0, ["k1"])
-    iota(kk[:, PC:PC + 1], [[0, 1]], 32, 1, ["p32"])
-    iota(kk[:, E16:E16 + 4], [[16, 2], [0, 2]], 0, 0, ["k2_"])
-    iota(T.vv[:], [[1, 32], [-8, 4]], 0, 0, ["vv"], 128)
+    rec("G", lambda: g.iota(T.i3[:], [[1, 2], [32, 8]], 64, 0), [], ["i3"], 0.16)
+    for t in range(2):
+        iota(T.vv[:, 64 * t:64 * t + 64], [[0, 2], [1, 8], [-8, 4]], 8 * t, 0, ["vv%d" % t], 64)
     iota(kk[:, UX:UX + 8], [[0, 2], [32, 4]], 0, 0, ["k7"])
-    iota(kk[:, LQ:LQ + 4], [[1, 2], [4, 2]], 0, 0, ["k9"])
-    ms(dd[:, 0:3], 0.0, ["dd%d%d" % (a, i) for a in range(4) for i in range(3)])
+    iota(kk[:, L0:L0 + 8], [[16, 2], [2, 2], [4, 2]], 0, 0, ["kl0"])
+    ms(dd[:, 0:2], 0.0, ["dd%d" % a for a in range(4)])
     for a in range(4):
-        dr, dc = DIR[2 * a]
-        for i, c in enumerate((dr, dc, -dr)):
+        for i, c in enumerate(DIR[2 * a]):
             if c:
-                ms(dd[32 * a:32 * a + 32, i:i + 1], float(c), ["dd%d%d" % (a, i)])
-    dks = ["dd%d%d" % (a, i) for a in range(4) for i in range(3)]
-    send(T.landp[:, 16:32], lambda o: T.landp[:, 32:48] if o == prv else T.landp[:, 0:16], 0, "ap", ["lpo"], "lpa", before=PB)
+                ms(dd[32 * a:32 * a + 32, i:i + 1], float(c), ["dd%d" % a])
+    given = send(T.landp[:, 16:32], lambda o: T.landp[:, 32:48] if o == prv else T.landp[:, 0:16], near, "ap", ["lpo"], "lpa", before=PB)
 
-    fields = [[(0, 15, 0, 1, 1, ["q"]), (0, 7, 0, 8, 1, ["r", 1, 2, 3, 4, 5, "r6", "r7"]), (4, 1, 0, 1, 1, ["ch"]),
-               (1, 7, 0, 15, 14, ["q1", "q7"]), (5, 3, 0, 1, 1, ["a"])],
-              [(2, 3, 0, 5, 4, ["k2", "k3"]), (3, 7, 0, 1, 1, ["lo"]), (1, 3, 1, 2, 1, ["k5"]), (3, 1, 0, 1, 1, ["w"])]]
-    col, i = {"p32": kk[:, PC:PC + 1]}, 0
+    fields = [[(0, 15, 0, 1, 1, ["q"]), (0, 7, 0, 3, 2, ["r", "r2"]), (4, 1, 0, 1, 1, ["ch"]), (1, 7, 0, 1, 1, ["q1"]),
+               (5, 3, 0, 1, 1, ["a"]), (3, 1, 0, 1, 1, ["w"]), (0, 1, 0, 1, 1, ["b0"])],
+              [(3, 7, 0, 1, 1, ["lo"]), (0, 3, 0, 4, 1, ["u", "v1", "v2", "z3"]), (1, 3, 0, 1, 1, ["k"]), (2, 3, 0, 1, 1, ["q2"]),
+               (1, 1, 0, 1, 1, ["b1"]), (2, 1, 0, 1, 1, ["k2"])]]
+    col, i = {}, 0
     for part in fields:
         i0, names = i, []
         for sh, an, j0, j1, st, nms in part:
@@ -238,7 +420,7 @@ def rank_program(g, core, T, topo):
             names.append("fi%d" % i)
             for nm in nms:
                 col[nm], i = ff[:, i:i + 1], i + 1
-        cp(ff[:, i0:i], T.fi[:, i0:i], names, [nm for f in part for nm in f[5] if isinstance(nm, str)])
+        cp(ff[:, i0:i], T.fi[:, i0:i], names, [nm for f in part for nm in f[5]])
     taken = [0]
 
     def lin(name, *terms):
@@ -253,22 +435,46 @@ def rank_program(g, core, T, topo):
             else:
                 af(out, col[nm], float(f), rest, [nm] + keys, [name])
             rest, keys = out, [name]
-        return out
+        return name
 
-    O_SP, O_R0, O_LC, O_FM, O_CP, O_OP, O_LQ, O_U, O_SG, O_R, O_RI, O_CQ, O_L, O_S = 0, 2, 6, 40, 120, 46, 48, 52, 68, 84, 92, 96, 100, 104
-    for i in range(2):
-        ts(of[:, O_SP + i:O_SP + i + 1], col["q"], 8.0, 128.0 * i, A.mult, A.add, ["q"], ["osp%d" % i])
+    places = {}
 
+    def listed(name, n):
+        a = sum(x[1] + x[1] % 2 for x in places.values())
+        places[name] = (a, n)
+        return of[:, a:a + n]
+
+    def lst(name, a=0, b=None):
+        return of[:, places[name][0] + a:places[name][0] + (places[name][1] if b is None else b)]
+
+    def row_list(name, n, row, f, c, keys):
+        ts(listed(name, n), row, float(f), col[c], A.mult, A.add, keys + [c], [name])
+
+    ms(T.sx[:, 128:512], 0.0, ["sxz"], 192)
+    for b in range(4):
+        mv(T.sx[:, b:128:4], T.xin[:, b:1024:32], ["xin"], ["sx%d" % b])
+    qz("snd", 0, 128, T.sx[:], ["sx0", "sx1", "sx2", "sx3", "sxz"], ["snd"])
+    for nm in ("ac", "asc"):
+        src = T.snds[:, 0:32] if nm == "asc" else T.sndc[:, 0:32].bitcast(dt.uint8)
+        lastw["gone" + nm[1:-1]] = send(src, lambda o: handed_ap(nm, me, 0), others, nm, ["snd"], "l" + nm, before=FIRSTB, hand=nm, behind=(given, 9))
+    row_list("own", 2, kk[:, EA:EA + 2], 16, "q", ["k0"])
+    pick("ls", 32 * me, "snd", 0, 128, lst("own"), 2, ["snd", "own"], "lso")
     qz("qa", 0, 256, T.xin[:], ["xin"], ["qa"])
-    osp = of[:, O_SP:O_SP + 2]
-    pick("snd", 0, "qa", 0, 256, osp, 2, ["qa", "osp0", "osp1"], "snd")
-    for nm in [m for m in HAND if m in ("ac", "asc")]:
-        src, key = (T.snds[:], "snds") if nm == "asc" else (T.sndc[:].bitcast(dt.uint8), "sndc")
-        lastw["sent"] = send(src, lambda o: handed_ap(nm, me, 0), 2, nm, [key], "ls" + nm[0:3:2], before=FIRSTB, hand=nm)
-    pick("ls", 32 * me, "qa", 0, 256, osp, 2, ["qa", "osp0", "osp1"], "lso")
-    for o in [iota(kk[:, SG:SG + 16], [[1, 4], [64, 4]], 0, 0, ["k8"]), iota(kk[:, TE:TE + 16], [[0, 2], [32, 4], [1, 2]], 0, 0, ["k3_"]),
-              iota(T.w2[:, 0:6], [[0, 3], [32, 2]], 0, 0, ["w2a"]), iota(T.w2[:, 6:14], [[0, 2], [32, 2], [0, 2]], 0, 0, ["w2b"])]:
-        o["after"] = [lastw["sent"]]
+    lsk = ["lsoc", "lsos", "lac", "lasc"]
+    for o in [iota(kk[:, SG:SG + 16], [[1, 8], [128, 2]], 0, 0, ["k8"], 16), iota(kk[:, PC:PC + 1], [[0, 1]], 32, 1, ["p32"]),
+              iota(kk[:, E8:E8 + 8], [[1, 2], [0, 4]], 0, 0, ["ke8"]),
+              iota(kk[:, L1:L1 + 8], [[4, 2], [1, 2], [2, 2]], 0, 0, ["kl1"]), iota(kk[:, L2:L2 + 8], [[2, 2], [16, 2], [1, 2]], 0, 0, ["kl2"]),
+              iota(kb[:, 4:20], [[0, 4], [1, 2], [0, 2]], 0, 0, ["kb0"], 16), iota(kb[:, 20:28], [[1, 2], [-80, 2], [0, 2]], 88, 0, ["kb1"]),
+              iota(kb[:, 28:32], [[1, 2], [0, 2]], 0, 0, ["kb2"]), iota(kb[:, 32:40], [[0, 8]], 0, 0, ["kb3"]),
+              iota(kb[:, 34:38], [[32, 2], [1, 2]], 0, 0, ["kb3"]), iota(kb[:, 0:4], [[32, 2], [1, 2]], 0, 0, ["kb4"]),
+              iota(T.fl[:, 0:256], [[0, 256]], 0, 0, ["fl00", "fl01"], 256), iota(T.fl[:, 256:512], [[0, 256]], 0, 0, ["flz"], 256),
+              iota(T.fl[:, 512:768], [[0, 256]], 0, 0, ["fl10", "fl11"], 256), iota(T.lq[:, 128:136], [[0, 8]], 0, 0, ["lqz"]),
+              iota(T.land1[:, 24:40], [[0, 16]], 0, 0, ["land1z"], 16), iota(T.land2[:, 24:40], [[0, 16]], 0, 0, ["land2z"], 16),
+              iota(T.po[:, 16:32], [[0, 16]], 0, 0, ["poz"], 16),
+              iota(T.w2[:, 0:4], [[0, 2], [32, 2]], 0, 0, ["w2a"]), iota(T.w2[:, 4:8], [[32, 2], [0, 2]], 0, 0, ["w2b"]),
+              iota(T.w2[:, 12:20], [[0, 2], [16, 2], [0, 2]], 16, 0, ["w2c"])]:
+        o["after"], lastw["gq"] = [lastw["gq"]], o
+    col["p32"] = kk[:, PC:PC + 1]
 
     ms(T.ez[:], 0.0, ["ez"], 260)
     ts(T.idn[:], T.idn[:], 0.0, None, A.is_equal, None, ["idn"], ["idn"])
@@ -279,269 +485,326 @@ def rank_program(g, core, T, topo):
         for b in range(4):
             qz("qe", 512 * v + 128 * b, 128, T.ez[:, 3 - b:515 - b], ["ez"], ["qe%d%d" % (v, b)])
 
+    ts(T.i3[:], T.i3[:], 255, None, A.bitwise_and, None, ["i3"], ["i3"])
+    row_list("oeo", 16, T.i3[:], 1, lin("q2x", (2, "q"), 0.0), ["i3"])
+    pick("qx1", 0, "qa", 0, 256, lst("oeo"), 16, ["qa", "oeo"], "qx1")
+
     for i, nm in enumerate(["dr", "dc", "ndr"]):
         col[nm] = dd[:, i:i + 1]
-    af(dd[:, 10:14], kk[:, EC:EC + 4], col["ndr"], col["dc"], ["k1"] + dks, ["dcl", "dr", "dc", "ndr"])
+    dcl, drt, dra, dcm, dr8, dc8, dl8 = dd[:, 4:8], dd[:, 8:12], dd[:, 12:16], dd[:, 16:18], dd[:, 20:28], dd[:, 28:36], dd[:, 36:44]
+    af(col["ndr"], col["dr"], -1.0, 0.0, ["dd%d" % a for a in range(4)], ["ndr", "dr", "dc"])
+    af(dcl, kk[:, EC:EC + 4], col["ndr"], col["dc"], ["k1", "dr"], ["dcl"])
     lin("rg", ("dc", "ch"), "dr")
-    lin("r2", (2, "r"), 16.0)
-    ts(of[:, O_R0:O_R0 + 4], kk[:, EC:EC + 4], lin("r0c", (8, "rg"), "r2"), None, A.add, None, ["k1", "r0c"], ["or0"])
+    row_list("or0", 4, kk[:, EC:EC + 4], 1, lin("rb", (8, "rg"), (2, "r2"), (48, "w"), 16.0), ["k1"])
 
-    af(T.w1[:, 0:4], dd[:, 10:14], float(STRIDE[0]), col["p32"], ["dcl", "p32"], ["w1a"])
-    af(T.w1[:, 4:5], col["a"], -8.0, lin("j8", (8, "q1"), 32.0), ["a", "j8"], ["w1b"])
+    af(T.w1[:, 0:4], dcl, 4.0, col[lin("c2", (1, "ch"), (1, "q2x"), 32.0)], ["dcl", "c2"], ["w1a"])
+    af(T.w1[:, 4:5], col["a"], -8.0, col[lin("j8", (8, "q1"), 32.0)], ["a", "j8"], ["w1b"])
     cp(T.i1[:, 0:5], T.w1[:, 0:5], ["w1a", "w1b"], ["i1"])
     ts(T.i1[:, 0:5], T.i1[:, 0:5], 31, None, A.bitwise_and, None, ["i1"], ["i1"])
     ts(T.i2[:, 0:4], T.i1[:, 0:4], 16, None, A.bitwise_and, None, ["i1"], ["i2"])
-    tt(T.w3[:, 4:8], kk[:, E16:E16 + 4], T.i1[:, 0:4], A.add, ["k2_", "i1"], ["w3"])
-    tt(T.w3[:, 4:8], T.w3[:, 4:8], T.i2[:, 0:4], A.add, ["w3", "i2"], ["w3"])
-    cp(of[:, O_LC:O_LC + 4], T.w3[:, 4:8], ["w3"], ["ol0"])
-    lin("b0", (-2, "q1"), "q")
-    ts(of[:, O_FM:O_FM + 4], kk[:, LQ:LQ + 4], 8.0, lin("fm", (16, "b0"), "q1"), A.mult, A.add, ["k9", "fm"], ["ofm"])
-
-    def cand_lists(x):
-        rot, rn = T["rot%d" % x], "rot%d" % x
-        o = O_LC + (6 + 4 * x if x else 0)
-        act(T.a3[:], T.gg[:].indirect(of[:, o:o + 4]), FN.Copy, ["gg", "oc" if x else "ol0"], ["a3"], gat(64))
-        tp(rot[:, 0:64], T.a3[:], ["a3"], [rn, rn + "l"])
-        cp(T.ol[:], rot[:, 0:64].indirect(of[:, O_FM + 2:O_FM + 4]), [rn + "l", "ofm"], ["ol"], gat(32))
-
-    def relabel(src, n, out, rkey, wkey, back):
-        s, step = slice(0, n), 64.0 if back else 4.0
-        big = 1.5 * 2.0 ** 23 * step
-        ts(T.p1[:, s], src, 0.5 - step / 2, big, A.add, A.add, [rkey], ["p1"])
-        ts(T.p2[:, s], T.p1[:, s], -big, -255.0 / step, A.add, A.mult, ["p1"], ["p2"])
-        af(T.p3[:, s], src, 256.0 / step, 0.0, [rkey], ["p3"])
-        tt(out, T.p2[:, s], T.p3[:, s], A.add, ["p2", "p3"], [wkey], 2 * n)
+    af(T.w1[:, 40:44], kk[:, EC:EC + 4], 16.0, 0.0, ["k1"], ["e16"])
+    tt(T.w1[:, 40:44], T.w1[:, 40:44], T.i1[:, 0:4], A.add, ["e16", "i1"], ["e16"])
+    tt(T.w1[:, 40:44], T.w1[:, 40:44], T.i2[:, 0:4], A.add, ["e16", "i2"], ["e16"])
+    cp(listed("oc0", 4), T.w1[:, 40:44], ["e16"], ["oc0"])
+    row_list("ol0", 2, kk[:, EA:EA + 2], 32, lin("f0", (16, "w"), "r"), ["k0"])
+    col["jb"] = T.w1[:, 44:45]
+    cp(col["jb"], T.i1[:, 4:5], ["i1"], ["jb"])
+    lin("lb", (8, "jb"), (32, "b0"), 0.0)
+    row_list("lq0", 8, kk[:, L0:L0 + 8], 1, lin("lb0", (1, "ch"), (1, "lb"), 8.0), ["kl0"])
 
     def spread(x):
-        rot, rn, sem, s = T["rot%d" % x], "rot%d" % x, newsem("d"), 0 if x else 64
+        rot, rn, sem, n = T["rot%d" % x], "rot%d" % x, newsem("d"), 128 if x == 2 else 64
         for j in range(1, 4):
-            c0 = s + 64 * j
-            dma("S", rot[0:128 - 32 * j, c0:c0 + 64], rot[32 * j:128, s:s + 64], [rn], [rn + "j%d" % j], sem, lat=START + 1.0)
-            dma("S", rot[128 - 32 * j:128, c0:c0 + 64], rot[0:32 * j, s:s + 64], [rn], [rn + "k%d" % j], sem, lat=START + 1.0)
-
-    def steps_of(x):
-        rot, rn = T["rot%d" % x], "rot%d" % x
+            dma("S", rot[0:128 - 32 * j, n * j:n * j + n], rot[32 * j:128, 0:n], [rn, "gone"], [rn + "j%d" % j], sem, lat=START + 1.2)
+            dma("S" if x else "A", rot[128 - 32 * j:128, n * j:n * j + n], rot[0:32 * j, 0:n], [rn, "gone"], [rn + "k%d" % j], sem, lat=START + 1.2)
         keys = [rn + jk + str(j) for jk in "jk" for j in range(1, 4)]
-        act(T.lq[:, 0:64], rot[:, (0 if x else 64):(256 if x else 320)].indirect(of[:, O_LQ:O_LQ + 4]), FN.Copy, [rn, "olq"] + keys, ["lq"], gat(64))
-        tt(T.df[:, 0:64], T.lq[:, 0:64], T.lq[:, 1:65], A.subtract, ["lq", "lqz"], ["df0"], 128)
-        act(T.df[:, 7:64:8], T.lq[:, 7:64:8], FN.Copy, ["lq"], ["df0"])
-        act(T.df[:, 64:128], T.df[:, 0:64], FN.Copy, ["df0"], ["df1"])
+        mv(T.lq[:, 0:128], rot[:].indirect(lst("lq%d" % x)), [rn, "lq%d" % x] + keys, ["lq"], gat(128))
+        tt(T.df[:], T.lq[:, 0:128], T.lq[:, 1:129], A.subtract, ["lq", "lqz"], ["df"], 256)
+        if x:
+            mv(T.df[:, 7:128:8], T.lq[:, 7:128:8], ["lq"], ["df"])
 
-    lin("l2", (32, "b0"), (2, "w"), (16, "ch"), 8.0)
-    ts(T.w3[:, 0:1], T.i1[:, 4:5], 8.0, col["l2"], A.mult, A.add, ["i1", "l2"], ["l1"])
-    ts(of[:, O_LQ:O_LQ + 4], kk[:, LQ:LQ + 4], T.w3[:, 0:1], None, A.add, None, ["k9", "l1"], ["olq"])
-    ms(T.lq[:, 64:72], 0.0, ["lqz"])
-
-    cp(T.a1[:], T.landp[:].indirect(of[:, O_R0:O_R0 + 4]), ["lpo", "lpa", "or0"], ["a1"], gat(64))
-    tp(T.gg[:], T.a1[:], ["a1"], ["gg"])
-    cand_lists(0)
-    relabel(T.rot0[:, 0:64], 64, T.rot0[:, 64:128], "rot0l", "rot0", False)
+    ts(T.landp[:, 48:96], T.landp[:, 0:48], 257.0, None, A.mult, None, ["lpo", "lpa"], ["lpr"])
+    ts(T.landp[:, 48:96], T.landp[:, 48:96], 3, 255, A.logical_shift_right, A.bitwise_and, ["lpr"], ["lpr"])
+    cp(T.a1[:, 0:64], T.landp[:].indirect(lst("or0")), ["lpr", "or0"], ["a10"], gat(64))
+    tp(T.gg[:, 0:64], T.a1[:, 0:64], ["a10"], ["gg0"])
+    mv(T.a3[:, 0:64], T.gg[:, 0:64].indirect(lst("oc0")), ["gg0", "oc0"], ["a3"], gat(64))
+    tp(T.rot0[:, 0:64], T.a3[:, 0:64], ["a3"], ["rot0"])
+    cp(T.ol[:, 0:32], T.rot0[:, 0:64].indirect(lst("ol0")), ["rot0", "ol0"], ["cand0"], gat(32))
     spread(0)
-    dma("S", T.qwc[:].bitcast(dt.uint8), T.wc[:], ["sent", "rot0"], ["qwc"], lat=START + 1.0)
-    dma("S", T.qws[:], T.ws[:], ["sent", "rot0"], ["qws"], lat=START + 1.2)
-    dma("S", T.vin[:], T.v[:], ["sent", "rot0"], ["vin"], lat=START + 1.7)
+    for o in [dma("S", T.qwc[:].bitcast(dt.uint8), T.wc[:], lsk, ["qwc"], lat=START + 2.0),
+              dma("S", T.qws[:], T.ws[:], lsk, ["qws"], lat=START + 2.0)]:
+        o["after"] = [lastw["rot0" + jk + str(j)] for jk in "jk" for j in range(1, 4)]
 
     val = cc[:, 63:64]
     ts(val, col["r"], col["lo"], None, A.is_gt, None, ["r", "lo"], ["val"])
     qz("qu", 0, 128, T.uin[:], ["uin"], ["qu"])
-    ts(of[:, O_U:O_U + 8], kk[:, UX:UX + 8], lin("ux", (16, "w"), 0.0), None, A.add, None, ["k7", "ux"], ["ou0"])
-    ts(of[:, O_U + 8:O_U + 16], kk[:, UX:UX + 8], 0.0, lin("uy", (16, "r"), 0.0), A.mult, A.add, ["k7", "uy"], ["ou1"])
-    pick("qup", 0, "qu", 0, 128, of[:, O_U:O_U + 16], 16, ["qu", "ou0", "ou1"], "qup")
-    ts(T.va[:], T.vv[:], col["r"], None, A.is_equal, None, ["vv", "r"], ["va"])
-    ts(T.vb[:], T.vv[:], col["lo"], None, A.is_equal, None, ["vv", "lo"], ["vb"])
+    row_list("ou0", 8, kk[:, UX:UX + 8], 1, lin("ux", (16, "w"), 0.0), ["k7"])
+    row_list("ou1", 8, kk[:, UX:UX + 8], 0, lin("uy", (16, "r"), 0.0), ["k7"])
+    pick("qup", 0, "qu", 0, 128, lst("ou0", 0, 16), 16, ["qu", "ou0", "ou1"], "qup")
+    ts(T.va[:], T.vv[:], col["r"], None, A.is_equal, None, ["vv0", "vv1", "r"], ["va"])
+    ts(T.vb[:], T.vv[:], col["lo"], None, A.is_equal, None, ["vv0", "vv1", "lo"], ["vb"])
     tt(T.va[:], T.va[:], T.vb[:], A.subtract, ["va", "vb"], ["va"], 256)
     for a in range(4):
         act(T.cb[:, 128 * a:128 * a + 128], T.va[:], FN.Identity, ["va", "val"], ["cb%d" % a], 128, scale=val)
     qz("qc", 0, 128, T.cb[:], ["cb0", "cb1", "cb2", "cb3"], ["qc"])
-    ms(T.fl[:, 256:512], 0.0, ["flz"], 128)
-    lin("tg0", (2, "r"), (4, "a"), -14.0)
-    lin("tg1", (1, "tg0"), 2.0)
-    ts(of[:, O_SG:O_SG + 16], kk[:, SG:SG + 16], lin("q4", (4, "q"), 0.0), None, A.add, None, ["k8", "q4"], ["osg"])
-    lin("cpb", (64, "b0"), (32, "q1"), (-64, "k2"), 7.0)
-    for x, nm in enumerate(["k2", "k3"]):
-        ts(of[:, O_CP + 2 * x:O_CP + 2 * x + 1], col[nm], 8.0, col["cpb"], A.mult, A.add, [nm, "cpb"], ["ocp%d" % x])
+    lin("tg", (2, "r"), (4, "a"), (2, "w"), -14.0)
+    row_list("osg", 16, kk[:, SG:SG + 16], 1, lin("q8", (8, "q"), 0.0), ["k8"])
 
-    af(dd[:, 4:8], kk[:, EC:EC + 4], col["dc"], col["dr"], ["k1", "dr"], ["drt"])
-    af(dd[:, 14:22], kk[:, EA:EA + 8], col["dc"], col["dr"], ["k0", "dr"], ["dra"])
-    lin("qq", (2, "q"), float(2 * (72 - 8 * me)))
-    for x, (now, then) in enumerate([("r", "r6"), ("r6", "r7")]):
-        h, h2 = STRIDE[x], STRIDE[x + 1]
-        lin("dw%d" % x, (-1, now), then)
-        lin("rw%d" % x, ("w", "dw%d" % x), now)
-        lin("hw%d" % x, (h2 - h, "w"), float(h))
-        af(T.w3[:, 12 + 4 * x:16 + 4 * x], dd[:, 4:8], col["hw%d" % x], col["rw%d" % x], ["drt", "hw%d" % x, "rw%d" % x], ["ra%d" % x])
-        af(T.w3[:, 24 + 8 * x:32 + 8 * x], dd[:, 14:22], 2.0 * h, col["qq"], ["dra", "qq"], ["sa%d" % x])
-    af(T.w3[:, 40:48], kk[:, EC:EC + 8], 0.5, 0.0, ["k1"], ["eh"])
-    tt(T.w3[:, 12:20], T.w3[:, 12:20], T.w3[:, 40:48], A.add, ["ra0", "ra1", "eh"], ["ra"])
-    ts(of[:, O_R:O_R + 8], T.w3[:, 12:20], 2.0, 16.0, A.mult, A.add, ["ra"], ["or"])
-    ts(of[:, O_RI:O_RI + 4], T.w3[:, 16:20], 2.0, 15.0, A.mult, A.min, ["ra"], ["ori"])
-    tt(T.i3[:], T.w3[:, 24:40], kk[:, TE:TE + 16], A.add, ["sa0", "sa1", "k3_"], ["i3"])
-    ts(T.i3[:], T.i3[:], 127, None, A.bitwise_and, None, ["i3"], ["i3"])
-    cp(of[:, O_S:O_S + 16], T.i3[:], ["i3"], ["os_"])
-    af(dd[:, 8:10], kk[:, EA:EA + 2], col["ndr"], col["dc"], ["k0", "dr"], ["dcm"])
+    af(drt, kk[:, EC:EC + 4], col["dc"], col["dr"], ["k1", "dr"], ["drt"])
+    af(dra, kk[:, EA:EA + 4], col["dc"], col["dr"], ["k0", "dr"], ["dra"])
+    af(dr8, kk[:, E8:E8 + 8], col["dc"], col["dr"], ["ke8", "dr"], ["dr8"])
+    ts(dd[:, 36:44:2], dd[:, 20:28:2], 0.0, None, A.min, None, ["dr8"], ["dl0"])
+    ts(dd[:, 37:44:2], dd[:, 21:28:2], 0.0, None, A.max, None, ["dr8", "dl0"], ["dl1"])
+    lin("sw", (-1, "w"), 2.0)
+    lin("sw2", (-2, "w"), 4.0)
+    lin("u4", (1, "u"), 4.0)
+    lin("q3", (1, "q"), 3.0)
+    lin("ve", (2, "v1"), 8.0)
+    lin("vc", (-80, "k2"), (1, "ve"), 80.0)
+    lin("km", (-2, "k2"), 2.0)
+    lin("vn", (-1, "ve"), 24.0)
+    lin("vm", ("k2", "vn"), "ve")
+    lin("vs", (1, "q2x"), float(112 - 8 * me))
+    lin("z6", (2, "z3"), 0.0)
+    lin("u6", (1, "u"), 6.0)
+    lin("ij", (1, "q1"), (1, "rg"), 1.0)
+    rows = [[(0, dra, "dra", 2, "q3", 4, "vs"), (4, drt, "drt", "sw", "u4", "sw2", "vc"), (8, drt, "drt", 2, "u4", 4, "ve"), (12,)],
+            [(12, drt, "drt", 1, "u4", "km", "vm"), (16, drt, "drt", 1, "u4", 2, "ve"), (20, dl8, "dl1", 1, "u6", 2, "z6"),
+             (28, drt, "drt", 1, "u4", 0, 0.0), (32, col["r2"], "r2", 1, 0.0, 2, "w"),
+             (33, col["rg"], "rg", 1, lin("b11", (1, "b1"), 1.0), 0, 0.0), (34, dra, "dra", 1, "q3", 2, "vs"),
+             (38, col["ij"], "ij", 1, 0.0, 8, 0.0), (39,)]]
+    for z, masks in (("0", ((40, 44, 57), (44, 52, 249))), ("1", ((52, 74, 249), (74, 78, 57), (78, 79, 32)))):
+        part, keys = rows[int(z)], [[], []]
+        for (c0, src, name, f0, c1, f1, c2), then in zip(part, part[1:]):
+            for side, f, c in ((0, f0, c1), (1, f1, c2)):
+                keys[side].append("tb%d" % (40 * side + c0))
+                af(tb[:, 40 * side + c0:40 * side + then[0]], src, col[f] if f in col else float(f), col.get(c, c),
+                   [name] + [y for y in (f, c) if y in col], keys[side][-1:])
+        a, b, tv = part[0][0], part[-1][0], ["tv%d" % m[0] for m in masks]
+        cp(ti[:, a:b], tb[:, a:b], keys[0], ["tu" + z])
+        tt(ti[:, 40 + a:40 + b], tb[:, 40 + a:40 + b], kb[:, a:b], A.add, keys[1] + ["kb0", "kb1", "kb2", "kb3", "kb4"], tv)
+        ts(ti[:, a:b], ti[:, a:b], 3, None, A.bitwise_and, None, ["tu" + z], ["tu" + z])
+        ts(ti[:, a:b], ti[:, a:b], 5.0, None, A.mult, None, ["tu" + z], ["tu" + z])
+        ts(ti[:, a:b], ti[:, a:b], 6, None, A.bitwise_and, None, ["tu" + z], ["tu" + z])
+        for (c0, c1, m), key in zip(masks, tv):
+            ts(ti[:, c0:c1], ti[:, c0:c1], m, None, A.bitwise_and, None, [key], [key])
+        tt(tb[:, a:b], ti[:, a:b], ti[:, 40 + a:40 + b], A.add, ["tu" + z] + tv, ["tr" + z] + keys[0])
+    for x in range(2):
+        ts(listed("osr%d" % x, 4), tb[:, 34 * x:34 * x + 4], 8.0, None, A.add, None, ["tr%d" % x], ["osr%d" % x])
+        cp(listed("orow%d" % x, 8 + 8 * x), tb[:, 4 + 8 * x:12 + 16 * x], ["tr%d" % x], ["orow%d" % x])
+    ts(listed("osc", 5), tb[:, 28:33], 8.0, 7.0, A.mult, A.add, ["tr1"], ["osc"])
+    ts(listed("oj", 1), tb[:, 38:39], col[lin("b16", (16, "b0"), 0.0)], None, A.add, None, ["tr1", "b16"], ["oj"])
+    col["out"] = cc[:, 62:63]
+    act(col["out"], col["rg"], FN.Relu, ["rg", lin("sg", (-2, "b1"), 1.0)], ["out"], scale=col["sg"])
+    lin("kf", (-32, "b1"), -32.0)
+    lin("kc", (1, "b16"), 64.0)
+    ts(listed("ok", 1), tb[:, 33:34], col[lin("ks", ("kf", "out"), "kc")], None, A.add, None, ["tr1", "ks"], ["ok"])
+    row_list("og3", 4, kk[:, EC:EC + 4], 8, lin("k16", (16, "k"), 7.0), ["k1"])
+    lin("fm", (1, "q1"), "b16")
+    cp(listed("ofm", 1), col["fm"], ["fm"], ["ofm"])
+    row_list("ol1", 2, kk[:, EA:EA + 2], 32, lin("fm8", (1, "fm"), 8.0), ["k0"])
+    row_list("ol2", 2, kk[:, EA:EA + 2], 64, lin("f3", (32, "b0"), (16, "b1"), "q2"), ["k0"])
+    lin("c16", (16, "ch"), 0.0)
+    row_list("lq1", 8, kk[:, L1:L1 + 8], 1, lin("lb1", (1, "lb"), (1, "c16"), 8.0), ["kl1"])
+    row_list("lq2", 8, kk[:, L2:L2 + 8], 1, lin("lb2", (2, "lb1"), -16.0), ["kl2"])
+
+    af(dcm, kk[:, EA:EA + 2], col["ndr"], col["dc"], ["k0", "dr"], ["dcm"])
+    af(dc8, kk[:, E8:E8 + 8], col["ndr"], col["dc"], ["ke8", "dr"], ["dc8"])
     lin("cg", ("ndr", "ch"), "dc")
-    lin("t8", (8, "k2"), 32.0)
-    lin("t32", (32, "q"), (-128, "k2"), 0.0)
-    for x, h in enumerate(STRIDE):
-        af(T.w1[:, 8 + 2 * x:10 + 2 * x], dd[:, 8:10], float(h), col["p32"], ["dcm", "p32"], ["w1m%d" % x])
-        if x:
-            af(T.w1[:, 10 + 4 * x:14 + 4 * x], dd[:, 10:14], float(h), col["p32"], ["dcl", "p32"], ["w1l%d" % x])
-    af(T.w1[:, 22:25], kk[:, E16 + 1:E16 + 4], (STRIDE[1] - STRIDE[0]) / 16, float(STRIDE[0]), ["k2_"], ["hs"])
-    af(T.w1[:, 22:25], T.w1[:, 22:25], col["cg"], col["t8"], ["hs", "cg", "t8"], ["hs"])
-    af(T.w2[:, 14:17], kk[:, EA:EA + 3], 0.0, col["t32"], ["k0", "t32"], ["w2c"])
-    cp(T.i1[:, 8:25], T.w1[:, 8:25], ["w1m0", "w1m1", "w1m2", "w1l1", "w1l2", "hs"], ["i4"])
-    ts(T.i1[:, 8:25], T.i1[:, 8:25], 31, None, A.bitwise_and, None, ["i4"], ["i4"])
-    tt(T.w1[:, 8:25], T.w2[:, 0:17], T.i1[:, 8:25], A.add, ["w2a", "w2b", "w2c", "i4"], ["w4"])
-    cp(of[:, O_LC + 4:O_LC + 21], T.w1[:, 8:25], ["w4"], ["oc"])
-    lin("cq", (-32, "b0"), (8, "k5"), 39.0)
-    ts(of[:, O_CQ:O_CQ + 4], kk[:, EC:EC + 4], 64.0, col["cq"], A.mult, A.add, ["k1", "cq"], ["ocq"])
-    ts(of[:, O_OP:O_OP + 1], col["w"], 64.0, col["cq"], A.mult, A.add, ["w", "cq"], ["oop"])
-    lin("row", (STRIDE[2], "rg"), "q7")
-    lin("b16", (16, "b0"), 32.0)
-    lin("lx", (25, "row"), "b16")
-    ts(T.w3[:, 20:21], col["row"], 0.0, 7.0, A.max, A.min, ["row"], ["in7"])
-    ts(of[:, O_L:O_L + 1], T.w3[:, 20:21], -24.0, col["lx"], A.mult, A.add, ["in7", "lx"], ["oll"])
-    ts(of[:, O_L + 2:O_L + 3], T.w3[:, 20:21], col["b16"], -32.0, A.add, A.add, ["in7", "b16"], ["oli"])
-    ms(T.po[:, 16:32], 0.0, ["poz"])
-    qz("qv", 0, 128, T.vin[:], ["vin"], ["qv"])
+    lin("q16", (1, "q"), 16.0)
+    lin("k4", (4, "k"), 16.0)
+    for at, n, src, f, c in [(8, 2, dcm, 2, "q16"), (10, 2, dcm, 1, "q16"), (12, 4, dcl, 1, "q16"), (16, 1, col["cg"], 2, "k4"),
+                             (17, 1, col["cg"], 1, "k4"), (18, 2, dcm, 1, "p32"), (20, 8, dc8, 1, "q16")]:
+        af(T.w1[:, at:at + n], src, float(f), col[c], [{2: "dcm", 4: "dcl", 1: "cg", 8: "dc8"}[n], c], ["w1%d" % at])
+    tt(T.w1[:, 20:28], T.w1[:, 20:28], T.w2[:, 12:20], A.add, ["w120", "w2c"], ["w120"])
+    cp(T.i1[:, 8:18], T.w1[:, 8:18], ["w1%d" % at for at in (8, 10, 12, 16, 17)], ["i15"])
+    cp(T.i1[:, 18:28], T.w1[:, 18:28], ["w118", "w120"], ["i31"])
+    ts(T.i1[:, 8:18], T.i1[:, 8:18], 15, None, A.bitwise_and, None, ["i15"], ["i15"])
+    ts(T.i1[:, 18:28], T.i1[:, 18:28], 31, None, A.bitwise_and, None, ["i31"], ["i31"])
+    tt(T.w2[:, 20:28], T.w2[:, 0:8], T.i1[:, 8:16], A.add, ["w2a", "w2b", "i15"], ["w2m"])
+    ts(listed("ocol", 8), T.w2[:, 20:28], col["c16"], None, A.add, None, ["w2m", "c16"], ["ocol"])
+    lin("sb", (32, "b0"), "ux")
+    for x in range(2):
+        ts(listed("osd%d" % x, 1), T.i1[:, 16 + x:17 + x], col["sb"], None, A.add, None, ["i15", "sb"], ["osd%d" % x])
+    tt(T.w2[:, 28:30], T.w2[:, 0:2], T.i1[:, 18:20], A.add, ["w2a", "i31"], ["w2n"])
+    cp(listed("oc3", 2), T.w2[:, 28:30], ["w2n"], ["oc3"])
+    ts(T.i2[:, 8:16], T.i1[:, 20:28], 65.0, None, A.mult, None, ["i31"], ["i65"])
+    ts(T.i2[:, 8:16], T.i2[:, 8:16], 1, 47, A.logical_shift_right, A.bitwise_and, ["i65"], ["i65"])
+    act(T.w2[:, 32:40], dr8, FN.Abs, ["dr8"], ["nz"])
+    af(T.w2[:, 32:40], T.w2[:, 32:40], col[lin("nx", (-32, "ch"), 16.0)], col["c16"], ["nz", "nx", "c16"], ["nz"])
+    af(T.w2[:, 40:48], kk[:, E8:E8 + 8], 64.0, 0.0, ["ke8"], ["e64"])
+    tt(T.w2[:, 32:40], T.w2[:, 32:40], T.w2[:, 40:48], A.add, ["nz", "e64"], ["nz"])
+    tt(T.w2[:, 32:40], T.w2[:, 32:40], T.i2[:, 8:16], A.add, ["nz", "i65"], ["nz"])
+    cp(listed("ocl3", 8), T.w2[:, 32:40], ["nz"], ["ocl3"])
 
-    def unpack(bank, src, to, names, c0=0, n=256):
+    def unpack(src, n, keys, to, width, name):
         for b in range(4):
-            mm(bank + b, n, "qe", 128 * b, src[0], src[1] + c0, True, True, ["qe0%d" % b] + src[2])
+            mm(4 + b, n, "qe", 128 * b, src, 0, True, True, ["qe0%d" % b] + keys)
         for b in range(4):
-            act(to[:, 256 * b + c0:256 * b + c0 + n], T["ps%d" % (bank + b)][:, 0:n], FN.Copy, ["ps%d" % (bank + b)],
-                ["%s%d" % (k, b) for k in names], n)
+            mv(to[:, width * b:width * b + n], T["ps%d" % (4 + b)][:, 0:n], ["ps%d" % (4 + b)], [name + str(b)], n)
 
-    def chunk(kind, bank, c0, n, off, key, src, fs, fname, pieces, new=None):
-        f0 = c0 % 256
+    def chunk(bank, n, off, key, src, c0, skeys, y0, pieces, new=None):
+        fs, width, fname = (T.bt, 256, "bt") if src[1] == "s" else (T.fo, FO, "fo")
+        slots = range(y0 // 128, (y0 + n + 127) // 128)
         for b in range(4):
-            mm(bank + b, n, "qe", 128 * b, src[0], src[1] + f0, True, False, ["qe0%d" % b] + src[2])
-        line["on"] = src[0] + key
+            mm(bank + b, n, "qe", 128 * b, src, c0, True, False, ["qe0%d" % b] + skeys)
+        k0, k = new or (0, n)
         for b in range(4):
-            k = new or n
-            out, win = T.yt[:, 4 * c0 + b:4 * (c0 + k):4], T.bt[:, 256 * b:256 * b + 256].indirect(off)
-            if GATHER[kind][b] == "V":
-                ts(out, win, 0.015625, None, A.mult, None, ["bt%d" % b, key], units("yt", c0, k, [b]), gat(k))
-            else:
-                act(out, win, FN.Copy, ["bt%d" % b, key], units("yt", c0, k, [b]), gat(k), scale=0.015625)
-        line["on"] = None
-        qz("qy", c0, n, T.yt[:, 4 * c0:4 * (c0 + n)], units("yt", c0, n), units("qy", c0, n, [0]))
+            mv(T.yt[:, 4 * (y0 + k0) + b:4 * (y0 + k0 + k):4], T.bt[:, 256 * b:256 * b + 256].indirect(off), ["bt%d" % b, key],
+               ["yt%d%d" % (s, b) for s in slots], gat(k), scale=0.015625)
+        qz("qy", y0, n, T.yt[:, 4 * y0:4 * (y0 + n)], ["yt%d%d" % (s, b) for s in slots for b in range(4)], ["qy%d" % s for s in slots])
         for b in range(4):
-            mm(bank + b, n, "qw", 128 * b, "qy", c0, False, True, ["qwc", "qws"] + units("qy", c0, n, [0]))
+            mm(bank + b, n, "qw", 128 * b, "qy", y0, False, True, ["qwc", "qws"] + ["qy%d" % s for s in slots])
         for b in range(4):
-            for t0, x0, m, st in pieces:
-                tt(T.xt[:, 4 * x0 + b:4 * (x0 - x0 % st + st * m):4 * st], T["ps%d" % (bank + b)][:, t0:t0 + m],
-                   fs[:, 256 * b + f0 + t0:256 * b + f0 + t0 + m], A.max, ["ps%d" % (bank + b)] + ["%s%d" % (f, b) for f in fname],
-                   units("xt", x0 - x0 % st, st * m, [b]), m)
+            for t0, x0, m, st, names in pieces:
+                tt(T.xt[:, 4 * x0 + b:4 * (x0 + st * (m - 1)) + b + 1:4 * st], T["ps%d" % (bank + b)][:, t0:t0 + m],
+                   fs[:, width * b + c0 + t0:width * b + c0 + t0 + m], A.max, ["ps%d" % (bank + b), fname + str(b)],
+                   ["xt%s%d" % (s, b) for s in names], m)
 
-    def shift_columns(win, keys, rows, x, out, okey):
-        cp(T.a1[:], win.indirect(rows), keys, ["a1"], gat(64))
-        tp(T.gg[:], T.a1[:], ["a1"], ["gg"])
-        cp(T.a2[:], T.gg[:].indirect(of[:, O_LC + 4 + 2 * x:O_LC + 6 + 2 * x]), ["gg", "oc"], ["a2_"], gat(32))
-        tp(out, T.a2[:], ["a2_"], [okey])
+    def state(name, a, slot, key):
+        qz(name, a, 128, T.xt[:, 512 * slot:512 * slot + 512], ["xt%d%s%d" % (slot, s, b) for s in "ab" for b in range(4)], [key])
 
-    def read_list(win, keys, rows, x, out, okey):
-        shift_columns(win, keys, rows, x, T.uu[:], "uu")
-        cp(out, T.uu[:].indirect(of[:, O_FM:O_FM + 1]), ["uu", "ofm"], [okey], gat(16))
+    def turn_twice(i, win, keys, rows, cols, ckey, out, okey):
+        a1, gg, a2, z = T.a1[:, 64 * i:64 * i + 64], T.gg[:, 64 * i:64 * i + 64], T.a2[:, 32 * i:32 * i + 32], str(i)
+        mv(a1, win.indirect(rows), keys, ["a1" + z], gat(64))
+        tp(gg, a1, ["a1" + z], ["gg" + z])
+        mv(a2, gg.indirect(cols), ["gg" + z, ckey], ["a2" + z], gat(32))
+        tp(out, a2, ["a2" + z], [okey])
 
+    def read_list(i, win, keys, rows, x, okey):
+        uu = T.uu[:, 32 * i:32 * i + 32]
+        turn_twice(i, win, keys, rows, lst("ocol", 2 * x, 2 * x + 2), "ocol", uu, "uu%d" % i)
+        cp(T[okey][:, 0:16], uu.indirect(lst("ofm")), ["uu%d" % i, "ofm"], [okey], gat(16))["mark"] = True
+
+    def differences(x, hf):
+        rd, z = x + 1, str(hf)
+        qx, pa = "qx%d" % rd, "pa%d" % rd
+        win, keys = ("ls", lsk) if x == 0 else ("qs%d" % rd, ["qs%ds" % rd, "qs%dt" % rd])
+        late = x + hf == 2 and x > 0
+        for e in ((0, 1, 2) if late else (2, 0, 1)):
+            c0, nm, o = 256 * hf + 128 * e, pa + str(2 * hf + e), 32 * x + 16 * e + 8 * hf
+            if e < 2:
+                pick(pa, c0, win, 0, 256, T.ol[:, o:o + 8], 8, keys + ["cand%d" % x], nm)
+            for b in range(4):
+                if e < 2:
+                    mm(4 * hf + b, 128, "qe", 512 * (e + 1) + 128 * b, pa, c0, late and e == 0, e == 1 and not late,
+                       ["qe%d%d" % (e + 1, b), nm + "c", nm + "s"])
+                else:
+                    mm(4 * hf + b, 128, "qe", 128 * b, qx, 128 * hf, not late, late, ["qe0%d" % b] + (["qx1c", "qx1s"] if x == 0 else [qx + z]))
+        for b in range(4):
+            mv(T.zt[:, 512 * hf + b:512 * hf + 512:4], T["ps%d" % (4 * hf + b)][:, 0:128], ["ps%d" % (4 * hf + b)], ["zt" + z + str(b)], 128, scale=-1.0)
+        qz("qz", 128 * hf, 128, T.zt[:, 512 * hf:512 * hf + 512], ["zt" + z + str(b) for b in range(4)], ["qz" + z])["mark"] = True
+
+    def deal(hf):
+        z, by, bx, c = str(hf), "ps%d" % (2 * hf), "ps%d" % (2 * hf + 1), slice(64 * hf, 64 * hf + 64)
+        mm(2 * hf, 128, "qup", 128, "qz", 128 * hf, True, True, ["qupc", "qups", "qz" + z])
+        mm(2 * hf + 1, 128, "qup", 0, "qz", 128 * hf, True, True, ["qupc", "qups", "qz" + z])
+        for t in range(2):
+            sy = T.sy[:, 128 * hf + 64 * t:128 * hf + 64 * t + 64]
+            act(sy, T[by][:, 64 * t:64 * t + 64], FN.Copy, [by], ["sy%d%d" % (hf, t)])
+            tt(T.fl[:, 512 * hf + t:512 * hf + 256:4], T[bx][:, 64 * t:64 * t + 64], sy, A.is_ge, [bx, "sy%d%d" % (hf, t)], ["fl%d%d" % (hf, t)])
+        qz("qf", 128 * hf, 128, T.fl[:, 256 * hf:256 * hf + 512], ["fl" + z + "0", "fl" + z + "1", "flz"], ["qf" + z])
+        mm(2 * hf, 128, "qc", 0, "qf", 128 * hf, True, True, ["qc", "qf" + z])
+        ts(T.ns[:, c], T[by][:, c], col["tg"], None, A.not_equal, None, [by, "tg"], ["ns" + z])
+        tp(T.nt[:, c], T.ns[:, c], ["ns" + z], ["nt" + z])
+        rec("V", lambda: g.vector.tensor_tensor_scan(T.sc[:, c], T.nt[:, c], T.df[:, c], 0.0, A.mult, A.add), ["nt" + z, "df"], ["sc" + z], size(64))
+
+    differences(0, 0)
+    differences(0, 1)
     for x in range(3):
         rd = x + 1
-        line["rd"] = "/%d" % rd
-        qx, nq, pa, land, ln = "qx%d" % rd, "qx%d" % (rd + 1), "pa%d" % rd, T["land%d" % rd], "land%d" % rd
-        half = [("qa", 0, ["qa"])] * 2 if x == 0 else [(qx, 0, [qx + "e"]), (qx, 0, [qx + "i"])]
-        own = (half[0][0], 0, half[0][2] + half[1][2])
-        win = ("ls", 0, ["lsoc", "lsos", "lsa", "lsac"]) if x == 0 else (qx, 256, [qx + "s", qx + "t"])
-        seeds = (qx, 256, [qx + "tc", qx + "ts"]) if x == 0 else win
-        for hf in range(2):
-            for b in range(4):
-                mm(4 * hf + b, 128, "qe", 128 * b, own[0], 128 * hf, True, False, ["qe0%d" % b] + half[hf][2])
-        line["on"] = pa
-        for hf in range(2):
-            for e in range(2):
-                c0, nm = 256 * hf + 128 * e, pa + str(2 * hf + e)
-                pick(pa, c0, win[0], win[1], 256, T.ol[:, 16 * e + 8 * hf:16 * e + 8 * hf + 8], 8, win[2] + ["ol"], nm)
-                for b in range(4):
-                    mm(4 * hf + b, 128, "qe", 512 * (e + 1) + 128 * b, pa, c0, False, e == 1, ["qe%d%d" % (e + 1, b), nm + "c", nm + "s"])
-        line["on"] = None
-        for hf in range(2):
-            for b in range(4):
-                out, src, bank = T.zt[:, 512 * hf + b:512 * hf + 512:4], T["ps%d" % (4 * hf + b)][:, 0:128], "ps%d" % (4 * hf + b)
-                if TURN[hf][b] == "A":
-                    act(out, src, FN.Copy, [bank], ["zt%d%d" % (hf, b)], 128, scale=-1.0)
-                else:
-                    ts(out, src, -1.0, None, A.mult, None, [bank], ["zt%d%d" % (hf, b)], 128)
-            qz("qz", 128 * hf, 128, T.zt[:, 512 * hf:512 * hf + 512], ["zt%d%d" % (hf, b) for b in range(4)], ["qz%d" % hf])
-        steps_of(x)
-        for hf in range(2):
-            mm(2 * hf, 128, "qup", 128, "qz", 128 * hf, True, True, ["qupc", "qups", "qz%d" % hf])
-            mm(2 * hf + 1, 128, "qup", 0, "qz", 128 * hf, True, True, ["qupc", "qups", "qz%d" % hf])
-            act(T.sy[:, 128 * hf:128 * hf + 128], T["ps%d" % (2 * hf)][:, 0:128], FN.Copy, ["ps%d" % (2 * hf)], ["sy%d" % hf], 128)
-            for t in (2 * hf, 2 * hf + 1):
-                tt(T.fl[:, t:256:4], T["ps%d" % (2 * hf + 1)][:, 64 * (t % 2):64 * (t % 2) + 64], T.sy[:, 64 * t:64 * t + 64], A.is_ge,
-                   ["ps%d" % (2 * hf + 1), "sy%d" % hf], ["fl%d" % t])
-        qz("qf", 0, 128, T.fl[:], ["fl0", "fl1", "fl2", "fl3", "flz"], ["qf"])
-        mm(0, 128, "qc", 0, "qf", 0, True, True, ["qc", "qf"])
-        for e in range(2):
-            ts(T.ns[:, 64 * e:64 * e + 64], T.ps0[:, 0:64], col["tg%d" % e], None, A.not_equal, None, ["ps0", "tg%d" % e], ["ns%d" % e])
-        tp(T.nt[:], T.ns[:], ["ns0", "ns1"], ["nt"])
-        rec("V", lambda: g.vector.tensor_tensor_scan(T.sc[:], T.nt[:], T.df[:], 0.0, A.mult, A.add), ["nt", "df0", "df1"], ["sc"], size(64))
-        wide = 16 if x < 2 else 32
-        mine = land[:, wide:2 * wide]
-
-        def slot(o, ld=land, n=wide):
-            return ld[:, n * ((me - o + 1) % N):n * ((me - o + 1) % N) + n]
-
-        if x < 2:
-            cp(mine, T.sc[:].indirect(of[:, O_CP + 2 * x:O_CP + 2 * x + 1]), ["sc", "ocp%d" % x], [ln + "o"], gat(16))
-        else:
-            shift_columns(T.sc[:], ["sc", "ocq"], of[:, O_CQ:O_CQ + 4], x, mine, ln + "o")
-        send(mine, slot, 0, "an%d" % rd, [ln + "o"], ln + "n", hand="af%d" % rd)
-        if x < 2:
-            send(mine, slot, 1, "af%d" % rd, [ln + "o"], ln + "f", before=FARB)
+        land, ln, qx, nq, qs, ns = T["land%d" % rd], "land%d" % rd, "qx%d" % rd, "qx%d" % (rd + 1), "qs%d" % rd, "qs%d" % (rd + 1)
+        deal(0)
+        deal(1)
         if x == 0:
-            pick(qx, 256, "ls", 0, 256, of[:, O_SG:O_SG + 16], 16, win[2] + ["osg"], qx + "t")
-        unpack(4, seeds, T.bt, ["bt"])
-        unpack(4, own, T.fo, ["fo"])
-        if x == 1:
-            read_list(mine, [ln + "o", "ori"], of[:, O_RI:O_RI + 4], x, T.oi[:], "oi")
-            chunk("inner1", 0, 128, 128, T.oi[:, 8:16], "oi", half[1], T.fo, ["fo"], [(0, 96, 128, 1)])
+            pick(qs, 0, "ls", 0, 256, lst("osg"), 16, lsk + ["osg"], qs)
+        seeds = [qs + "c", qs + "s"] if x == 0 else [qs + "s", qs + "t"]
+        own = [["qx1c", "qx1s"], [qx + "0", qx + "1"], [qx + "0", qx + "1", qx + "c", qx + "s"]][x]
+        unpack(qs, 256, seeds, T.bt, 256, "bt")
+        unpack(qx, (256, 256, 288)[x], own, T.fo, FO, "fo")
         if x == 2:
-            cp(T.oi[:], mine.indirect(of[:, O_L + 2:O_L + 3]), [ln + "o", "oli"], ["oi"], gat(16))
-            chunk("inner2", 0, 64, 192, T.oi[:, 4:16], "oi", own, T.fo, ["fo"], [(0, 64, 192, 1)])
-        if x < 2:
-            read_list(land[:, 0:48], [ln + "o", ln + "n", "or"], of[:, O_R + 4 * x:O_R + 4 * x + 4], x, T.om[:], "om")
-        else:
-            cp(T.om[:], land[:].indirect(of[:, O_L:O_L + 1]), [ln + "o", ln + "n", "oll"], ["om"], gat(16))
+            break
+        for hf in range(2):
+            mine, dealt = land[:, 88 - 80 * hf:96 - 80 * hf], T.sc[:, 64 * hf + 7:64 * hf + 64:8]
+            if x:
+                mv(mine, dealt, ["sc%d" % hf], [ln + "o%d" % hf])
+            else:
+                tt(mine, dealt, T.lq[:, 64 * hf + 8:64 * hf + 72:8], A.add, ["sc%d" % hf, "lq", "lqz"], [ln + "o%d" % hf])
+
+        def slot(c0, turn, ld=land):
+            return lambda o: ld[:, c0 + 8 * ((me - o + turn) % N):c0 + 8 * ((me - o + turn) % N) + 8]
+
+        lastw["left"] = send(land[:, 88:96], slot(40, 6), near, "an%d" % rd, [ln + "o0"], ln + "n0", before=0.3, hand="af%d" % rd)
+        far = send(land[:, 88:96], slot(40, 6), [o for o in others if o not in near], "af%d" % rd, [ln + "o0"], ln + "f", before=FARB)
+        if x == 1:
+            read_list(0, T.sc[:, 0:64], ["sc0", "osc"], lst("osc", 0, 4), x, "oi")
+            chunk(0, 128, T.oi[:, 0:4], "oi", qx, 0, own, 0, [(0, 128, 64, 2, ["1a"])], (0, 64))
+        send(land[:, 8:16], slot(0, 1), near, "ao%d" % rd, [ln + "o1"] + [["left"], ["yt00", "yt01", "yt02", "yt03"]][x], ln + "n1", behind=(far, 2))
+        both = [ln + s for s in ("o0", "o1", "n0", "n1", "f", "z")] + ["orow%d" % x]
         if x == 0:
-            chunk("own", 4, 0, 256, T.om[:], "om", own, T.fo, ["fo"], [(0, 64, 192, 1), (192, 0, 64, 1)])
-        if x == 1:
-            chunk("edge1", 4, 0, 128, T.om[:, 0:8], "om", half[0], T.fo, ["fo"], [(0, 224, 32, 1), (32, 0, 96, 1)])
-        if x == 2:
-            chunk("edge2", 4, 0, 128, T.om[:, 0:4], "om", half[0], T.fo, ["fo"], [(0, 0, 64, 1)], 64)
-        if x < 2:
-            for hf in range(2):
-                qz(nq, 128 * hf, 128, T.xt[:, 512 * hf:512 * hf + 512], units("xt", 128 * hf, 128), [nq + "ei"[hf]])
-            cand_lists(rd)
-            spread(rd)
-            act(T.s1[:], land[:].indirect(of[:, O_S + 8 * x:O_S + 8 * x + 8]), FN.Copy, [ln + "o", ln + "n", ln + "f", "os_"], ["s1"], gat(128))
-            tp(T.s2[:], T.s1[:], ["s1"], ["s2"])
-            cp(T.osd[:], T.s2[:].indirect(of[:, O_LC + 18 + 2 * x:O_LC + 19 + 2 * x]), ["s2", "oc"], ["os"], gat(16))
-            for hf in range(2):
-                nm, c0 = "st"[hf], 256 + 128 * hf
-                chunk(nm + str(x), 4 * hf, c0, 128, T.osd[:, 8 * hf:8 * hf + 8], "os", seeds, T.bt, ["bt"], [(0, c0, 128, 1)])
-                qz(nq, c0, 128, T.xt[:, 4 * c0:4 * c0 + 512], units("xt", c0, 128), [nq + nm])
+            read_list(0, land[:, 80:104], [ln + "o0", ln + "n0", "orow0"], lst("orow0", 4, 8), x, "oi")
+            chunk(4, 128, T.oi[:, 0:8], "oi", qx, 0, own, 0, [(0, 0, 128, 1, ["0a", "0b"])])
+            state(nq, 0, 0, nq + "0")
+            read_list(1, land[:, 0:104], both, lst("orow0", 0, 4), x, "om")
+            mv(T.a3[:, 0:64], T.gg[:, 64:128].indirect(lst("ocol", 4, 8)), ["gg1", "ocol"], ["a3"], gat(64))
+            tp(T.rot1[:, 0:64], T.a3[:, 0:64], ["a3"], ["rot1"])
+            cp(T.ol[:, 32:64], T.rot1[:, 0:64].indirect(lst("ol1")), ["rot1", "ol1"], ["cand1"], gat(32))
         else:
-            act(T.pt[:, 0:16], T.sc[:].indirect(of[:, O_OP:O_OP + 1]), FN.Copy, ["sc", "oop"], ["pt"])
-            relabel(T.pt[:, 0:16], 16, T.po[:, 0:16], "pt", "po", True)
-            tp(T.pt[:], T.po[:], ["po", "poz"], ["pt"])
+            mv(land[:, 104:112], T.sc[:, 71:128:8], ["sc1"], [ln + "o2"])
+            read_list(1, land[:, 80:112], [ln + "o0", ln + "o2", ln + "n0", "orow1"], lst("orow1", 0, 4), x, "om")
+            chunk(4, 128, T.om[:, 4:12], "om", qx, 64, own, 128, [(0, 0, 64, 2, ["0a"]), (64, 129, 64, 2, ["1b"])])
+            state(nq, 128, 1, nq + "1")
+            mv(T.a4[:], land[:, 0:104].indirect(lst("orow1", 8, 16)), both, ["a4"], gat(128))
+            tp(T.g4[:], T.a4[:], ["a4"], ["g4"])
+            mv(T.a3[:], T.g4[:].indirect(lst("ocl3")), ["g4", "ocl3"], ["a3"], gat(128))
+            tp(T.rot2[:, 0:128], T.a3[:], ["a3"], ["rot2"])
+            cp(T.ol[:, 64:96], T.rot2[:, 0:128].indirect(lst("ol2")), ["rot2", "ol2"], ["cand2"], gat(32))
+        spread(rd)
+        mv(T.s1[:], land[:, 32:104].indirect(lst("osr%d" % x)), [ln + "o0", ln + "n0", ln + "f", ln + "z", "osr%d" % x], ["s1"], gat(64))
+        tp(T.s2[:], T.s1[:], ["s1"], ["s2"])
+        cp(T.osd[:], T.s2[:].indirect(lst("osd%d" % x)), ["s2", "osd%d" % x], ["os"], gat(16))["mark"] = True
+        for hf in range(2):
+            chunk(4 * hf, 128, T.osd[:, 8 * hf:8 * hf + 8], "os", qs, 128 * hf, seeds, 256 + 128 * hf,
+                  [(0, 256 + 128 * hf, 128, 1, ["%da" % (2 + hf), "%db" % (2 + hf)])])
+            state(ns, 128 * hf, 2 + hf, ns + "st"[hf])
+        if x == 0:
+            dma("S", T.vin[:], T.v[:], [ns + "s"], ["vin"], lat=START + 1.7)
+            qz("qv", 0, 128, T.vin[:], ["vin"], ["qv"])
+        if x == 1:
+            read_list(2, land[:, 0:24], [ln + "o1", ln + "n1", "orow1"], lst("orow1", 4, 8), x, "oe")
+            chunk(0, 128, T.oe[:, 4:8], "oe", qx, 128, own, 0, [(64, 1, 64, 2, ["0b"])], (64, 64))
+            state(nq, 0, 0, nq + "0")
+        differences(rd, 0)
+        if x == 0:
+            chunk(4, 128, T.om[:, 8:16], "om", qx, 128, own, 128, [(0, 128, 128, 1, ["1a", "1b"])])
+            state(nq, 128, 1, nq + "1")
+        differences(rd, 1)
+        if x == 1:
             sem = newsem("d")
-            for a in range(4):
-                dma("S", T.op[2 * a:2 * a + 2, :], T.pt[32 * a:32 * a + 16, :], ["pt"], [], sem)
+            dma("S", T.qx3c[:, 256:288].bitcast(dt.uint8), T.qx3c[:, 0:32].bitcast(dt.uint8), [nq + "0"], [nq + "c"], sem, lat=START + 0.6)
+            dma("S", T.qx3s[:, 256:288], T.qx3s[:, 0:32], [nq + "0"], [nq + "s"], sem, lat=START + 0.6)
+
+    for hf in range(2):
+        turn_twice(hf, T.sc[:, 64 * hf:64 * hf + 64], ["sc%d" % hf, "og3"], lst("og3"), lst("oc3"), "oc3",
+                   land[:, 64 + 32 * hf:96 + 32 * hf], ln + "o%d" % hf)
+    send(land[:, 64:96], lambda o: land[:, 32:64] if o == prv else land[:, 0:32], near, "an3", [ln + "o0"], ln + "n")
+    cp(T.oi[:, 0:16], land[:, 64:128].indirect(lst("oj")), [ln + "o0", ln + "o1", "oj"], ["oi"], gat(16))["mark"] = True
+    chunk(4, 192, T.oi[:, 4:16], "oi", qx, 96, own, 128, [(0, 64, 192, 1, ["0b", "1a", "1b"])])
+    cp(T.om[:], land[:, 0:96].indirect(lst("ok")), [ln + "o0", ln + "n", "ok"], ["om"], gat(16))["mark"] = True
+    chunk(0, 128, T.om[:, 0:4], "om", qx, 0, own, 0, [(32, 0, 64, 1, ["0a"])], (32, 64))
+    cp(T.i2[:], T.sc[:].indirect(lst("osc", 4, 5)), ["sc0", "sc1", "osc"], ["pn", "i2", "i65"], gat(16))
+    ts(T.i2[:], T.i2[:], 257.0, None, A.mult, None, ["pn"], ["pn"])
+    ts(T.i2[:], T.i2[:], 5, 255, A.logical_shift_right, A.bitwise_and, ["pn"], ["pn"])
+    cp(T.po[:, 0:16], T.i2[:], ["pn"], ["po"])
+    tp(T.pt[:], T.po[:], ["po", "poz"], ["pt"])
+    sem = newsem("d")
+    for a in range(4):
+        dma("S", T.op[2 * a:2 * a + 2, :], T.pt[32 * a:32 * a + 16, :], ["pt"], [], sem)
 
     for hf in (1, 0):
-        qz("qx4", 128 * hf, 128, T.xt[:, 512 * hf:512 * hf + 512], units("xt", 128 * hf, 128), ["qx4%d" % hf])
-        mm(hf, 128, "qv", 0, "qx4", 128 * hf, True, True, ["qv", "qx4%d" % hf])
-    cp(T.ysb[:, 96:224], T.ps1[:, 0:128], ["ps1"], ["y1"], 128)
+        state("qx4", 128 * hf, hf, "qx4%d" % hf)
+        mm(4 * hf, 128, "qv", 0, "qx4", 128 * hf, True, True, ["qv", "qx4%d" % hf])
+    mv(T.ysb[:, 96:224], T.ps4[:, 0:128], ["ps4"], ["y1"], 128)
     cp(T.ysb[:, 224:256], T.ps0[:, 0:32], ["ps0"], ["y2"])
     cp(T.ysb[:, 0:96], T.ps0[:, 32:128], ["ps0"], ["y0"], 96)
     dma("A", T.y[:], T.ysb[:], ["y0", "y1", "y2"], [], lat=START + 0.9)
@@ -551,81 +814,22 @@ def rank_program(g, core, T, topo):
         for k in range(4):
             dma("SA"[i and k > 1], T.osc[4 * k:4 * k + 4, j0:j0 + n], T.qx4s[32 * k:32 * k + 4, t0:t0 + n], ["qx40", "qx41"], [], sem, lat=START + 0.5)
 
-    def place(need, first, rank, careful):
-        start, busy, left = {}, {q: [] for q in Q}, sorted(range(len(ops)), key=lambda n: (rank[n], n))
-        while left:
-            n = [m for m in left if all(a in start for a, d in need[m])][0]
-            left.remove(n)
-            q, c = ops[n]["q"], ops[n]["c"]
-            ready = t = max([first[n]] + [start[a] + ops[a]["c"] + d for a, d in need[n]])
-            for s, e in busy[q]:
-                if max(t, ready + careful * MARGIN) + c + careful * ROOM[q] <= s:
-                    t = max(t, ready + careful * MARGIN)
-                    break
-                t = max(t, e)
-            start[n] = t
-            busy[q] = sorted(busy[q] + [(t, t + c)])
-        return start
-
-    def replay(need, lines, case):
-        compute, gather, product, remote, wake, first = case
-        cost = [o["c"] * (product if o["q"] == "P" else gather if o["gather"] else compute if o["q"] in "VA" else 1.0) for o in ops]
-        far = [first if o["tok"] == "l0" else remote if o["q"] == "G" else 1.0 for o in ops]
-        start, why, at, free = {}, {}, {q: 0 for q in Q}, {q: (0.0, None) for q in Q}
-        while len(start) < len(ops):
-            for q in Q:
-                while at[q] < len(lines[q]) and all(a in start for a, d in need[lines[q][at[q]]]):
-                    n = lines[q][at[q]]
-                    t, w = free[q]
-                    for a, d in need[n]:
-                        e = start[a] + cost[a] + (d and (d - WAKE) * far[a] + wake)
-                        if e > t:
-                            t, w = e, -1 - a
-                    start[n], why[n], free[q] = t, w, (t + cost[n], n)
-                    at[q] += 1
-        last = n = max(start, key=lambda m: start[m] + cost[m] + ops[m]["lat"])
-        pairs = []
-        while why[n] is not None:
-            if why[n] >= 0:
-                pairs.append((why[n], n))
-            n = why[n] if why[n] >= 0 else -1 - why[n]
-        return start[last] + cost[last] + ops[last]["lat"], pairs, start
-
-    if not ORDER:
-        before, after = [[] for op in ops], [[] for op in ops]
+    if "order" not in PLAN:
+        before = []
         for op in ops:
             gaps = {a["n"]: 0.0 for a in op["after"]}
-            for a in [d.get("like", d) for d in op["deps"]]:
+            for d in op["deps"]:
+                a = d.get("like", d)
                 gaps[a["n"]] = 0.0 if op["q"] == "P" and a["q"] == "P" else a["lat"] + WAKE
-            for a, d in gaps.items():
-                before[op["n"]].append((a, d))
-                after[a].append((op["n"], d))
-        rank, best = [-op["n"] for op in ops], None
-        for turn in range(TURNS):
-            back = place(after, [op["lat"] for op in ops], rank, 0)
-            start = place(before, [0.0] * len(ops), [-back[n] - ops[n]["c"] - ops[n]["ahead"] for n in range(len(ops))], 1)
-            rank = [-start[n] - ops[n]["c"] for n in range(len(ops))]
-            end = max(start[n] + ops[n]["c"] + ops[n]["lat"] for n in start)
-            if best is None or end < best[0]:
-                best = (end, start)
-        lines = {q: [n for n in sorted(best[1], key=lambda n: (best[1][n], n)) if ops[n]["q"] == q] for q in Q}
-        runs, moved = [replay(before, lines, case) for case in CASES], True
-        while moved:
-            moved = False
-            for a, b in sorted({pair for run in runs for pair in run[1]}):
-                q, start = ops[a]["q"], runs[0][2]
-                i = lines[q].index(b)
-                for k in range(1, min(i, 8) + 1) if lines[q][i - 1] == a else []:
-                    if any(start[z] >= start[lines[q][i - k]] for z, d in before[b]):
-                        break
-                    trial = dict(lines)
-                    trial[q] = lines[q][:i - k] + [b] + lines[q][i - k:i] + lines[q][i + 1:]
-                    new = [replay(before, trial, case) for case in CASES]
-                    if sum(r[0] / s[0] for r, s in zip(new, runs)) < len(CASES) - 1e-5:
-                        lines, runs, moved = trial, new, True
-                        break
-        ORDER.extend(sorted(runs[0][2], key=lambda n: (runs[0][2][n], n)))
-    order = [ops[n] for n in ORDER]
+                if d.get("behind"):
+                    a = d["behind"][0]
+                    gaps[a["n"]] = max(gaps.get(a["n"], 0.0), a["lat"] + WAKE + d["behind"][1])
+            before.append(list(gaps.items()))
+        PLAN["ops"] = ops
+        PLAN["order"], PLAN["queue"] = lay_out(ops, before)
+    order = [ops[n] for n in PLAN["order"]]
+    for op in ops:
+        op["q"] = PLAN["queue"][op["n"]]
 
     for op in ops:
         op["deps"] = [o for o in op["deps"] if not (op["q"] == "P" and o["q"] == "P")]
@@ -648,7 +852,7 @@ def rank_program(g, core, T, topo):
             if seen[op["q"]].get(s, 0) < v:
                 Q[op["q"]].wait_ge(T.sem[s], v)
                 seen[op["q"]][s] = v
-        ins = op["fn"]()
+        ins = op["fn"][op["q"]]()
         if op["tok"] is None and op["need"]:
             ins.then_inc(T.sem[op["at"][0]], 1)
     for s, v in totals.items():

import math
from concourse.bass import DstId, RemoteDMATransfer
from concourse.mybir import dt, AluOpType, ActivationFunctionType

F32, BF, I32, U16, U8, CODE = "float32", "bfloat16", "int32", "uint16", "uint8", "float8_e4m3fn_x4"
N = 8
DIR = [(-1, 0), (-1, 1), (0, 1), (1, 1), (1, 0), (1, -1), (0, -1), (-1, -1)]
HAND = {"ac": [(0, (4, 2)), (1, (3,)), (2, (5,))], "asc": [(0, (4,)), (1, (3,))], "af1": [(0, (4,))], "af2": [(0, (4,))]}
ACROSS = (False, True, False)
FO = 288

SCRATCH = {}
for _n, _w, _d in [
    ("xin", 1024, BF), ("sx", 512, BF), ("uin", 512, BF), ("vin", 512, BF), ("landp", 96, I32),
    ("land1", 112, BF), ("land2", 112, BF), ("land3", 128, BF), ("oe", 16, U16),
    ("ez", 520, BF), ("idn", 128, BF), ("vv", 128, BF), ("va", 128, BF), ("vb", 128, BF), ("cb", 512, BF),
    ("pi", 16, I32), ("fi", 24, I32), ("ff", 24, F32), ("kk", 128, F32), ("cc", 64, F32), ("dd", 48, F32),
    ("w1", 48, F32), ("w2", 48, F32), ("tb", 80, F32), ("kb", 80, F32), ("ti", 80, I32), ("i1", 48, I32), ("i2", 16, I32), ("i3", 16, I32),
    ("of", 192, U16),
    ("zt", 1024, BF), ("yt", 2048, BF), ("xt", 2048, BF), ("bt", 1024, BF), ("fo", 4 * FO, BF),
    ("sy", 256, F32), ("fl", 768, BF), ("ns", 128, BF), ("nt", 128, BF), ("sc", 128, BF),
    ("lq", 136, BF), ("df", 128, BF), ("a1", 192, BF), ("gg", 192, BF), ("a2", 96, BF), ("uu", 96, BF), ("a3", 128, BF),
    ("a4", 128, BF), ("g4", 128, BF), ("s1", 64, BF), ("s2", 64, BF), ("rot0", 256, BF), ("rot1", 256, BF), ("rot2", 512, BF),
    ("om", 16, U16), ("oi", 32, U16), ("osd", 16, U16), ("ol", 96, U16),
    ("po", 32, F32), ("pt", 32, F32),
    ("ysb", 256, F32),
]:
    SCRATCH[_n] = ("sbuf", [128, _w], _d)
for _n, _w in [("qa", 256), ("snd", 128), ("ls", 256), ("qx1", 256), ("qx2", 256), ("qx3", 288), ("qx4", 256),
               ("qs1", 256), ("qs2", 256), ("qs3", 256), ("pa1", 512), ("pa2", 512), ("pa3", 512), ("qe", 1536), ("qc", 128),
               ("qu", 128), ("qup", 256), ("qv", 128), ("qw", 512), ("qz", 256), ("qf", 256), ("qy", 512)]:
    SCRATCH[_n + "c"] = ("sbuf", [128, _w], CODE)
    SCRATCH[_n + "s"] = ("sbuf", [128, _w], U8)
for _b in range(8):
    SCRATCH["ps%d" % _b] = ("psum", [128, 512], F32)

SEMAPHORES = (["eV", "eA", "eP", "eG"] + ["d%d" % _i for _i in range(24)] + ["l%d" % _i for _i in range(12)]
              + ["ap", "ac", "asc", "an1", "an2", "an3", "ao1", "ao2", "af1", "af2", "hac", "hasc", "haf1", "haf2"])

PLAN = {}
FARB, FIRSTB, PB = 1, 7, 7
CASES = [(1.0, 1.0, 1.0, 1.0, 0.22, 1.0), (1.45, 1.45, 1.6, 1.15, 0.22, 1.15), (1.1, 1.15, 1.2, 1.3, 0.3, 1.4)]
TRIES, STEPS = 200, 330000
PULL, HEAT, BURST = 0.05, 0.1, 200
A = AluOpType
FN = ActivationFunctionType
CY, PE, WAKE, ROW, START, ISSUE = 0.00085, 0.0005, 0.22, 0.018, 0.9, 0.3


def lay_out(ops, before):
    n, seed = len(ops), [6]
    q = [o["q"] for o in ops]
    flex = [len(o["fn"]) > 1 for o in ops]

    def rnd():
        seed[0] = (seed[0] * 1103515245 + 12345) % 2147483648
        return (seed[0] + 0.5) / 2147483648

    cases = []
    for compute, gather, product, remote, wake, first in CASES:
        cost = [o["c"] * (product if o["q"] == "P" else gather if o["gather"] else 1.0 if o["tok"] else compute) for o in ops]
        far = [first if o["tok"] == "l0" else remote if o["tok"] else 1.0 for o in ops]
        cases.append((cost, [[(a, cost[a] + (d and (d - WAKE) * far[a] + wake)) for a, d in before[m]] for m in range(n)],
                      [cost[m] + ops[m]["lat"] for m in range(n)]))
    pre = [{a for a, d in before[m]} for m in range(n)]

    def replay(order, case):
        cost, need, tail = case
        start, why, free, last, end, at = [0.0] * n, [None] * n, {}, {}, 0.0, 0
        for m in order:
            k = q[m]
            t, w, z = free.get(k, 0.0), last.get(k, -1), True
            for a, d in need[m]:
                if start[a] + d > t:
                    t, w, z = start[a] + d, a, False
            start[m], why[m], free[k], last[k] = t, (w, z), t + cost[m], m
            if t + tail[m] > end:
                end, at = t + tail[m], m
        return end, start, why, at

    def place(cost, need, after, first, rank, choose):
        left, start, busy = [len(x) for x in need], [0.0] * n, {k: [] for k in "VAPGS"}
        ready = sorted((rank[m], m) for m in range(n) if not left[m])
        while ready:
            m = ready.pop()[1]
            r, best = max([first[m]] + [start[a] + cost[a] + d for a, d in need[m]]), None
            for k in ("AV" if choose and flex[m] else q[m]):
                line, t = busy[k], r
                i = len(line)
                while i and line[i - 1][1] > r:
                    i -= 1
                while i < len(line) and line[i][0] < t + cost[m]:
                    t, i = max(t, line[i][1]), i + 1
                if best is None or t < best[0] - 0.05:
                    best = (t, k, i)
            start[m], q[m] = best[0], best[1]
            busy[best[1]].insert(best[2], (best[0], best[0] + cost[m]))
            for f, d in after[m]:
                left[f] -= 1
                if not left[f]:
                    ready.append((rank[f], f))
                    ready.sort()
        return start

    views = []
    for cost, need, tail in cases:
        need = [[(a, d - cost[a]) for a, d in x] for x in need]
        after = [[] for m in range(n)]
        for m in range(n):
            for a, d in need[m]:
                after[a].append((m, d))
        lat, way = [tail[m] - cost[m] for m in range(n)], [0.0] * n
        for m in reversed(range(n)):
            way[m] = cost[m] + max([lat[m]] + [d + way[f] for f, d in after[m]])
        views.append((cost, need, after, lat, way))
    best, kept, base = None, [0.0] * n, None
    for it in range(TRIES):
        cost, need, after, lat, way = views[it % len(views)]
        bias = [b + (rnd() - 0.5 if rnd() < 0.1 else 0.0) for b in kept]
        rank = [way[m] + bias[m] for m in range(n)]
        for turn in range(3):
            start = place(cost, need, after, [0.0] * n, rank, True)
            order = sorted(range(n), key=lambda m: (start[m], m))
            ends = [replay(order, c)[0] for c in cases]
            base = base or ends
            v = sum(e / b for e, b in zip(ends, base))
            if best is None or v < best[0]:
                best, kept = (v, order, list(q)), bias
            if turn < 2:
                back = place(cost, after, need, lat, [start[m] + cost[m] for m in range(n)], False)
                rank = [back[m] + cost[m] + bias[m] for m in range(n)]
    order, q[:] = list(best[1]), best[2]
    best, begun, none = (best[0], list(order), list(q)), [0.0] * n, {k: -1 for k in "VAPGS"}
    for turn in range(STEPS // BURST):
        heat = HEAT * 0.04 ** (turn * BURST / STEPS)
        lo = int(rnd() * (n - 40))
        hi = min(n, lo + 40 + int(rnd() * 50))
        inside, view = set(order[lo:hi]), []
        for cost, need, tail in cases:
            start, way, head, free = replay(order, (cost, need, tail))[1], list(tail), {}, {k: 0.0 for k in none}
            for m in reversed(order[hi:]):
                way[m] = head[q[m]] = max(way[m], cost[m] + head.get(q[m], 0.0))
                for a, d in need[m]:
                    way[a] = max(way[a], d + way[m])
            for m in order[:lo]:
                free[q[m]] = start[m] + cost[m]
            rest = max([0.0] + [start[m] + way[m] for m in order[:lo]])
            first = {m: max([0.0] + [start[a] + d for a, d in need[m] if a not in inside]) for m in inside}
            view.append((cost, {m: [(a, d) for a, d in need[m] if a in inside] for m in inside}, way, head, free, rest, first))

        def run(part):
            out, v = [], 0.0
            for (cost, need, way, head, free, end, first), b in zip(view, base):
                why, free, last, pull, at = {}, dict(free), dict(none), 0.0, part[-1]
                for m in part:
                    k = q[m]
                    t = free[k]
                    w = last[k]
                    if first[m] > t:
                        t = first[m]
                        w = -1
                    for a, d in need[m]:
                        d += begun[a]
                        if d > t:
                            t = d
                            w = a
                    begun[m] = t
                    why[m] = w
                    free[k] = t + cost[m]
                    last[k] = m
                    pull += t
                    if t + way[m] > end:
                        end, at = t + way[m], m
                for k in last:
                    if last[k] >= 0 and free[k] + head.get(k, 0.0) > end:
                        end, at = free[k] + head.get(k, 0.0), last[k]
                out.append((end, why, at))
                v += (end + PULL * pull / len(part)) / b
            return v * base[0] / len(base), out

        part = order[lo:hi]
        now, runs = run(part)
        for it in range(BURST):
            r = runs[int(rnd() * len(runs))]
            m, pairs = r[2] if rnd() < 0.6 else part[int(rnd() * len(part))], []
            while m >= 0:
                a = r[1][m]
                if a >= 0 and a not in pre[m]:
                    pairs.append((a, m))
                m = a
            if not pairs:
                continue
            a, b = pairs[int(rnd() * len(pairs))]
            u, k, flip, new = rnd(), (1, 1, 2, 3, 5, 8)[int(rnd() * 6)], None, part
            if u < 0.15:
                flip = a if rnd() < 0.6 else b
                if not flex[flip]:
                    continue
                q[flip] = "V" if q[flip] == "A" else "A"
            else:
                m, step = (b, -1) if u < 0.55 else (a, 1)
                i = j = part.index(m)
                while 0 <= j + step < len(part) and k:
                    j += step
                    k -= q[part[j]] == q[m]
                along, needs, lines = {m}, set(pre[m]), set()
                for s in (part[j:i][::-1] if step < 0 else part[i + 1:j + 1]):
                    if q[s] in lines or (s in needs if step < 0 else pre[s] & along):
                        along.add(s)
                        needs |= pre[s]
                        if q[s] != q[m]:
                            lines.add(q[s])
                if part[j] in along:
                    continue
                i, j = min(i, j), max(i, j) + 1
                new = part[:i] + [s for side in (step < 0, step > 0) for s in part[i:j] if (s in along) == side] + part[j:]
            v, tried = run(new)
            if v < now - heat * math.log(rnd()):
                part, runs, now = new, tried, v
                v = sum(r[0] / b for r, b in zip(runs, base))
                if v < best[0]:
                    best = (v, order[:lo] + part + order[hi:], list(q))
            elif flip is not None:
                q[flip] = "V" if q[flip] == "A" else "A"
        order[lo:hi] = part
        start = replay(order, cases[turn % len(cases)])[1]
        order.sort(key=lambda m: start[m])
    q[:] = best[2]
    PLAN["ends"] = [replay(best[1], c) for c in cases]
    return best[1], best[2]


def rank_program(g, core, T, topo):
    me = T.rank_of(core)

    def helpers(k):
        out = []
        for j, across in enumerate(ACROSS):
            serves = [T.cores[(k + d) % N] for v in HAND.values() for i, ds in v if i == j for d in ds]
            out.append([c for c in topo.cores_of(T.cores[k]) if T.rank_of(c) is None and c not in out
                        and (topo.die(c) != topo.die(T.cores[k])) == across and all(topo.may_write(c, o) for o in serves)][0])
        return out

    def handed_ap(nm, k, d):
        if nm == "ac":
            return T.lsc[:, 32 * k:32 * k + 32].bitcast(dt.uint8)
        if nm == "asc":
            return T.lss[:, 32 * k:32 * k + 32]
        return {"af1": T.land1, "af2": T.land2}[nm][:, 40 + 8 * ((6 - d) % N):48 + 8 * ((6 - d) % N)]

    def dst(c):
        return DstId(rid=topo.addr(c)[0], pnc=topo.addr(c)[1])

    def ones(m):
        return bin(m).count("1")

    def inside(k):
        return topo.mask(T.cores[k], helpers(k)[0]) & ~topo.mask(T.cores[k], T.cores[(k + 1) % N])

    if me is None:
        for k in range(N):
            if core in helpers(k):
                j, sent = helpers(k).index(core), 0
                for nm, ds in [(x, ds) for x in HAND for i, ds in HAND[x] if i == j]:
                    to = [T.cores[(k + d) % N] for d in ds]
                    m = topo.mask(core, to[0])
                    sent += ones(m)
                    g.wait_ge(T.sem["h" + nm], ones(inside(k)))
                    g.remote_dma_fused([RemoteDMATransfer(dst_ids=[dst(c) for c in to], dma_engine_mask=m, remote_sem=T.sem[nm],
                                                          srcs=[handed_ap(nm, k, 0)], dsts=[handed_ap(nm, k, d) for d in ds])],
                                       local_sem=T.sem["l0"])
                g.wait_ge(T.sem["l0"], sent)
        return
    Q = {"V": g.vector, "A": g.scalar, "P": g.tensor, "G": g, "S": g.sync}
    ops, lastw, readers, totals, used, line = [], {}, {}, {}, {"d": 0, "l": 0}, {"on": None}

    def rec(q, fn, r, w, c, tok=None, lat=0.0, other=None):
        op = {"q": q, "fn": {q: fn}, "deps": [], "need": False, "tok": tok, "c": c, "lat": lat, "n": len(ops), "after": [],
              "gather": line.pop("gather", False), "mark": False, "w": w[:1]}
        if other:
            op["fn"]["A" if q == "V" else "V"] = other
        if line["on"]:
            op["after"] = line.get((line["on"], q), [])
            line[(line["on"], q)] = [op]
        for k in r:
            op["deps"].append(lastw[k])
            if k.startswith("ps"):
                op["deps"].extend(o for o in readers.get(k, []) if o["q"] != q or other or len(o["fn"]) > 1)
        for k in w:
            if k in lastw:
                op["deps"].append(lastw[k])
            op["deps"].extend(readers.get(k, []))
        for k in r:
            readers.setdefault(k, []).append(op)
        for k in w:
            lastw[k] = op
            readers[k] = []
        ops.append(op)
        return op

    def newsem(kind):
        used[kind] += 1
        return "%s%d" % (kind, used[kind] - 1)

    def dma(q, out, in_, r, w, sem=None, lat=START):
        sem = sem or newsem("d")
        totals[sem] = totals.get(sem, 0) + 16
        return rec(q, lambda: Q[q].dma_start(out, in_).then_inc(T.sem[sem], 16), r, w, 0.1, tok=sem, lat=lat)

    prv, nxt = (me - 1) % N, (me + 1) % N
    near, others = [prv, nxt], [o for o in range(N) if o != me]

    def send(src, place, to, rsem, r, key, before=0, hand=None, behind=None):
        m, senders = -1, len(to)
        for o in to:
            m &= topo.mask(T.cores[me], T.cores[o])
        to = [o for o in to if o not in [(me + d) % N for i, ds in HAND.get(rsem, ()) for d in ds]]
        sem = newsem("l")
        trs = [RemoteDMATransfer(dst_ids=[dst(T.cores[o]) for o in to], dma_engine_mask=m, remote_sem=T.sem[rsem], srcs=[src],
                                 dsts=[place(o) for o in to])]
        if hand:
            trs.append(RemoteDMATransfer(dst_ids=[dst(helpers(me)[i]) for i, ds in HAND[hand]], dma_engine_mask=inside(me),
                                         remote_sem=T.sem["h" + hand], srcs=[src], dsts=[handed_ap(hand, me, 0) for i in HAND[hand]]))
        totals[sem] = ones(m) + (ones(inside(me)) if hand else 0)
        op = rec("G", lambda: g.remote_dma_fused(trs, local_sem=T.sem[sem]), r + ["gq"], ["gq"], ISSUE, tok=sem,
                 lat=START - ISSUE + ROW * 128 * (len(to) + before) / ones(m))
        op["deps"], op["after"] = op["deps"][:len(r)], op["deps"][len(r):]
        for k in r:
            if k[:2] == "yt":
                readers[k].remove(op)
        totals[rsem] = ones(m) * senders
        lastw[key] = {"q": "R", "tok": rsem, "like": op, "behind": behind and (behind[0], ROW * 128 * behind[1] / ones(m))}
        return op

    def size(n):
        return max(64, n) * CY

    def ts(out, in0, s1, s2, o0, o1, r, w, n=64):
        if o1 is None:
            return rec("V", lambda: g.vector.tensor_scalar(out, in0, s1, None, o0), r, w, size(n))
        return rec("V", lambda: g.vector.tensor_scalar(out, in0, s1, s2, o0, o1), r, w, size(n))

    def af(out, in0, scale, bias, r, w, n=64):
        return rec("A", lambda: g.scalar.activation(out, in0, FN.Identity, bias=bias, scale=scale), r, w, size(n),
                   other=lambda: g.vector.tensor_scalar(out, in0, scale, bias, A.mult, A.add))

    def mv(out, in_, r, w, n=64, scale=None):
        if scale is None:
            return rec("A", lambda: g.scalar.activation(out, in_, FN.Copy), r, w, size(n), other=lambda: g.vector.tensor_copy(out, in_))
        return rec("A", lambda: g.scalar.activation(out, in_, FN.Copy, scale=scale), r, w, size(n),
                   other=lambda: g.vector.tensor_scalar(out, in_, scale, None, A.mult))

    def tt(out, a, b, o, r, w, n=64):
        return rec("V", lambda: g.vector.tensor_tensor(out, a, b, o), r, w, size(n))

    def cp(out, in_, r, w, n=64):
        return rec("V", lambda: g.vector.tensor_copy(out, in_), r, w, size(n))

    def ms(out, c, w, n=64):
        return rec("V", lambda: g.vector.memset(out, c), [], w, size(n))

    def tp(out, in_, r, w, n=64):
        return rec("V", lambda: g.vector.transpose(out, in_), r, w, size(n))

    def act(out, in_, fn, r, w, n=64, **kw):
        return rec("A", lambda: g.scalar.activation(out, in_, fn, **kw), r, w, size(n))

    def iota(out, pat, base, cm, w, n=8):
        return rec("G", lambda: g.iota(out, pat, base, cm, allow_small_or_imprecise_dtypes=True), [], w, 0.13 + 2 * n * CY)

    def qz(name, a, n, tile, r, w):
        return rec("V", lambda: g.vector.quantize_mx(T[name + "c"][:, a:a + n], T[name + "s"][:, a:a + n], tile), r, w, 0.012 + 0.0009 * n)

    def mm(bank, n, sn, sa, mn, ma, start, stop, r):
        return rec("P", lambda: g.tensor.matmul_mx(T["ps%d" % bank][:, 0:n], T[sn + "c"][:, sa:sa + 128], T[sn + "s"][:, sa:sa + 128],
                                                   T[mn + "c"][:, ma:ma + n], T[mn + "s"][:, ma:ma + n], start, stop),
                   r, ["ps%d" % bank], (n + 16) * PE)

    def gat(n):
        line["gather"] = True
        return int(65 + 1.5 * n)

    def pick(dn, da, sn, sa, sw, off, k, r, w):
        n = 16 * k
        cp(T[dn + "c"][:, da:da + n].bitcast(dt.uint32), T[sn + "c"][:, sa:sa + sw].bitcast(dt.uint32).indirect(off), r, [w + "c"], gat(n))
        mv(T[dn + "s"][:, da:da + n], T[sn + "s"][:, sa:sa + sw].indirect(off), r, [w + "s"], gat(n))

    ff, kk, cc, of, dd, tb, kb, ti = T.ff, T.kk, T.cc, T.of, T.dd, T.tb, T.kb, T.ti

    dma("A", T.landp[:, 16:32], T.p[:], [], ["lpo"], lat=START + 0.5)
    dma("S", T.xin[:], T.x[:], [], ["xin"], lat=START + 1.2)
    dma("S", T.uin[:], T.u[:], ["lpo"], ["uin"], lat=START + 0.5)

    lastw["gq"] = rec("G", lambda: g.iota(T.pi[:], [[1, 16]], 0, 1), [], ["pi"], 0.13)
    EA, EC, UX, SG, PC, E8, L0, L1, L2 = 0, 8, 16, 24, 40, 44, 52, 60, 68
    iota(T.idn[:], [[-1, 128]], 0, 1, ["idn"], 128)
    iota(kk[:, EA:EA + 8], [[0, 4], [1, 2]], 0, 0, ["k0"])
    iota(kk[:, EC:EC + 8], [[0, 2], [1, 2], [0, 2]], 0, 0, ["k1"])
    rec("G", lambda: g.iota(T.i3[:], [[1, 2], [32, 8]], 64, 0), [], ["i3"], 0.16)
    for t in range(2):
        iota(T.vv[:, 64 * t:64 * t + 64], [[0, 2], [1, 8], [-8, 4]], 8 * t, 0, ["vv%d" % t], 64)
    iota(kk[:, UX:UX + 8], [[0, 2], [32, 4]], 0, 0, ["k7"])
    iota(kk[:, L0:L0 + 8], [[16, 2], [2, 2], [4, 2]], 0, 0, ["kl0"])
    ms(dd[:, 0:2], 0.0, ["dd%d" % a for a in range(4)])
    for a in range(4):
        for i, c in enumerate(DIR[2 * a]):
            if c:
                ms(dd[32 * a:32 * a + 32, i:i + 1], float(c), ["dd%d" % a])
    given = send(T.landp[:, 16:32], lambda o: T.landp[:, 32:48] if o == prv else T.landp[:, 0:16], near, "ap", ["lpo"], "lpa", before=PB)

    fields = [[(0, 15, 0, 1, 1, ["q"]), (0, 7, 0, 3, 2, ["r", "r2"]), (4, 1, 0, 1, 1, ["ch"]), (1, 7, 0, 1, 1, ["q1"]),
               (5, 3, 0, 1, 1, ["a"]), (3, 1, 0, 1, 1, ["w"]), (0, 1, 0, 1, 1, ["b0"])],
              [(3, 7, 0, 1, 1, ["lo"]), (0, 3, 0, 4, 1, ["u", "v1", "v2", "z3"]), (1, 3, 0, 1, 1, ["k"]), (2, 3, 0, 1, 1, ["q2"]),
               (1, 1, 0, 1, 1, ["b1"]), (2, 1, 0, 1, 1, ["k2"])]]
    col, i = {}, 0
    for part in fields:
        i0, names = i, []
        for sh, an, j0, j1, st, nms in part:
            ts(T.fi[:, i:i + len(nms)], T.pi[:, j0:j1:st], sh, an, A.logical_shift_right, A.bitwise_and, ["pi"], ["fi%d" % i])
            names.append("fi%d" % i)
            for nm in nms:
                col[nm], i = ff[:, i:i + 1], i + 1
        cp(ff[:, i0:i], T.fi[:, i0:i], names, [nm for f in part for nm in f[5]])
    taken = [0]

    def lin(name, *terms):
        taken[0] += 1
        out = col[name] = cc[:, taken[0] - 1:taken[0]]
        rest, keys = terms[-1], []
        if isinstance(rest, str):
            rest, keys = col[rest], [rest]
        for f, nm in terms[:-1]:
            if isinstance(f, str):
                af(out, col[nm], col[f], rest, [nm, f] + keys, [name])
            else:
                af(out, col[nm], float(f), rest, [nm] + keys, [name])
            rest, keys = out, [name]
        return name

    places = {}

    def listed(name, n):
        a = sum(x[1] + x[1] % 2 for x in places.values())
        places[name] = (a, n)
        return of[:, a:a + n]

    def lst(name, a=0, b=None):
        return of[:, places[name][0] + a:places[name][0] + (places[name][1] if b is None else b)]

    def row_list(name, n, row, f, c, keys):
        ts(listed(name, n), row, float(f), col[c], A.mult, A.add, keys + [c], [name])

    ms(T.sx[:, 128:512], 0.0, ["sxz"], 192)
    for b in range(4):
        mv(T.sx[:, b:128:4], T.xin[:, b:1024:32], ["xin"], ["sx%d" % b])
    qz("snd", 0, 128, T.sx[:], ["sx0", "sx1", "sx2", "sx3", "sxz"], ["snd"])
    for nm in ("ac", "asc"):
        src = T.snds[:, 0:32] if nm == "asc" else T.sndc[:, 0:32].bitcast(dt.uint8)
        lastw["gone" + nm[1:-1]] = send(src, lambda o: handed_ap(nm, me, 0), others, nm, ["snd"], "l" + nm, before=FIRSTB, hand=nm, behind=(given, 9))
    row_list("own", 2, kk[:, EA:EA + 2], 16, "q", ["k0"])
    pick("ls", 32 * me, "snd", 0, 128, lst("own"), 2, ["snd", "own"], "lso")
    qz("qa", 0, 256, T.xin[:], ["xin"], ["qa"])
    lsk = ["lsoc", "lsos", "lac", "lasc"]
    for o in [iota(kk[:, SG:SG + 16], [[1, 8], [128, 2]], 0, 0, ["k8"], 16), iota(kk[:, PC:PC + 1], [[0, 1]], 32, 1, ["p32"]),
              iota(kk[:, E8:E8 + 8], [[1, 2], [0, 4]], 0, 0, ["ke8"]),
              iota(kk[:, L1:L1 + 8], [[4, 2], [1, 2], [2, 2]], 0, 0, ["kl1"]), iota(kk[:, L2:L2 + 8], [[2, 2], [16, 2], [1, 2]], 0, 0, ["kl2"]),
              iota(kb[:, 4:20], [[0, 4], [1, 2], [0, 2]], 0, 0, ["kb0"], 16), iota(kb[:, 20:28], [[1, 2], [-80, 2], [0, 2]], 88, 0, ["kb1"]),
              iota(kb[:, 28:32], [[1, 2], [0, 2]], 0, 0, ["kb2"]), iota(kb[:, 32:40], [[0, 8]], 0, 0, ["kb3"]),
              iota(kb[:, 34:38], [[32, 2], [1, 2]], 0, 0, ["kb3"]), iota(kb[:, 0:4], [[32, 2], [1, 2]], 0, 0, ["kb4"]),
              iota(T.fl[:, 0:256], [[0, 256]], 0, 0, ["fl00", "fl01"], 256), iota(T.fl[:, 256:512], [[0, 256]], 0, 0, ["flz"], 256),
              iota(T.fl[:, 512:768], [[0, 256]], 0, 0, ["fl10", "fl11"], 256), iota(T.lq[:, 128:136], [[0, 8]], 0, 0, ["lqz"]),
              iota(T.land1[:, 24:40], [[0, 16]], 0, 0, ["land1z"], 16), iota(T.land2[:, 24:40], [[0, 16]], 0, 0, ["land2z"], 16),
              iota(T.po[:, 16:32], [[0, 16]], 0, 0, ["poz"], 16),
              iota(T.w2[:, 0:4], [[0, 2], [32, 2]], 0, 0, ["w2a"]), iota(T.w2[:, 4:8], [[32, 2], [0, 2]], 0, 0, ["w2b"]),
              iota(T.w2[:, 12:20], [[0, 2], [16, 2], [0, 2]], 16, 0, ["w2c"])]:
        o["after"], lastw["gq"] = [lastw["gq"]], o
    col["p32"] = kk[:, PC:PC + 1]

    ms(T.ez[:], 0.0, ["ez"], 260)
    ts(T.idn[:], T.idn[:], 0.0, None, A.is_equal, None, ["idn"], ["idn"])
    lin("nev", (1, "ch"), -1.0)
    lin("nod", (-1, "ch"), 0.0)
    for v, nm in enumerate([None, "nev", "nod"]):
        act(T.ez[:, 3:515:4], T.idn[:], FN.Identity, ["idn"] + ([nm] if nm else []), ["ez"], 128, scale=col[nm] if nm else 1.0)
        for b in range(4):
            qz("qe", 512 * v + 128 * b, 128, T.ez[:, 3 - b:515 - b], ["ez"], ["qe%d%d" % (v, b)])

    ts(T.i3[:], T.i3[:], 255, None, A.bitwise_and, None, ["i3"], ["i3"])
    row_list("oeo", 16, T.i3[:], 1, lin("q2x", (2, "q"), 0.0), ["i3"])
    pick("qx1", 0, "qa", 0, 256, lst("oeo"), 16, ["qa", "oeo"], "qx1")

    for i, nm in enumerate(["dr", "dc", "ndr"]):
        col[nm] = dd[:, i:i + 1]
    dcl, drt, dra, dcm, dr8, dc8, dl8 = dd[:, 4:8], dd[:, 8:12], dd[:, 12:16], dd[:, 16:18], dd[:, 20:28], dd[:, 28:36], dd[:, 36:44]
    af(col["ndr"], col["dr"], -1.0, 0.0, ["dd%d" % a for a in range(4)], ["ndr", "dr", "dc"])
    af(dcl, kk[:, EC:EC + 4], col["ndr"], col["dc"], ["k1", "dr"], ["dcl"])
    lin("rg", ("dc", "ch"), "dr")
    row_list("or0", 4, kk[:, EC:EC + 4], 1, lin("rb", (8, "rg"), (2, "r2"), (48, "w"), 16.0), ["k1"])

    af(T.w1[:, 0:4], dcl, 4.0, col[lin("c2", (1, "ch"), (1, "q2x"), 32.0)], ["dcl", "c2"], ["w1a"])
    af(T.w1[:, 4:5], col["a"], -8.0, col[lin("j8", (8, "q1"), 32.0)], ["a", "j8"], ["w1b"])
    cp(T.i1[:, 0:5], T.w1[:, 0:5], ["w1a", "w1b"], ["i1"])
    ts(T.i1[:, 0:5], T.i1[:, 0:5], 31, None, A.bitwise_and, None, ["i1"], ["i1"])
    ts(T.i2[:, 0:4], T.i1[:, 0:4], 16, None, A.bitwise_and, None, ["i1"], ["i2"])
    af(T.w1[:, 40:44], kk[:, EC:EC + 4], 16.0, 0.0, ["k1"], ["e16"])
    tt(T.w1[:, 40:44], T.w1[:, 40:44], T.i1[:, 0:4], A.add, ["e16", "i1"], ["e16"])
    tt(T.w1[:, 40:44], T.w1[:, 40:44], T.i2[:, 0:4], A.add, ["e16", "i2"], ["e16"])
    cp(listed("oc0", 4), T.w1[:, 40:44], ["e16"], ["oc0"])
    row_list("ol0", 2, kk[:, EA:EA + 2], 32, lin("f0", (16, "w"), "r"), ["k0"])
    col["jb"] = T.w1[:, 44:45]
    cp(col["jb"], T.i1[:, 4:5], ["i1"], ["jb"])
    lin("lb", (8, "jb"), (32, "b0"), 0.0)
    row_list("lq0", 8, kk[:, L0:L0 + 8], 1, lin("lb0", (1, "ch"), (1, "lb"), 8.0), ["kl0"])

    def spread(x):
        rot, rn, sem, n = T["rot%d" % x], "rot%d" % x, newsem("d"), 128 if x == 2 else 64
        for j in range(1, 4):
            dma("S", rot[0:128 - 32 * j, n * j:n * j + n], rot[32 * j:128, 0:n], [rn, "gone"], [rn + "j%d" % j], sem, lat=START + 1.2)
            dma("S" if x else "A", rot[128 - 32 * j:128, n * j:n * j + n], rot[0:32 * j, 0:n], [rn, "gone"], [rn + "k%d" % j], sem, lat=START + 1.2)
        keys = [rn + jk + str(j) for jk in "jk" for j in range(1, 4)]
        mv(T.lq[:, 0:128], rot[:].indirect(lst("lq%d" % x)), [rn, "lq%d" % x] + keys, ["lq"], gat(128))
        tt(T.df[:], T.lq[:, 0:128], T.lq[:, 1:129], A.subtract, ["lq", "lqz"], ["df"], 256)
        if x:
            mv(T.df[:, 7:128:8], T.lq[:, 7:128:8], ["lq"], ["df"])

    ts(T.landp[:, 48:96], T.landp[:, 0:48], 257.0, None, A.mult, None, ["lpo", "lpa"], ["lpr"])
    ts(T.landp[:, 48:96], T.landp[:, 48:96], 3, 255, A.logical_shift_right, A.bitwise_and, ["lpr"], ["lpr"])
    cp(T.a1[:, 0:64], T.landp[:].indirect(lst("or0")), ["lpr", "or0"], ["a10"], gat(64))
    tp(T.gg[:, 0:64], T.a1[:, 0:64], ["a10"], ["gg0"])
    mv(T.a3[:, 0:64], T.gg[:, 0:64].indirect(lst("oc0")), ["gg0", "oc0"], ["a3"], gat(64))
    tp(T.rot0[:, 0:64], T.a3[:, 0:64], ["a3"], ["rot0"])
    cp(T.ol[:, 0:32], T.rot0[:, 0:64].indirect(lst("ol0")), ["rot0", "ol0"], ["cand0"], gat(32))
    spread(0)
    for o in [dma("S", T.qwc[:].bitcast(dt.uint8), T.wc[:], lsk, ["qwc"], lat=START + 2.0),
              dma("S", T.qws[:], T.ws[:], lsk, ["qws"], lat=START + 2.0)]:
        o["after"] = [lastw["rot0" + jk + str(j)] for jk in "jk" for j in range(1, 4)]

    val = cc[:, 63:64]
    ts(val, col["r"], col["lo"], None, A.is_gt, None, ["r", "lo"], ["val"])
    qz("qu", 0, 128, T.uin[:], ["uin"], ["qu"])
    row_list("ou0", 8, kk[:, UX:UX + 8], 1, lin("ux", (16, "w"), 0.0), ["k7"])
    row_list("ou1", 8, kk[:, UX:UX + 8], 0, lin("uy", (16, "r"), 0.0), ["k7"])
    pick("qup", 0, "qu", 0, 128, lst("ou0", 0, 16), 16, ["qu", "ou0", "ou1"], "qup")
    ts(T.va[:], T.vv[:], col["r"], None, A.is_equal, None, ["vv0", "vv1", "r"], ["va"])
    ts(T.vb[:], T.vv[:], col["lo"], None, A.is_equal, None, ["vv0", "vv1", "lo"], ["vb"])
    tt(T.va[:], T.va[:], T.vb[:], A.subtract, ["va", "vb"], ["va"], 256)
    for a in range(4):
        act(T.cb[:, 128 * a:128 * a + 128], T.va[:], FN.Identity, ["va", "val"], ["cb%d" % a], 128, scale=val)
    qz("qc", 0, 128, T.cb[:], ["cb0", "cb1", "cb2", "cb3"], ["qc"])
    lin("tg", (2, "r"), (4, "a"), (2, "w"), -14.0)
    row_list("osg", 16, kk[:, SG:SG + 16], 1, lin("q8", (8, "q"), 0.0), ["k8"])

    af(drt, kk[:, EC:EC + 4], col["dc"], col["dr"], ["k1", "dr"], ["drt"])
    af(dra, kk[:, EA:EA + 4], col["dc"], col["dr"], ["k0", "dr"], ["dra"])
    af(dr8, kk[:, E8:E8 + 8], col["dc"], col["dr"], ["ke8", "dr"], ["dr8"])
    ts(dd[:, 36:44:2], dd[:, 20:28:2], 0.0, None, A.min, None, ["dr8"], ["dl0"])
    ts(dd[:, 37:44:2], dd[:, 21:28:2], 0.0, None, A.max, None, ["dr8", "dl0"], ["dl1"])
    lin("sw", (-1, "w"), 2.0)
    lin("sw2", (-2, "w"), 4.0)
    lin("u4", (1, "u"), 4.0)
    lin("q3", (1, "q"), 3.0)
    lin("ve", (2, "v1"), 8.0)
    lin("vc", (-80, "k2"), (1, "ve"), 80.0)
    lin("km", (-2, "k2"), 2.0)
    lin("vn", (-1, "ve"), 24.0)
    lin("vm", ("k2", "vn"), "ve")
    lin("vs", (1, "q2x"), float(112 - 8 * me))
    lin("z6", (2, "z3"), 0.0)
    lin("u6", (1, "u"), 6.0)
    lin("ij", (1, "q1"), (1, "rg"), 1.0)
    rows = [[(0, dra, "dra", 2, "q3", 4, "vs"), (4, drt, "drt", "sw", "u4", "sw2", "vc"), (8, drt, "drt", 2, "u4", 4, "ve"), (12,)],
            [(12, drt, "drt", 1, "u4", "km", "vm"), (16, drt, "drt", 1, "u4", 2, "ve"), (20, dl8, "dl1", 1, "u6", 2, "z6"),
             (28, drt, "drt", 1, "u4", 0, 0.0), (32, col["r2"], "r2", 1, 0.0, 2, "w"),
             (33, col["rg"], "rg", 1, lin("b11", (1, "b1"), 1.0), 0, 0.0), (34, dra, "dra", 1, "q3", 2, "vs"),
             (38, col["ij"], "ij", 1, 0.0, 8, 0.0), (39,)]]
    for z, masks in (("0", ((40, 44, 57), (44, 52, 249))), ("1", ((52, 74, 249), (74, 78, 57), (78, 79, 32)))):
        part, keys = rows[int(z)], [[], []]
        for (c0, src, name, f0, c1, f1, c2), then in zip(part, part[1:]):
            for side, f, c in ((0, f0, c1), (1, f1, c2)):
                keys[side].append("tb%d" % (40 * side + c0))
                af(tb[:, 40 * side + c0:40 * side + then[0]], src, col[f] if f in col else float(f), col.get(c, c),
                   [name] + [y for y in (f, c) if y in col], keys[side][-1:])
        a, b, tv = part[0][0], part[-1][0], ["tv%d" % m[0] for m in masks]
        cp(ti[:, a:b], tb[:, a:b], keys[0], ["tu" + z])
        tt(ti[:, 40 + a:40 + b], tb[:, 40 + a:40 + b], kb[:, a:b], A.add, keys[1] + ["kb0", "kb1", "kb2", "kb3", "kb4"], tv)
        ts(ti[:, a:b], ti[:, a:b], 3, None, A.bitwise_and, None, ["tu" + z], ["tu" + z])
        ts(ti[:, a:b], ti[:, a:b], 5.0, None, A.mult, None, ["tu" + z], ["tu" + z])
        ts(ti[:, a:b], ti[:, a:b], 6, None, A.bitwise_and, None, ["tu" + z], ["tu" + z])
        for (c0, c1, m), key in zip(masks, tv):
            ts(ti[:, c0:c1], ti[:, c0:c1], m, None, A.bitwise_and, None, [key], [key])
        tt(tb[:, a:b], ti[:, a:b], ti[:, 40 + a:40 + b], A.add, ["tu" + z] + tv, ["tr" + z] + keys[0])
    for x in range(2):
        ts(listed("osr%d" % x, 4), tb[:, 34 * x:34 * x + 4], 8.0, None, A.add, None, ["tr%d" % x], ["osr%d" % x])
        cp(listed("orow%d" % x, 8 + 8 * x), tb[:, 4 + 8 * x:12 + 16 * x], ["tr%d" % x], ["orow%d" % x])
    ts(listed("osc", 5), tb[:, 28:33], 8.0, 7.0, A.mult, A.add, ["tr1"], ["osc"])
    ts(listed("oj", 1), tb[:, 38:39], col[lin("b16", (16, "b0"), 0.0)], None, A.add, None, ["tr1", "b16"], ["oj"])
    col["out"] = cc[:, 62:63]
    act(col["out"], col["rg"], FN.Relu, ["rg", lin("sg", (-2, "b1"), 1.0)], ["out"], scale=col["sg"])
    lin("kf", (-32, "b1"), -32.0)
    lin("kc", (1, "b16"), 64.0)
    ts(listed("ok", 1), tb[:, 33:34], col[lin("ks", ("kf", "out"), "kc")], None, A.add, None, ["tr1", "ks"], ["ok"])
    row_list("og3", 4, kk[:, EC:EC + 4], 8, lin("k16", (16, "k"), 7.0), ["k1"])
    lin("fm", (1, "q1"), "b16")
    cp(listed("ofm", 1), col["fm"], ["fm"], ["ofm"])
    row_list("ol1", 2, kk[:, EA:EA + 2], 32, lin("fm8", (1, "fm"), 8.0), ["k0"])
    row_list("ol2", 2, kk[:, EA:EA + 2], 64, lin("f3", (32, "b0"), (16, "b1"), "q2"), ["k0"])
    lin("c16", (16, "ch"), 0.0)
    row_list("lq1", 8, kk[:, L1:L1 + 8], 1, lin("lb1", (1, "lb"), (1, "c16"), 8.0), ["kl1"])
    row_list("lq2", 8, kk[:, L2:L2 + 8], 1, lin("lb2", (2, "lb1"), -16.0), ["kl2"])

    af(dcm, kk[:, EA:EA + 2], col["ndr"], col["dc"], ["k0", "dr"], ["dcm"])
    af(dc8, kk[:, E8:E8 + 8], col["ndr"], col["dc"], ["ke8", "dr"], ["dc8"])
    lin("cg", ("ndr", "ch"), "dc")
    lin("q16", (1, "q"), 16.0)
    lin("k4", (4, "k"), 16.0)
    for at, n, src, f, c in [(8, 2, dcm, 2, "q16"), (10, 2, dcm, 1, "q16"), (12, 4, dcl, 1, "q16"), (16, 1, col["cg"], 2, "k4"),
                             (17, 1, col["cg"], 1, "k4"), (18, 2, dcm, 1, "p32"), (20, 8, dc8, 1, "q16")]:
        af(T.w1[:, at:at + n], src, float(f), col[c], [{2: "dcm", 4: "dcl", 1: "cg", 8: "dc8"}[n], c], ["w1%d" % at])
    tt(T.w1[:, 20:28], T.w1[:, 20:28], T.w2[:, 12:20], A.add, ["w120", "w2c"], ["w120"])
    cp(T.i1[:, 8:18], T.w1[:, 8:18], ["w1%d" % at for at in (8, 10, 12, 16, 17)], ["i15"])
    cp(T.i1[:, 18:28], T.w1[:, 18:28], ["w118", "w120"], ["i31"])
    ts(T.i1[:, 8:18], T.i1[:, 8:18], 15, None, A.bitwise_and, None, ["i15"], ["i15"])
    ts(T.i1[:, 18:28], T.i1[:, 18:28], 31, None, A.bitwise_and, None, ["i31"], ["i31"])
    tt(T.w2[:, 20:28], T.w2[:, 0:8], T.i1[:, 8:16], A.add, ["w2a", "w2b", "i15"], ["w2m"])
    ts(listed("ocol", 8), T.w2[:, 20:28], col["c16"], None, A.add, None, ["w2m", "c16"], ["ocol"])
    lin("sb", (32, "b0"), "ux")
    for x in range(2):
        ts(listed("osd%d" % x, 1), T.i1[:, 16 + x:17 + x], col["sb"], None, A.add, None, ["i15", "sb"], ["osd%d" % x])
    tt(T.w2[:, 28:30], T.w2[:, 0:2], T.i1[:, 18:20], A.add, ["w2a", "i31"], ["w2n"])
    cp(listed("oc3", 2), T.w2[:, 28:30], ["w2n"], ["oc3"])
    ts(T.i2[:, 8:16], T.i1[:, 20:28], 65.0, None, A.mult, None, ["i31"], ["i65"])
    ts(T.i2[:, 8:16], T.i2[:, 8:16], 1, 47, A.logical_shift_right, A.bitwise_and, ["i65"], ["i65"])
    act(T.w2[:, 32:40], dr8, FN.Abs, ["dr8"], ["nz"])
    af(T.w2[:, 32:40], T.w2[:, 32:40], col[lin("nx", (-32, "ch"), 16.0)], col["c16"], ["nz", "nx", "c16"], ["nz"])
    af(T.w2[:, 40:48], kk[:, E8:E8 + 8], 64.0, 0.0, ["ke8"], ["e64"])
    tt(T.w2[:, 32:40], T.w2[:, 32:40], T.w2[:, 40:48], A.add, ["nz", "e64"], ["nz"])
    tt(T.w2[:, 32:40], T.w2[:, 32:40], T.i2[:, 8:16], A.add, ["nz", "i65"], ["nz"])
    cp(listed("ocl3", 8), T.w2[:, 32:40], ["nz"], ["ocl3"])

    def unpack(src, n, keys, to, width, name):
        for b in range(4):
            mm(4 + b, n, "qe", 128 * b, src, 0, True, True, ["qe0%d" % b] + keys)
        for b in range(4):
            mv(to[:, width * b:width * b + n], T["ps%d" % (4 + b)][:, 0:n], ["ps%d" % (4 + b)], [name + str(b)], n)

    def chunk(bank, n, off, key, src, c0, skeys, y0, pieces, new=None):
        fs, width, fname = (T.bt, 256, "bt") if src[1] == "s" else (T.fo, FO, "fo")
        slots = range(y0 // 128, (y0 + n + 127) // 128)
        for b in range(4):
            mm(bank + b, n, "qe", 128 * b, src, c0, True, False, ["qe0%d" % b] + skeys)
        k0, k = new or (0, n)
        for b in range(4):
            mv(T.yt[:, 4 * (y0 + k0) + b:4 * (y0 + k0 + k):4], T.bt[:, 256 * b:256 * b + 256].indirect(off), ["bt%d" % b, key],
               ["yt%d%d" % (s, b) for s in slots], gat(k), scale=0.015625)
        qz("qy", y0, n, T.yt[:, 4 * y0:4 * (y0 + n)], ["yt%d%d" % (s, b) for s in slots for b in range(4)], ["qy%d" % s for s in slots])
        for b in range(4):
            mm(bank + b, n, "qw", 128 * b, "qy", y0, False, True, ["qwc", "qws"] + ["qy%d" % s for s in slots])
        for b in range(4):
            for t0, x0, m, st, names in pieces:
                tt(T.xt[:, 4 * x0 + b:4 * (x0 + st * (m - 1)) + b + 1:4 * st], T["ps%d" % (bank + b)][:, t0:t0 + m],
                   fs[:, width * b + c0 + t0:width * b + c0 + t0 + m], A.max, ["ps%d" % (bank + b), fname + str(b)],
                   ["xt%s%d" % (s, b) for s in names], m)

    def state(name, a, slot, key):
        qz(name, a, 128, T.xt[:, 512 * slot:512 * slot + 512], ["xt%d%s%d" % (slot, s, b) for s in "ab" for b in range(4)], [key])

    def turn_twice(i, win, keys, rows, cols, ckey, out, okey):
        a1, gg, a2, z = T.a1[:, 64 * i:64 * i + 64], T.gg[:, 64 * i:64 * i + 64], T.a2[:, 32 * i:32 * i + 32], str(i)
        mv(a1, win.indirect(rows), keys, ["a1" + z], gat(64))
        tp(gg, a1, ["a1" + z], ["gg" + z])
        mv(a2, gg.indirect(cols), ["gg" + z, ckey], ["a2" + z], gat(32))
        tp(out, a2, ["a2" + z], [okey])

    def read_list(i, win, keys, rows, x, okey):
        uu = T.uu[:, 32 * i:32 * i + 32]
        turn_twice(i, win, keys, rows, lst("ocol", 2 * x, 2 * x + 2), "ocol", uu, "uu%d" % i)
        cp(T[okey][:, 0:16], uu.indirect(lst("ofm")), ["uu%d" % i, "ofm"], [okey], gat(16))["mark"] = True

    def differences(x, hf):
        rd, z = x + 1, str(hf)
        qx, pa = "qx%d" % rd, "pa%d" % rd
        win, keys = ("ls", lsk) if x == 0 else ("qs%d" % rd, ["qs%ds" % rd, "qs%dt" % rd])
        late = x + hf == 2 and x > 0
        for e in ((0, 1, 2) if late else (2, 0, 1)):
            c0, nm, o = 256 * hf + 128 * e, pa + str(2 * hf + e), 32 * x + 16 * e + 8 * hf
            if e < 2:
                pick(pa, c0, win, 0, 256, T.ol[:, o:o + 8], 8, keys + ["cand%d" % x], nm)
            for b in range(4):
                if e < 2:
                    mm(4 * hf + b, 128, "qe", 512 * (e + 1) + 128 * b, pa, c0, late and e == 0, e == 1 and not late,
                       ["qe%d%d" % (e + 1, b), nm + "c", nm + "s"])
                else:
                    mm(4 * hf + b, 128, "qe", 128 * b, qx, 128 * hf, not late, late, ["qe0%d" % b] + (["qx1c", "qx1s"] if x == 0 else [qx + z]))
        for b in range(4):
            mv(T.zt[:, 512 * hf + b:512 * hf + 512:4], T["ps%d" % (4 * hf + b)][:, 0:128], ["ps%d" % (4 * hf + b)], ["zt" + z + str(b)], 128, scale=-1.0)
        qz("qz", 128 * hf, 128, T.zt[:, 512 * hf:512 * hf + 512], ["zt" + z + str(b) for b in range(4)], ["qz" + z])["mark"] = True

    def deal(hf):
        z, by, bx, c = str(hf), "ps%d" % (2 * hf), "ps%d" % (2 * hf + 1), slice(64 * hf, 64 * hf + 64)
        mm(2 * hf, 128, "qup", 128, "qz", 128 * hf, True, True, ["qupc", "qups", "qz" + z])
        mm(2 * hf + 1, 128, "qup", 0, "qz", 128 * hf, True, True, ["qupc", "qups", "qz" + z])
        for t in range(2):
            sy = T.sy[:, 128 * hf + 64 * t:128 * hf + 64 * t + 64]
            act(sy, T[by][:, 64 * t:64 * t + 64], FN.Copy, [by], ["sy%d%d" % (hf, t)])
            tt(T.fl[:, 512 * hf + t:512 * hf + 256:4], T[bx][:, 64 * t:64 * t + 64], sy, A.is_ge, [bx, "sy%d%d" % (hf, t)], ["fl%d%d" % (hf, t)])
        qz("qf", 128 * hf, 128, T.fl[:, 256 * hf:256 * hf + 512], ["fl" + z + "0", "fl" + z + "1", "flz"], ["qf" + z])
        mm(2 * hf, 128, "qc", 0, "qf", 128 * hf, True, True, ["qc", "qf" + z])
        ts(T.ns[:, c], T[by][:, c], col["tg"], None, A.not_equal, None, [by, "tg"], ["ns" + z])
        tp(T.nt[:, c], T.ns[:, c], ["ns" + z], ["nt" + z])
        rec("V", lambda: g.vector.tensor_tensor_scan(T.sc[:, c], T.nt[:, c], T.df[:, c], 0.0, A.mult, A.add), ["nt" + z, "df"], ["sc" + z], size(64))

    differences(0, 0)
    differences(0, 1)
    for x in range(3):
        rd = x + 1
        land, ln, qx, nq, qs, ns = T["land%d" % rd], "land%d" % rd, "qx%d" % rd, "qx%d" % (rd + 1), "qs%d" % rd, "qs%d" % (rd + 1)
        deal(0)
        deal(1)
        if x == 0:
            pick(qs, 0, "ls", 0, 256, lst("osg"), 16, lsk + ["osg"], qs)
        seeds = [qs + "c", qs + "s"] if x == 0 else [qs + "s", qs + "t"]
        own = [["qx1c", "qx1s"], [qx + "0", qx + "1"], [qx + "0", qx + "1", qx + "c", qx + "s"]][x]
        unpack(qs, 256, seeds, T.bt, 256, "bt")
        unpack(qx, (256, 256, 288)[x], own, T.fo, FO, "fo")
        if x == 2:
            break
        for hf in range(2):
            mine, dealt = land[:, 88 - 80 * hf:96 - 80 * hf], T.sc[:, 64 * hf + 7:64 * hf + 64:8]
            if x:
                mv(mine, dealt, ["sc%d" % hf], [ln + "o%d" % hf])
            else:
                tt(mine, dealt, T.lq[:, 64 * hf + 8:64 * hf + 72:8], A.add, ["sc%d" % hf, "lq", "lqz"], [ln + "o%d" % hf])

        def slot(c0, turn, ld=land):
            return lambda o: ld[:, c0 + 8 * ((me - o + turn) % N):c0 + 8 * ((me - o + turn) % N) + 8]

        lastw["left"] = send(land[:, 88:96], slot(40, 6), near, "an%d" % rd, [ln + "o0"], ln + "n0", before=0.3, hand="af%d" % rd)
        far = send(land[:, 88:96], slot(40, 6), [o for o in others if o not in near], "af%d" % rd, [ln + "o0"], ln + "f", before=FARB)
        if x == 1:
            read_list(0, T.sc[:, 0:64], ["sc0", "osc"], lst("osc", 0, 4), x, "oi")
            chunk(0, 128, T.oi[:, 0:4], "oi", qx, 0, own, 0, [(0, 128, 64, 2, ["1a"])], (0, 64))
        send(land[:, 8:16], slot(0, 1), near, "ao%d" % rd, [ln + "o1"] + [["left"], ["yt00", "yt01", "yt02", "yt03"]][x], ln + "n1", behind=(far, 2))
        both = [ln + s for s in ("o0", "o1", "n0", "n1", "f", "z")] + ["orow%d" % x]
        if x == 0:
            read_list(0, land[:, 80:104], [ln + "o0", ln + "n0", "orow0"], lst("orow0", 4, 8), x, "oi")
            chunk(4, 128, T.oi[:, 0:8], "oi", qx, 0, own, 0, [(0, 0, 128, 1, ["0a", "0b"])])
            state(nq, 0, 0, nq + "0")
            read_list(1, land[:, 0:104], both, lst("orow0", 0, 4), x, "om")
            mv(T.a3[:, 0:64], T.gg[:, 64:128].indirect(lst("ocol", 4, 8)), ["gg1", "ocol"], ["a3"], gat(64))
            tp(T.rot1[:, 0:64], T.a3[:, 0:64], ["a3"], ["rot1"])
            cp(T.ol[:, 32:64], T.rot1[:, 0:64].indirect(lst("ol1")), ["rot1", "ol1"], ["cand1"], gat(32))
        else:
            mv(land[:, 104:112], T.sc[:, 71:128:8], ["sc1"], [ln + "o2"])
            read_list(1, land[:, 80:112], [ln + "o0", ln + "o2", ln + "n0", "orow1"], lst("orow1", 0, 4), x, "om")
            chunk(4, 128, T.om[:, 4:12], "om", qx, 64, own, 128, [(0, 0, 64, 2, ["0a"]), (64, 129, 64, 2, ["1b"])])
            state(nq, 128, 1, nq + "1")
            mv(T.a4[:], land[:, 0:104].indirect(lst("orow1", 8, 16)), both, ["a4"], gat(128))
            tp(T.g4[:], T.a4[:], ["a4"], ["g4"])
            mv(T.a3[:], T.g4[:].indirect(lst("ocl3")), ["g4", "ocl3"], ["a3"], gat(128))
            tp(T.rot2[:, 0:128], T.a3[:], ["a3"], ["rot2"])
            cp(T.ol[:, 64:96], T.rot2[:, 0:128].indirect(lst("ol2")), ["rot2", "ol2"], ["cand2"], gat(32))
        spread(rd)
        mv(T.s1[:], land[:, 32:104].indirect(lst("osr%d" % x)), [ln + "o0", ln + "n0", ln + "f", ln + "z", "osr%d" % x], ["s1"], gat(64))
        tp(T.s2[:], T.s1[:], ["s1"], ["s2"])
        cp(T.osd[:], T.s2[:].indirect(lst("osd%d" % x)), ["s2", "osd%d" % x], ["os"], gat(16))["mark"] = True
        for hf in range(2):
            chunk(4 * hf, 128, T.osd[:, 8 * hf:8 * hf + 8], "os", qs, 128 * hf, seeds, 256 + 128 * hf,
                  [(0, 256 + 128 * hf, 128, 1, ["%da" % (2 + hf), "%db" % (2 + hf)])])
            state(ns, 128 * hf, 2 + hf, ns + "st"[hf])
        if x == 0:
            dma("S", T.vin[:], T.v[:], [ns + "s"], ["vin"], lat=START + 1.7)
            qz("qv", 0, 128, T.vin[:], ["vin"], ["qv"])
        if x == 1:
            read_list(2, land[:, 0:24], [ln + "o1", ln + "n1", "orow1"], lst("orow1", 4, 8), x, "oe")
            chunk(0, 128, T.oe[:, 4:8], "oe", qx, 128, own, 0, [(64, 1, 64, 2, ["0b"])], (64, 64))
            state(nq, 0, 0, nq + "0")
        differences(rd, 0)
        if x == 0:
            chunk(4, 128, T.om[:, 8:16], "om", qx, 128, own, 128, [(0, 128, 128, 1, ["1a", "1b"])])
            state(nq, 128, 1, nq + "1")
        differences(rd, 1)
        if x == 1:
            sem = newsem("d")
            dma("S", T.qx3c[:, 256:288].bitcast(dt.uint8), T.qx3c[:, 0:32].bitcast(dt.uint8), [nq + "0"], [nq + "c"], sem, lat=START + 0.6)
            dma("S", T.qx3s[:, 256:288], T.qx3s[:, 0:32], [nq + "0"], [nq + "s"], sem, lat=START + 0.6)

    for hf in range(2):
        turn_twice(hf, T.sc[:, 64 * hf:64 * hf + 64], ["sc%d" % hf, "og3"], lst("og3"), lst("oc3"), "oc3",
                   land[:, 64 + 32 * hf:96 + 32 * hf], ln + "o%d" % hf)
    send(land[:, 64:96], lambda o: land[:, 32:64] if o == prv else land[:, 0:32], near, "an3", [ln + "o0"], ln + "n")
    cp(T.oi[:, 0:16], land[:, 64:128].indirect(lst("oj")), [ln + "o0", ln + "o1", "oj"], ["oi"], gat(16))["mark"] = True
    chunk(4, 192, T.oi[:, 4:16], "oi", qx, 96, own, 128, [(0, 64, 192, 1, ["0b", "1a", "1b"])])
    cp(T.om[:], land[:, 0:96].indirect(lst("ok")), [ln + "o0", ln + "n", "ok"], ["om"], gat(16))["mark"] = True
    chunk(0, 128, T.om[:, 0:4], "om", qx, 0, own, 0, [(32, 0, 64, 1, ["0a"])], (32, 64))
    cp(T.i2[:], T.sc[:].indirect(lst("osc", 4, 5)), ["sc0", "sc1", "osc"], ["pn", "i2", "i65"], gat(16))
    ts(T.i2[:], T.i2[:], 257.0, None, A.mult, None, ["pn"], ["pn"])
    ts(T.i2[:], T.i2[:], 5, 255, A.logical_shift_right, A.bitwise_and, ["pn"], ["pn"])
    cp(T.po[:, 0:16], T.i2[:], ["pn"], ["po"])
    tp(T.pt[:], T.po[:], ["po", "poz"], ["pt"])
    sem = newsem("d")
    for a in range(4):
        dma("S", T.op[2 * a:2 * a + 2, :], T.pt[32 * a:32 * a + 16, :], ["pt"], [], sem)

    for hf in (1, 0):
        state("qx4", 128 * hf, hf, "qx4%d" % hf)
        mm(4 * hf, 128, "qv", 0, "qx4", 128 * hf, True, True, ["qv", "qx4%d" % hf])
    mv(T.ysb[:, 96:224], T.ps4[:, 0:128], ["ps4"], ["y1"], 128)
    cp(T.ysb[:, 224:256], T.ps0[:, 0:32], ["ps0"], ["y2"])
    cp(T.ysb[:, 0:96], T.ps0[:, 32:128], ["ps0"], ["y0"], 96)
    dma("A", T.y[:], T.ysb[:], ["y0", "y1", "y2"], [], lat=START + 0.9)
    sem = newsem("d")
    for i, (t0, j0, n) in enumerate([(32, 0, 224), (0, 224, 32)]):
        dma("SA"[i], T.oc[:, 4 * j0:4 * (j0 + n)], T.qx4c[:, t0:t0 + n].bitcast(dt.uint8), ["qx40", "qx41"], [], sem, lat=START + 1.2)
        for k in range(4):
            dma("SA"[i and k > 1], T.osc[4 * k:4 * k + 4, j0:j0 + n], T.qx4s[32 * k:32 * k + 4, t0:t0 + n], ["qx40", "qx41"], [], sem, lat=START + 0.5)

    if "order" not in PLAN:
        before = []
        for op in ops:
            gaps = {a["n"]: 0.0 for a in op["after"]}
            for d in op["deps"]:
                a = d.get("like", d)
                gaps[a["n"]] = 0.0 if op["q"] == "P" and a["q"] == "P" else a["lat"] + WAKE
                if d.get("behind"):
                    a = d["behind"][0]
                    gaps[a["n"]] = max(gaps.get(a["n"], 0.0), a["lat"] + WAKE + d["behind"][1])
            before.append(list(gaps.items()))
        PLAN["ops"] = ops
        PLAN["order"], PLAN["queue"] = lay_out(ops, before)
    order = [ops[n] for n in PLAN["order"]]
    for op in ops:
        op["q"] = PLAN["queue"][op["n"]]

    for op in ops:
        op["deps"] = [o for o in op["deps"] if not (op["q"] == "P" and o["q"] == "P")]
        for o in op["deps"]:
            o["need"] = True
    count = {"V": 0, "A": 0, "P": 0, "G": 0}
    for op in order:
        if op["tok"] is None and op["need"]:
            count[op["q"]] += 1
            op["at"] = ("e" + op["q"], count[op["q"]])
    for q in count:
        totals["e" + q] = count[q]
    seen = {q: {} for q in Q}
    for op in order:
        want = {}
        for o in op["deps"]:
            s, v = (o["tok"], totals[o["tok"]]) if o["tok"] else o["at"]
            want[s] = max(want.get(s, 0), v)
        for s, v in want.items():
            if seen[op["q"]].get(s, 0) < v:
                Q[op["q"]].wait_ge(T.sem[s], v)
                seen[op["q"]][s] = v
        ins = op["fn"][op["q"]]()
        if op["tok"] is None and op["need"]:
            ins.then_inc(T.sem[op["at"][0]], 1)
    for s, v in totals.items():
        if v and max(seen[q].get(s, 0) for q in Q) < v:
            g.sync.wait_ge(T.sem[s], v)
